import numpy as np, ml_dtypes
CORES = [5,29,101,125,133,157,229,253]
N = 8
BF = ml_dtypes.bfloat16
W, NS, TS = 2048, 256, 6
B = W // NS
def parts(rng):
    size = rng.choice(np.array([256, 256, 256, 64, 16]), (N, 8, 1, W))
    x = (rng.random((N, 8, 16, W)) * size).astype(np.int64)
    v = rng.integers(0, W, (N, 8, 16, W)); s = rng.integers(0, W, (N, 8, 16, NS)); z = rng.integers(0, 256, (N, 8, 16, NS)); w = rng.integers(0, 256, (N, 8, 16))
    h = np.where(rng.random((N, 8, 16)) < 0.75, rng.integers(0, 600, (N, 8, 16)), rng.integers(600, 1600, (N, 8, 16)))
    return x, v, s, z, w, h, rng.integers(0, 2, (N, 8, NS))
def pack(x, v, s, z, w, h, a):
    return {"reg": np.ascontiguousarray(x.reshape(N, 128, W)).astype(np.float32).astype(BF), "vw": np.ascontiguousarray((v[..., :W // 2] + W * v[..., W // 2:]).reshape(N, 128, W // 2)).astype(np.int32),
            "scan": np.ascontiguousarray(s.reshape(N, 128, NS)).astype(np.int32), "z0": np.ascontiguousarray(z.reshape(N, 128, NS)).astype(np.float32).astype(BF),
            "wt": np.ascontiguousarray(w.reshape(N, 128, 1)).astype(np.int32), "th": np.ascontiguousarray(h.reshape(N, 128, 1)).astype(np.int32), "warm": np.ascontiguousarray(a).astype(np.int32)}
def setup_inputs(rng):
    return pack(*parts(rng))
def setup_inputs_corners(rng):
    x, v, s, z, w, h, a = parts(rng); i = np.arange(NS)[None, :]; k = np.arange(16)[:, None]; d = np.arange(W)[None, :]
    for q in range(N):
        for g in range(8):
            c = (g + 3 * q) % 8
            x[q, g][:, ::7] = 0; x[q, g][:, 3::7] = 255; x[q, g][:, W - 1] = 255
            if (q + g) % 3 == 0: a[q, g] = 0
            if (q + g) % 3 == 1: a[q, g] = 1
            if c == 0: s[q, g] = 0; w[q, g] = 255
            if c == 1: s[q, g] = W - 1; h[q, g] = 4079
            if c == 2: s[q, g] = B * i + k % B; h[q, g] = 0
            if c == 3: s[q, g] = B * rng.integers(0, NS, (16, NS)); w[q, g] = 0; h[q, g] = 0; a[q, g] = rng.integers(0, 2, NS)
            if c == 4: s[q, g] = (16 * i + k + 1) % W; v[q, g] = np.where(k >= 0, (d + 1) % W, 0)
            if c == 5: v[q, g] = np.where(k >= 0, d, 0); w[q, g] = 255 * rng.integers(0, 2, 16)
            if c == 6: v[q, g] = (W - 1) * rng.integers(0, 2, (1, W)); h[q, g] = 4079 * rng.integers(0, 2, 16)
            if c == 7: s[q, g] = B * rng.integers(0, NS, (16, NS)) + B - 1; a[q, g] = rng.integers(0, 2, NS); h[q, g] = 0
            if c % 3 == 0: z[q, g] = 0
            if c % 3 == 1: z[q, g] = 255
    return pack(x, v, s, z, w, h, a)
def setup_inputs_crowd(rng):
    x, v, s, z, w, h, a = parts(rng); h = rng.integers(0, 1000, (N, 8, 16))
    for q in range(N):
        for g in range(8):
            pl = rng.permutation(W)[:4]; x[q, g][:, pl[:3]] = rng.integers(200, 256, (16, 3)); x[q, g][:, pl[3]] = 0
            s[q, g] = rng.choice(pl[:1 + 2 * (g % 2)], (16, NS)); a[q, g] = 1
            if g % 4 == 1: w[q, g] = 0
            if g % 4 == 2: w[q, g] = 255
            o = int(rng.integers(0, NS)) if g < 7 else NS - 1
            if q % 4 == 3:
                a[q, g] = 0
                if g == 7: a[q, g, o] = 1
            elif (q % 4 == 1 and g == 7) or (q % 4 == 2 and g % 2 == 1):
                way = (g // 2 + q) % 3
                if way == 0: a[q, g, o] = 0
                else: s[q, g, :, o] = pl[3]
                if way == 2: s[q, g, int(rng.integers(0, 16)), o] = pl[0]
    return pack(x, v, s, z, w, h, a)
def setup_inputs_ends(rng):
    x = np.where(rng.random((N, 8, 1, W)) < 0.5, 255 * rng.integers(0, 2, (N, 8, 1, W)), 255 * rng.integers(0, 2, (N, 8, 16, W)))
    x[..., 0] = 0; x[..., W - 1] = 255; x[:, 1, :, 0] = 255; x[:, 1, :, W - 1] = 0
    e = (W - 1) * rng.integers(0, 2, (N, 8, 16, W // 2)); c = rng.random(e.shape) < 0.7
    v = np.concatenate([np.where(c, e, rng.integers(0, W, e.shape)), np.where(c, e, rng.integers(0, W, e.shape))], axis=3)
    s = np.where(rng.random((N, 8, 16, NS)) < 0.72, (W - 1) * rng.integers(0, 2, (N, 8, 16, NS)), rng.integers(0, W, (N, 8, 16, NS)))
    z = np.where(rng.random((N, 8, 1, NS)) < 0.5, 255 * rng.integers(0, 2, (N, 8, 1, NS)), 255 * rng.integers(0, 2, (N, 8, 16, NS)))
    w = 255 * rng.integers(0, 2, (N, 8, 16)); w[:, 2] = 255; w[:, 6] = 255
    w[:, 3] = 0; w[:, 3, 15] = 255; w[:, 3, 0] = 2; w[:, 7] = w[:, 3]; w[0, 7] = 255
    h = 4079 * rng.integers(0, 2, (N, 8, 16)); h[..., 0] = 4079; h[..., 8] = 0; h[..., 15] = 0
    a = (rng.random((N, 8, NS)) < 0.6).astype(np.int64); i = np.arange(NS); last = i[i % 8 == 7]; one = i[i % 8 == 6]; two = i[i % 8 == 1]; three = i[i % 8 == 5]; late = 5 * B - 1
    for q in range(N):
        b = (N - 1 - q) % 2 == 0
        v[q, :, :, W - 1] = W - 1 if b else 0; v[q, :, :, W // 2 - 1] = W - 1 if b else 0
        s[q][:, :, last] = W - 1; z[q][:, :, last] = 0 if b else 255; a[q][:, last] = 1
        if b:
            both = np.concatenate([one, two]); s[q][:, :, both] = 0; z[q][:, :, both] = 255; a[q][:, both] = 1
            s[q][:, 15, one] = W - 1; s[q][:, 8, two] = W - 1
            for g in (3, 7):
                x[q, g][:, late] = 0; s[q, g][:, 4] = W - 1; z[q, g][:, 4] = 0; a[q, g, 4] = 1
                s[q, g][:, three] = 0; s[q, g][15, three] = W - 1; s[q, g][8, three] = late; z[q, g][:, three] = 0; a[q, g, three] = 1
    s[0, :, 3] = W - 1; s[0, :, 15] = W - 1; s[0, 1, 3] = 0; s[0, 1, 15] = 0; a[0] = 1; a[0, 0, 0] = 0
    return pack(x, v, s, z, w, h, a)
def setup_inputs_spread(rng):
    x, v, s, z, w, h, a = parts(rng)
    x = (np.exp2(8 * rng.random((N, 8, 1, W))) * rng.random((N, 8, 16, W))).astype(np.int64)
    z = (np.exp2(8 * rng.random((N, 8, 1, NS))) * rng.random((N, 8, 16, NS))).astype(np.int64)
    w = np.minimum(np.exp2(8 * rng.random((N, 8, 16))).astype(np.int64), 255); h = np.minimum(np.exp2(12 * rng.random((N, 8, 16))).astype(np.int64) - 1, 4079)
    p = rng.choice(np.array([0.5, 1.0, 2.0, 3.0]), (N, 8, 1, 1))
    s = np.minimum((W * rng.random((N, 8, 16, NS)) ** p).astype(np.int64), W - 1); v = np.minimum((W * rng.random((N, 8, 16, W)) ** p).astype(np.int64), W - 1)
    a = (rng.random((N, 8, NS)) < rng.choice(np.array([0.1, 0.5, 0.9]), (N, 8, 1))).astype(np.int64)
    return pack(x, v, s, z, w, h, a)
def setup_inputs_ties(rng):
    x, v, s, z, w, h, a = parts(rng); lane = np.arange(16)[:, None]
    for q in range(N):
        for g in range(8):
            if g % 2 == 0:
                c = (0, 16, 1000, 4079)[(g // 2 + q) % 4]
                m = np.minimum(np.maximum(c + rng.integers(-1, 2, W), 0), 4080)
                x[q, g] = m // 16 + ((lane + rng.integers(0, 16, W)) % 16 < m % 16); h[q, g] = c
                z[q, g] = z[q, g] * rng.integers(0, 2, (1, NS)); a[q, g] = rng.random(NS) < 0.8
            else:
                x[q, g] = rng.integers(0, 16, (16, W)); x[q, g][:, W // 2:] = x[q, g][:, :W // 2]
                s[q, g, 1::2] = (s[q, g, 0::2] + W // 2) % W; h[q, g] = rng.integers(10, 70, 16); z[q, g] = rng.integers(0, 16, (16, NS))
                x[q, g][:, 5] = 255; x[q, g, (g + q) % 16, 5] = 254; x[q, g][:, W - 1] = 255
                s[q, g][:, NS - 2:] = 5; s[q, g, 15, NS - 2:] = W - 1; z[q, g][:, NS - 2:] = 0; a[q, g, NS - 2:] = 1
                if g % 4 == 3:
                    x[q, g][:, W - 3] = 0; x[q, g][:, W // 2 - 3] = 0; w[q, g, 0] = 1; w[q, g, 1] = 16
                    s[q, g][:, 4:6] = W - 3; z[q, g][:, 4:6] = 0; z[q, g, 0, 4:6] = 11; z[q, g, 1, 4:6] = W // 16 - 2; a[q, g, 4:6] = 1
    return pack(x, v, s, z, w, h, a)
def check_inputs(d):
    bad = []
    for k, lo, hi in (("reg", 0, 255), ("vw", 0, W * W - 1), ("scan", 0, W - 1), ("z0", 0, 255), ("wt", 0, 255), ("th", 0, 4079), ("warm", 0, 1)):
        a = np.asarray(d[k]).astype(np.float64)
        if not (np.min(a) >= lo and np.max(a) <= hi): bad.append("range of " + k)
        elif np.any(a != np.floor(a)): bad.append("whole numbers in " + k)
    return bad
def pick(x, ix):
    return np.take_along_axis(x, ix.reshape(N, 8, 1, 16 * NS), 3).reshape(N, 8, 16, 16, NS)
def reference(reg, vw, scan, z0, wt, th, warm):
    X = reg.astype(np.float32).astype(np.int32).reshape(N, 8, 16, W); pk = vw.astype(np.int64).reshape(N, 8, 16, W // 2)
    V = np.concatenate([pk % W, pk // W], axis=3)
    S = scan.astype(np.int64).reshape(N, 8, 16, NS); z = z0.astype(np.float32).astype(np.int32).reshape(N, 8, 16, NS)
    wl = wt.astype(np.int64).reshape(N, 8, 16, 1); theta = th.astype(np.int64).reshape(N, 8, 16, 1); new = warm == 0
    last = np.zeros((N, 8, 16, 16, NS), np.int32); m = np.zeros((N, 8, 16, NS), np.int64); A = np.zeros((N, 1, 1, 1), np.int64)
    row37 = 37 * np.arange(16).reshape(1, 1, 16, 1); sc = np.arange(NS)
    for t in range(TS):
        C = pick(X, S)
        moved = (np.add.reduce(np.abs(C - last), axis=2) > theta + A % 32) & ~new[:, :, None, :]
        m = m + moved; some = np.any(moved, axis=2)
        clean = ~new & ~some; borrow = some & (np.add.reduce(m, axis=2) >= 2); has = clean | borrow
        key = 4096 * m + np.add.reduce(np.abs(C - z[:, :, :, None, :]), axis=2)
        donor = np.argmax(key, axis=2)
        dr = np.take_along_axis(S, donor[:, :, None, :], 2)
        F = np.where(borrow[:, :, None, :], np.take_along_axis(V, dr, 3), S)
        D = pick(X, F); y = (np.max(D, axis=3) + np.min(D, axis=3)) >> 1
        z = np.where(has[:, :, None, :], np.abs(y - z), z)
        u = np.add.reduce(wl * z, axis=2, keepdims=True) % W
        place = B * sc + u[:, :, 0, :] % B
        X = X.copy(); V = V.copy()
        for r in range(N):
            for odd in range(2):
                q = (r + odd * (1 + t % 3)) % N
                gi, si = np.nonzero(has[r] & (sc % 2 == odd)); pl = place[r][gi, si]
                X[q][gi, :, pl] = y[r][gi, :, si]
                if t < TS - 1: V[q][gi, :, pl] = F[r][gi, :, si]
        S = np.where(has[:, :, None, :], (((F * u) >> 5) + F + row37 + A) % W, S)
        m = np.where(has[:, :, None, :], 0, m); new = has; last = C
        A = np.add.reduce(borrow.astype(np.int64).reshape(N, 8 * NS), axis=1).reshape(N, 1, 1, 1)
    return {"yx": X.reshape(N, 128, W).astype(np.float32).astype(BF), "ys": S.reshape(N, 128, NS).astype(np.float32), "yz": z.reshape(N, 128, NS).astype(np.float32).astype(BF)}

@@ -1,0 +1,549 @@
+from concourse.mybir import AluOpType, ActivationFunctionType
+
+AL = AluOpType
+AF = ActivationFunctionType
+TS = 6
+XW = 4352
+RING, V0, VLOG = 16, 784, 2832
+VW = VLOG + 4 * 256
+SPARE = 2304.0
+M1 = 12582912.0
+M2 = M1 * 2048.0
+DCH = {0: [(256, "s"), (256, "v"), (512, "s"), (512, "s"), (256, "s"), (256, "v")], 1: [(512, "s"), (512, "s"), (512, "s"), (256, "s"), (256, "s")]}
+ALPHA = [-0.05, 30, 150]
+FAR = [4000, 6500]
+SEED = [3097, 1500]
+JOINT = [True, False]
+
+bf, f32, i32, u16 = "bfloat16", "float32", "int32", "uint16"
+SCRATCH = {
+    "X": ("sbuf", [128, XW], bf), "P": ("sbuf", [128, XW], f32), "WA": ("sbuf", [128, 384], bf), "WB": ("sbuf", [128, 384], bf),
+    "ra": ("sbuf", [128, 256], f32), "rb": ("sbuf", [128, 256], f32), "VT": ("sbuf", [128, VW], i32),
+    "vwi": ("sbuf", [128, 1024], i32), "sci": ("sbuf", [128, 256], i32), "zin": ("sbuf", [128, 256], bf),
+    "wti": ("sbuf", [128, 4], i32), "thi": ("sbuf", [128, 4], i32), "wai": ("sbuf", [128, 256], i32), "wab": ("sbuf", [128, 256], bf),
+    "zs": ("sbuf", [128, 7 * 256], bf), "zr0": ("sbuf", [128, 4096], bf), "zr1": ("sbuf", [128, 4096], bf),
+    "M0": ("sbuf", [128, 8, 256], bf), "M1": ("sbuf", [128, 8, 256], bf), "G0": ("sbuf", [128, 8, 256], bf), "G1": ("sbuf", [128, 8, 256], bf),
+    "D0": ("sbuf", [128, 2048], bf), "D1": ("sbuf", [128, 2048], bf),
+    "MX": ("sbuf", [128, 4096], bf), "MN": ("sbuf", [128, 4096], bf),
+    "mk0": ("sbuf", [128, 1024], bf), "mkB": ("sbuf", [128, 1024], bf),
+    "soff": ("sbuf", [128, 256], u16), "fu": ("sbuf", [128, 256], u16), "lst": ("sbuf", [128, 64], u16),
+    "fs": ("sbuf", [128, 6 * 128], i32), "fe": ("sbuf", [128, 128], i32), "fl4": ("sbuf", [128, 128], i32),
+    "ysn": ("sbuf", [128, 6 * 136], bf), "W": ("sbuf", [128, 6 * 264], bf),
+    "mv": ("sbuf", [128, 512], bf), "pm": ("sbuf", [128, 256], f32), "fg": ("sbuf", [128, 256], bf), "nf": ("sbuf", [128, 256], bf),
+    "fd": ("sbuf", [128, 256], f32), "s2": ("sbuf", [128, 256], f32),
+    "dz": ("sbuf", [128, 512], f32), "r0": ("sbuf", [128, 256], f32), "rr": ("sbuf", [128, 256], f32), "pr": ("sbuf", [128, 256], f32), "qi": ("sbuf", [128, 256], i32),
+    "dd": ("sbuf", [128, 256], bf), "ad": ("sbuf", [128, 256], bf), "t1": ("sbuf", [128, 512], bf),
+    "tf": ("sbuf", [128, 256], f32), "ti": ("sbuf", [128, 64], i32), "bo": ("sbuf", [128, 16], bf),
+    "col": ("sbuf", [128, 64], f32), "BI": ("sbuf", [128, 16], f32), "BS": ("sbuf", [128, 16], f32),
+    "th0": ("sbuf", [128, 128], f32), "thT": ("sbuf", [128, 128], f32), "dkf": ("sbuf", [128, 128], f32), "Bf": ("sbuf", [128, 128], f32),
+    "CI": ("sbuf", [128, 256], bf), "KI": ("sbuf", [128, 128], bf), "GI": ("sbuf", [128, 128], bf), "HI": ("sbuf", [128, 128], bf),
+    "ZM": ("sbuf", [128, 144], bf), "ZR": ("sbuf", [128, 144], bf), "ZD": ("sbuf", [128, 144], bf), "ZW": ("sbuf", [128, 144], bf), "Z8": ("sbuf", [128, 144], bf),
+    "I1": ("sbuf", [128, 128], bf), "Ih": ("sbuf", [128, 128], bf), "In": ("sbuf", [128, 128], bf), "I8": ("sbuf", [128, 128], bf),
+    "BW": ("sbuf", [128, 128], bf), "BX": ("sbuf", [128, 128], bf), "Bc": ("sbuf", [128, 128], bf),
+    "one": ("sbuf", [128, 128], bf), "o4": ("sbuf", [128, 128], bf), "TB": ("sbuf", [128, 128], bf),
+    "cY": ("sbuf", [128, 256], bf), "cU": ("sbuf", [128, 256], bf), "zer": ("sbuf", [128, 128], bf),
+    "yso": ("sbuf", [128, 256], f32), "yzo": ("sbuf", [128, 256], bf),
+    "pK0": ("psum", [128, 512], f32), "pK1": ("psum", [128, 512], f32), "pD0": ("psum", [128, 512], f32), "pD1": ("psum", [128, 512], f32),
+    "pN": ("psum", [128, 512], f32), "pY": ("psum", [128, 512], f32), "pU": ("psum", [128, 512], f32), "pV": ("psum", [128, 512], f32),
+}
+DMAS = ["reg", "vw", "scan", "z0", "wt", "th", "warm", "oz", "os_", "ox"]
+SEMAPHORES = (["cv", "cs", "cp", "cg", "sent"] + ["d" + n for n in DMAS]
+              + ["aF%d" % t for t in range(TS)] + ["aY%d" % t for t in range(TS)])
+CYC, PCYC, GATH, SCAT, LAT = 1.04, 0.52, 1.56, 3.8, 110.0
+
+
+def route(T, topo, r, t):
+    src, dst = T.cores[r], T.cores[(r + 1 + t % 3) % len(T.cores)]
+    if topo.may_write(src, dst):
+        return dst, None
+    c = [h for h in topo.cores_of(src) if T.rank_of(h) is None and topo.may_write(h, dst)]
+    c.sort(key=lambda h: (topo.die(h) != topo.die(src), h))
+    return dst, c[0]
+
+
+def landing(T, kind, t):
+    if kind == "Y":
+        return T.W[:, 264 * t + 128:264 * t + 264]
+    return T.VT[:, VLOG + 256 * t + 128:VLOG + 256 * t + 256] if t < 4 else T.fl4[:, :]
+
+
+def write(g, T, topo, src, dst, in_ap, kind, t):
+    rid, pid = topo.addr(dst, src)
+    g.remote_dma(landing(T, kind, t), in_ap, T.sem["a%s%d" % (kind, t)], T.sem.sent, pid, rid, topo.mask(src, dst))
+    return len(topo.engines(src, dst))
+
+
+def helper_program(g, core, T, topo):
+    n = 0
+    for t in range(TS):
+        for r in range(len(T.cores)):
+            dst, h = route(T, topo, r, t)
+            if h != core:
+                continue
+            for kind in ("F", "Y") if t < TS - 1 else ("Y",):
+                g.wait_ge(T.sem["a%s%d" % (kind, t)], len(topo.engines(T.cores[r], core)))
+                n += write(g, T, topo, core, dst, landing(T, kind, t), kind, t)
+    if n:
+        g.wait_ge(T.sem.sent, n)
+
+
+def plan(g, core, T, topo, rank):
+    V, S, PE = g.vector, g.scalar, g.tensor
+    ops = []
+    sent = [0]
+
+    def op(e, fn, r, w, cost, sem=None, n=1, hold=None):
+        ops.append((e, fn, list(r), list(w), float(cost), sem, n, float(cost if hold is None else hold)))
+
+    def ts(o, i, s1, s2, a, b, r, w, n):
+        if b is None:
+            op("v", lambda: [V.tensor_scalar(o, i, s1, None, a)], r, w, max(64, n) * CYC)
+        else:
+            op("v", lambda: [V.tensor_scalar(o, i, s1, s2, a, b)], r, w, max(64, n) * CYC)
+
+    def tt(o, x, y, a, r, w, n):
+        op("v", lambda: [V.tensor_tensor(o, x, y, a)], r, w, max(64, n) * CYC)
+
+    def cp(o, i, r, w, n):
+        op("v", lambda: [V.tensor_copy(o, i)], r, w, max(64, n) * CYC)
+
+    def ms(o, c, w, n):
+        op("v", lambda: [V.memset(o, c)], [], w, max(64, n) * CYC)
+
+    def scan(o, d0, d1, a, b, r, w, n):
+        op("v", lambda: [V.tensor_tensor_scan(o, d0, d1, 0.0, a, b)], r, w, max(64, n) * CYC)
+
+    def act(o, i, f, r, w, n, bias=0.0, scale=1.0):
+        op("s", lambda: [S.activation(o, i, f, bias=bias, scale=scale)], r, w, max(64, n) * CYC)
+
+    def mm(lst, r, w, cols):
+        k = 2 if len(lst) == 16 else 1
+        for j in range(k):
+            part = lst[j * len(lst) // k:(j + 1) * len(lst) // k]
+            op("p", lambda part=part: [PE.matmul(*a) for a in part], r, w, cols * PCYC / k + 30, n=len(part))
+
+    def iota(o, pat, base, cm, w, n, small=True):
+        if small:
+            op("g", lambda: [g.iota(o, pat, base, cm, allow_small_or_imprecise_dtypes=True)], [], w, 160 + 2 * n * CYC)
+        else:
+            op("g", lambda: [g.iota(o, pat, base, cm)], [], w, 160 + 2 * n * CYC)
+
+    def dma(q, name, o, i, r, w, cost):
+        e = g.sync if q == "y" else S
+        op(q, lambda: [e.dma_start(o, i)], r, w, cost, sem="d" + name, n=16, hold=60)
+
+    def c(j):
+        return T.col[:, j:j + 1]
+    PF, LF, GF, C15, C16G, C8G, C8G1, C4, WF, THF, WR, MLO, WD, TA, TBc, TC, B37, L16, P15, A4, AQ = range(21)
+    C32 = 32
+    def tl(j, h=None):
+        return T.tf[:, 16 * j:16 * j + 16] if h is None else T.tf[:, 16 * j + 8 * h:16 * j + 8 * h + 8]
+    NP0, BASE, SNN, SPTR, LIM, T3, NH, EE, SP2, OFF, CE = 0, 3, 4, 5, 6, 7, 8, 9, 10, 11, 12
+
+    dma("y", "reg", T.X[:, 0:2048], T.reg[:], [], ["X"], 4500)
+    dma("s", "z0", T.zin[:], T.z0[:], [], ["zin"], 2200)
+    dma("s", "scan", T.sci[:], T.scan[:], [], ["sci"], 2400)
+    dma("s", "warm", T.wai[0:8, :], T.warm[:], [], ["wai"], 2400)
+    dma("s", "wt", T.wti[:, 0:1], T.wt[:], [], ["wti"], 2500)
+    dma("s", "th", T.thi[:, 0:1], T.th[:], [], ["thi"], 2600)
+    dma("y", "vw", T.vwi[:], T.vw[:], [], ["vwi"], 7000)
+    iota(T.ti[:, 0:1], [[0, 1]], 0, 1, ["ti0"], 1, small=False)
+    iota(T.CI[:], [[1, 256]], 0, 0, ["CI"], 256)
+    iota(T.KI[:], [[0, 8], [1, 16]], 0, 0, ["KI"], 128)
+    iota(T.HI[:], [[1, 32], [0, 4]], 0, 0, ["HI"], 128)
+    iota(T.GI[:], [[1, 8], [0, 16]], 0, 0, ["GI"], 128)
+    iota(tl(NP0), [[128, 2], [16, 8]], RING, 0, ["np0"], 16)
+    iota(tl(BASE), [[8, 2], [256, 8]], 0, 0, ["base"], 16)
+    ms(T.X[:, 2048:2064], 0.0, ["Xs"], 8)
+    ms(T.P[:, 2048:2064], 0.0, ["Ps"], 8)
+    iota(T.X[:, 2064:XW], [[0, XW - 2064]], 0, 0, ["Xt"], XW - 2064)
+    iota(T.P[:, 2064:XW], [[0, XW - 2064]], 0, 0, ["Pt"], XW - 2064)
+    ms(T.VT[:, 0:RING], 2048, ["VTd"], 16)
+    ms(T.VT[:, RING + 256:V0], 0, ["S10", "S11", "S20", "S21"], 512)
+    ms(T.mk0[:], 1.0, ["mk0"], 512); ms(T.mk0[:, ::16], 0.0, ["mk0"], 32)
+    ms(T.mkB[:], 0.0, ["mkB"], 512); ms(T.mkB[:, ::16], 256.0, ["mkB"], 32)
+    ms(T.one[:], 1.0, ["one"], 64); ms(T.o4[:], 4096.0, ["o4"], 64); ms(T.zer[:], 0.0, ["zer"], 64)
+    ms(T.cY[0:1, :], -0.25, ["cY"], 128)
+    ms(T.cU[0:2, 0:128], 0.5, ["cU"], 64); ms(T.cU[0:1, 0:128], -1024.0, ["cU"], 64); ms(T.cU[0:2, 128:256], 16.0, ["cU"], 64)
+    ms(tl(LIM), 8192.0, ["lim"], 16)
+    for j, v in enumerate((M1, -M1, M2, -M2)):
+        ms(c(40 + j), v, ["m1"], 1)
+    cp(c(PF), T.ti[:, 0:1], ["ti0"], ["pf"], 1)
+    ts(T.ti[:, 1:2], T.ti[:, 0:1], 15, None, AL.bitwise_and, None, ["ti0"], ["ti1"], 1)
+    cp(c(LF), T.ti[:, 1:2], ["ti1"], ["lf"], 1)
+    tt(c(C16G), c(PF), c(LF), AL.subtract, ["pf", "lf"], ["c16g"], 1)
+    ts(c(C15), c(C16G), 15.0, None, AL.add, None, ["c16g"], ["c15"], 1)
+    ts(c(C4), c(C16G), 4.0, None, AL.add, None, ["c16g"], ["c4"], 1)
+    ts(c(GF), c(C16G), 0.0625, None, AL.mult, None, ["c16g"], ["gf"], 1)
+    ts(c(C8G), c(C16G), 0.25, None, AL.mult, None, ["c16g"], ["c8g"], 1)
+    ts(c(P15), c(PF), 16.0, 15.0, AL.mult, AL.add, ["pf"], ["p15"], 1)
+    ts(c(B37), c(LF), 1184.0, None, AL.mult, None, ["lf"], ["b37"], 1)
+    ts(c(L16), c(LF), 16.0, None, AL.mult, None, ["lf"], ["l16"], 1)
+    ts(c(WR), c(LF), 1.0, -2.0 ** -12, AL.is_le, AL.mult, ["lf"], ["wr"], 1)
+    cp(c(WF), T.wti[:, 0:1], ["wti"], ["wf"], 1)
+    cp(c(THF), T.thi[:, 0:1], ["thi"], ["thf"], 1)
+    ts(T.dkf[:], T.KI[:], c(LF), None, AL.is_equal, None, ["KI", "lf"], ["dkf"], 128)
+
+    def dk(k):
+        return T.dkf[:, k:k + 1]
+    tt(c(MLO), dk(1), dk(3), AL.add, ["dkf"], ["mlo"], 1)
+    tt(c(TA), dk(2), dk(3), AL.add, ["dkf"], ["ta"], 1)
+    tt(c(TBc), dk(4), dk(5), AL.add, ["dkf"], ["tb"], 1)
+    ts(c(TC), dk(6), 4080.0 * 4096.0, c(TBc), AL.mult, AL.add, ["dkf", "tb"], ["tc"], 1)
+    ts(c(WD), c(TA), 4096.0, c(TC), AL.mult, AL.add, ["ta", "tc"], ["wd"], 1)
+    ts(T.BI[:], T.CI[:, 0:16], -256.0, -float(V0), AL.mult, AL.add, ["CI"], ["BI"], 16)
+    ms(T.BI[:, 12:13], -float(V0), ["BI"], 1)
+    ts(T.BI[:], T.BI[:], dk(5), None, AL.mult, None, ["BI", "dkf"], ["BI"], 16)
+    ts(T.BS[:], T.CI[:, 0:16], -1.0, dk(6), AL.mult, AL.mult, ["CI", "dkf"], ["BS"], 16)
+    tt(T.BI[:, 8:13], T.BI[:, 8:13], T.BS[:, 1:6], AL.add, ["BI", "BS"], ["BI"], 16)
+    ts(T.col[:, 48:53], T.BI[:, 8:13], -1.0, None, AL.mult, None, ["BI"], ["BJ"], 16)
+    for nm, s2, r in (("ZM", 2.0 ** -11, []), ("ZR", c(WR), ["wr"]), ("ZD", c(WD), ["wd"]), ("ZW", c(WF), ["wf"])):
+        ts(T[nm][:], T.CI[:, 0:144], c(C15), s2, AL.is_equal, AL.mult, ["CI", "c15"] + r, [nm], 72)
+    ts(T.Z8[0:8, :], T.CI[0:8, 0:144], T.col[0:8, P15:P15 + 1], None, AL.is_equal, None, ["CI", "p15"], ["Z8"], 72)
+    for nm, s2 in (("I1", 1.0), ("Ih", 0.5), ("In", -1.0), ("I8", 8192.0)):
+        ts(T[nm][:], T.CI[:, 0:128], c(PF), s2, AL.is_equal, AL.mult, ["CI", "pf"], [nm], 64)
+    ts(T.BW[:], T.GI[:], c(GF), c(WF), AL.is_equal, AL.mult, ["GI", "gf", "wf"], ["BW"], 64)
+    ts(T.Bf[:], T.GI[:], c(GF), None, AL.is_equal, None, ["GI", "gf"], ["Bf"], 128)
+    ts(T.BX[:], T.HI[:], c(C8G), None, AL.is_equal, None, ["HI", "c8g"], ["BX"], 64)
+    ms(T.WA[:], 0.0, ["WA"], 192)
+    ts(c(TA + 32), c(LF), 1.0, None, AL.is_le, None, ["lf"], ["lp"], 1)
+    ts(c(TA + 33), c(LF), 1.0, -1.0, AL.is_le, AL.mult, ["lf"], ["ln"], 1)
+    for m0, j, s2 in ((0, 0, -1.0), (0, 1, 1.0), (0, 2, 1.0), (0, 3, -1.0), (128, 2, -2.0), (128, 3, 2.0), (256, 2, c(TA + 32)), (256, 3, c(TA + 33))):
+        ts(T.WA[:, m0 + j:m0 + 128:16], T.GI[:, 0::16], c(GF), s2, AL.is_equal, AL.mult, ["GI", "gf", "lp", "ln"], ["WA"], 8)
+    cp(T.WB[:], T.WA[:], ["WA"], ["WB"], 192)
+    ms(T.WB[:, 0::2], 0.0, ["WB"], 96)
+    ts(T.Bc[:], T.CI[:, 0:128], c(C4), dk(0), AL.is_equal, AL.mult, ["CI", "c4", "dkf"], ["Bc"], 64)
+    ts(T.TB[:], T.KI[:], -2.0 ** -16, 15 * 2.0 ** -16, AL.mult, AL.add, ["KI"], ["TB"], 64)
+    ts(tl(NP0), tl(NP0), c(LF), None, AL.add, None, ["np0", "lf"], ["np0"], 16)
+    ts(tl(NP0 + 1), tl(NP0), 256.0, None, AL.add, None, ["np0"], ["np1"], 16)
+    ts(tl(NP0 + 2), tl(NP0), 512.0, None, AL.add, None, ["np0"], ["np2"], 16)
+    ts(tl(BASE), tl(BASE), c(L16), None, AL.add, None, ["base", "l16"], ["base"], 16)
+    cp(tl(SPTR), tl(NP0), ["np0"], ["sptr"], 16)
+    cp(c(C32), c(B37), ["b37"], ["c320"], 1)
+    ts(T.thT[:], T.dkf[:], c(THF), None, AL.mult, None, ["dkf", "thf"], ["thT"], 128)
+    mm([(T.pU[:, 0:128], T.Bf[:], T.thT[:], True, True)], ["Bf", "thT"], ["pU"], 512)
+    ts(T.th0[:], T.pU[:, 0:128], 4096.0, 4095.0, AL.mult, AL.add, ["pU"], ["th0"], 128)
+    for h in (0, 1):
+        cp(T.VT[:, RING + 128 * h:RING + 128 * h + 128], T.sci[:, h::2], ["sci"], ["S0%d" % h], 128)
+        cp(T.zs[:, 128 * h:128 * h + 128], T.zin[:, h::2], ["zin"], ["z0%d" % h], 64)
+    cp(T.wab[0:8, :], T.wai[0:8, :], ["wai"], ["wab"], 256)
+    mm([(T.pN[:, 8 * h:8 * h + 8], T.Z8[0:8, 15 - a:143 - a], T.wab[0:8, 2 * a + h::32], a == 0, a == 15)
+        for h in (0, 1) for a in range(16)], ["Z8", "wab"], ["pN"], 32 * 64)
+    tt(tl(SNN), T.pN[:, 0:16], tl(NP0), AL.mult, ["pN", "np0"], ["snn"], 16)
+    ring = ["VTd"] + ["S%d%d" % (s, h) for s in range(3) for h in (0, 1)]
+
+    def next_lists():
+        cp(T.lst[:, 32:48], tl(SNN), ["snn"], ["sl"], 16)
+        for h in (1, 0):
+            cp(T.soff[:, 128 * h:128 * h + 128], T.VT[:, 0:V0].indirect(T.lst[:, 32 + 8 * h:40 + 8 * h]), ring + ["sl"], ["soff%d" % h], 50 + 128 * GATH)
+    next_lists()
+    for k in range(16):
+        if k % 4 == 0:
+            op("g", lambda k=k: [g.affine_select(T.zr0[:, k::16], T.zs[:, 0:256], [[0, 256]], AL.is_ge, 0.0, 0, 0)],
+               ["z00", "z01"], ["zr0%d" % k], 210 + 512 * CYC)
+        elif k % 4 != 2 or k > 10:
+            cp(T.zr0[:, k::16], T.zs[:, 0:256], ["z00", "z01"], ["zr0%d" % k], 128)
+        else:
+            act(T.zr0[:, k::16], T.zs[:, 0:256], AF.Copy, ["z00", "z01"], ["zr0%d" % k], 256)
+    for j in range(8):
+        pb = ("pK0", "pD0", "pV", "pY")[j % 4]
+        sl = slice(256 * j, 256 * j + 256)
+        tv = T.t1[:, 256 * (j % 2):256 * (j % 2) + 256]
+        mm([(T[pb][:, 0:256], T.BX[:], T.X[:, sl], True, False), (T[pb][:, 0:256], T.Bc[:], T.CI[:], False, True)],
+           ["BX", "Bc", "CI", "X"], [pb], 512)
+        act(tv, T[pb][:, 0:256], AF.Identity, [pb, "mlo", "BI"], ["t1%d" % (j % 2)], 256, bias=T.BI[:, j:j + 1], scale=c(MLO))
+        tt(T.P[:, sl], T[pb][:, 0:256], tv, AL.subtract, [pb, "t1%d" % (j % 2)], ["P%d" % j], 256)
+    Pk = ["Ps"] + ["P%d" % j for j in range(8)]
+    ts(T.VT[:, V0:V0 + 1024], T.vwi[:], 2047, None, AL.bitwise_and, None, ["vwi"], ["V0a"], 1024)
+    ts(T.VT[:, V0 + 1024:V0 + 2048], T.vwi[:], 11, None, AL.logical_shift_right, None, ["vwi"], ["V0b"], 1024)
+
+    for t in range(TS):
+        last = t == TS - 1
+        zr = T.zr0 if t < 2 or t % 2 else T.zr1
+        zrk = ["zr%d%d" % (0 if t < 2 or t % 2 else 1, k) for k in range(16)]
+        thk, thb = ("th0", T.th0) if t == 0 else ("thT", T.thT)
+        dst, hop = route(T, topo, rank, t)
+        srcrank = (rank - 1 - t % 3) % len(T.cores)
+        shop = route(T, topo, srcrank, t)[1]
+        narr = len(topo.engines(T.cores[srcrank] if shop is None else shop, core))
+        far = FAR[0 if hop is None else 1]
+
+        def send(kind, ap, r, t=t, to=dst if hop is None else hop, narr=narr, far=far):
+            def fn():
+                sent[0] += write(g, T, topo, core, to, ap, kind, t)
+                return []
+            op("g", fn, r, ["m%s%d" % (kind, t)], far, n=0, hold=1500)
+            op("x", None, ["m%s%d" % (kind, t)], ["l%s%d" % (kind, t)], 0, sem="a%s%d" % (kind, t), n=narr)
+
+        if 1 <= t <= 4:
+            zn = (T.zr1, 1) if t % 2 else (T.zr0, 0)
+            for k in range(16):
+                op("g", lambda k=k, zn=zn, t=t: [g.affine_select(zn[0][:, k::16], T.zs[:, 256 * t:256 * t + 256], [[0, 256]], AL.is_ge, 0.0, 0, 0)],
+                   ["z%d0" % t, "z%d1" % t], ["zr%d%d" % (zn[1], k)], 210 + 512 * CYC)
+        vkeys = ring + ["V0a", "V0b"] + ["VL%d" % s for s in range(min(t, 4))] + ["lF%d" % s for s in range(min(t, 4))]
+        for h in (1, 0):
+            M, G, D = T["M%d" % h], T["G%d" % h], T["D%d" % h]
+            pK, pD, kK, kD = T["pK%d" % h], T["pD%d" % h], "pK%d" % h, "pD%d" % h
+            hs = slice(128 * h, 128 * h + 128)
+            mvn, mvo = 256 * (t % 2) + 128 * h, 256 * (1 - t % 2) + 128 * h
+            first = [(pK[:, 0:128], T.I1[:], T.TB[:], True, False)]
+            if t:
+                first.append((pK[:, 0:128], T.I1[:], T.mv[:, mvo:mvo + 128], False, False))
+            mm(first, ["I1", "TB", "mv%d%d" % (1 - t % 2, h)], [kK], 256)
+            mm([(pD[:, 0:128], T.I1[:], T.zer[:], True, False)], ["I1", "zer"], [kD], 128)
+            for q in range(8):
+                off = T.soff[:, 128 * h + 16 * q:128 * h + 16 * q + 16]
+                e0 = 2048 * h + 256 * q
+                act(G[:, q, :], T.P[:, 0:2064].indirect(off), AF.Identity, Pk + ["soff%d" % h, "BS"], ["G%d%d" % (h, q)],
+                    65 + 256 * GATH, bias=T.BS[:, t:t + 1])
+                tt(M[:, q, :], T.X[:, 0:2064].indirect(off), zr[:, e0:e0 + 256], AL.max,
+                   ["X", "Xs", "soff%d" % h] + zrk, ["M%d%d" % (h, q)], 50 + 256 * GATH)
+            for q in (0, 1):
+                qs = range(4 * q, 4 * q + 4)
+                o = slice(64 * q, 64 * q + 64)
+                mm([(pD[:, o], T.ZD[:, 15 - a:143 - a], G[:, 4 * q:4 * q + 4, 16 * a:16 * a + 16], False, q == 1 and a == 15) for a in range(16)],
+                   ["ZD"] + ["G%d%d" % (h, x) for x in qs], [kD], 1024)
+                mm([(pK[:, o], T.ZM[:, 15 - a:143 - a], M[:, 4 * q:4 * q + 4, 16 * a:16 * a + 16], False, False) for a in range(16)],
+                   ["ZM"] + ["M%d%d" % (h, x) for x in qs], [kK], 1024)
+                mm([(pK[:, o], T.ZR[:, 15 - a:143 - a], G[:, 4 * q:4 * q + 4, 16 * a:16 * a + 16], False, False) for a in range(16)],
+                   ["ZR"] + ["G%d%d" % (h, x) for x in qs], [kK], 1024)
+            mvk = "mv%d%d" % (t % 2, h)
+            mv = T.mv[:, mvn:mvn + 128]
+            H = str(h)
+            tt(mv, pD[:, 0:128], thb[:], AL.is_gt, [kD, thk], [mvk], 128)
+            mm([(pK[:, 0:128], T.I1[:], mv, False, True)], ["I1", mvk], [kK], 128)
+            nB = T.pN[:, 8 * h:8 * h + 8]
+            mm([(nB, T.I8[:], T.mv[:, mvn + k:mvn + 128:16], k == 0, k == 15) for k in range(16)], ["I8", mvk], ["pN"], 1024)
+            scan(T.pm[:, hs], T.mk0[:, 0:128], pK[:, 0:128], AL.mult, AL.max, ["mk0", kK], ["pm" + H], 128)
+            tt(T.fg[:, hs], pK[:, 0:128], T.pm[:, hs], AL.is_equal, [kK, "pm" + H], ["fg" + H], 128)
+            tt(T.fd[:, hs], pD[:, 0:128], T.fg[:, hs], AL.mult, [kD, "fg" + H], ["fd" + H], 128)
+            ts(T.nf[:, hs], T.fg[:, hs], -1.0, 1.0, AL.mult, AL.add, ["fg" + H], ["nf" + H], 64)
+            tt(T.bo[:, 8 * h:8 * h + 8], nB, tl(LIM, h), AL.is_gt, ["pN", "lim"], ["bo" + H], 8)
+            tt(tl(EE, h), tl(SNN, h), nB, AL.subtract, ["pN", "snn"], ["ee" + H], 8)
+            scan(T.s2[:, hs], T.nf[:, hs], T.fd[:, hs], AL.mult, AL.add, ["nf" + H, "fd" + H], ["s2" + H], 128)
+            ia, ib = T.ti[:, 16 + 8 * h:24 + 8 * h], T.ti[:, 32 + 8 * h:40 + 8 * h]
+            tt(ia, T.s2[:, 128 * h + 15:128 * h + 128:16], T.bo[:, 8 * h:8 * h + 8], AL.mult, ["s2" + H, "bo" + H], ["ia" + H], 16)
+            ts(ib, ia, 4095, None, AL.bitwise_and, None, ["ia" + H], ["ib" + H], 8)
+            tt(tl(T3, h), ib, tl(EE, h), AL.max, ["ib" + H, "ee" + H], ["t3" + H], 16)
+            fo = T.lst[:, 8 * h:8 * h + 8]
+            cp(fo, tl(T3, h), ["t3" + H], ["fo" + H], 8)
+            cp(T.fu[:, hs], T.VT[:, 0:VLOG + 256 * min(t, 4)].indirect(fo), vkeys + ["fo" + H], ["fu" + H], 50 + 128 * GATH)
+        for h in (1, 0):
+            D, H = T["D%d" % h], str(h)
+            hs = slice(128 * h, 128 * h + 128)
+            ia, ib = T.ti[:, 16 + 8 * h:24 + 8 * h], T.ti[:, 32 + 8 * h:40 + 8 * h]
+            p0 = 0
+            ND = len(DCH[h])
+            for q, (n, who) in enumerate(DCH[h]):
+                dq = D[:, p0:p0 + n]
+                src = T.X[:, 0:2064].indirect(T.fu[:, 128 * h + p0 // 16:128 * h + (p0 + n) // 16])
+                if who == "s":
+                    act(dq, src, AF.Copy, ["X", "Xs", "fu" + H], ["D%d%d" % (h, q)], 65 + n * GATH)
+                else:
+                    cp(dq, src, ["X", "Xs", "fu" + H], ["D%d%d" % (h, q)], 50 + n * GATH)
+                e = slice(2048 * h + p0, 2048 * h + p0 + n)
+                scan(T.MX[:, e], T.mk0[:, 0:n], dq, AL.mult, AL.max, ["mk0", "D%d%d" % (h, q)], ["MX%d%d" % (h, q)], n // 2)
+                scan(T.MN[:, e], T.mkB[:, 0:n], dq, AL.add, AL.min, ["mkB", "D%d%d" % (h, q)], ["MN%d%d" % (h, q)], n // 2)
+                p0 += n
+            ts(tl(NH, h), tl(T3, h), 0.0, SPARE, AL.is_equal, AL.mult, ["t3" + H], ["nh" + H], 8)
+            if h == 0:
+                tt(tl(CE, 0), tl(BASE, 0), tl(NH, 0), AL.add, ["base", "nh0"], ["ce"], 16)
+            if h:
+                Fi, fk = T.fs[:, 128 * t:128 * t + 128], "fs%d" % t
+            elif t < 4:
+                Fi, fk = T.VT[:, VLOG + 256 * t:VLOG + 256 * t + 128], "VL%d" % t
+            elif t == 4:
+                Fi, fk = T.VT[:, V0:V0 + 128], "V0a"
+            else:
+                Fi, fk = T.fe[:], "fe"
+            cp(Fi, T.fu[:, hs], ["fu" + H], [fk], 128)
+            if h and not last:
+                send("F", Fi, [fk])
+            ends = slice(2048 * h + 15, 2048 * h + 2048, 16)
+            zo, zn_ = T.zs[:, 256 * t + 128 * h:256 * t + 128 * h + 128], T.zs[:, 256 * (t + 1) + 128 * h:256 * (t + 1) + 128 * h + 128]
+            zk = "z%d%d" % (t + 1, h)
+            mm([(T.pY[:, 0:256], T.one[0:1, :], T.cY[0:1, :], True, False), (T.pY[:, 0:128], T.In[:], zo, False, False)],
+               ["one", "cY", "In", "z%d%d" % (t, h)], ["pY"], 384)
+            mm([(T.pY[:, 0:128], T.Ih[:], T.MX[:, ends], False, False), (T.pY[:, 128:256], T.Ih[:], T.MX[:, ends], False, False),
+                (T.pY[:, 0:128], T.Ih[:], T.MN[:, ends], False, False), (T.pY[:, 128:256], T.Ih[:], T.MN[:, ends], False, True)],
+               ["Ih"] + ["M%s%d%d" % (x, h, q) for x in "XN" for q in range(ND)], ["pY"], 512)
+            yo, yk = (T.ysn[:, 136 * t:136 * t + 128], "ya%d" % t) if h else (T.W[:, 264 * t:264 * t + 128], "W%d" % t)
+            act(T.dz[:, 256 * h:256 * h + 256], T.pY[:, 0:256], AF.Identity, ["pY", "m1"], ["dz" + H], 256, bias=c(40))
+            act(zn_, T.dz[:, 256 * h:256 * h + 128], AF.Abs, ["dz" + H, "m1"], [zk], 128, bias=c(41))
+            act(yo, T.dz[:, 256 * h + 128:256 * h + 256], AF.Identity, ["dz" + H, "m1"], [yk], 128, bias=c(41))
+            z0c = 256 * (t + 1) + 128 * h
+            mm([(T.pV[:, 256:264], T.ZW[:, 15 - a:143 - a], T.zs[:, z0c + a:z0c + 128:16], a == 0, a == 15) for a in range(16)],
+               ["ZW", zk], ["pV"], 1024)
+            mm([(T.pU[:, 0:256], T.one[0:2, :], T.cU[0:2, :], True, False), (T.pU[:, 0:128], T.BW[:], zn_, False, False),
+                (T.pU[:, 128:256], T.BW[:], zn_, False, True)], ["one", "cU", "BW", zk], ["pU"], 512)
+            cp(ia, T.pV[:, 256:264], ["pV"], ["ia" + H], 8)
+            ts(ib, ia, 7, None, AL.bitwise_and, None, ["ia" + H], ["ib" + H], 8)
+            if h:
+                tt(T.ysn[:, 136 * t + 128:136 * t + 136], ib, tl(NH, h), AL.add, ["ib" + H, "nh" + H], ["yb%d" % t], 16)
+                send("Y", T.ysn[:, 136 * t:136 * t + 136], ["ya%d" % t, "yb%d" % t])
+            else:
+                tt(tl(OFF, 0), ib, tl(CE, 0), AL.add, ["ib0", "ce"], ["off0"], 16)
+            act(T.r0[:, hs], T.pU[:, 0:128], AF.Identity, ["pU", "m1"], ["r0" + H], 128, bias=c(42))
+            act(T.rr[:, hs], T.r0[:, hs], AF.Identity, ["r0" + H, "m1"], ["rr" + H], 128, bias=c(43))
+            tt(T.pU[:, 256:384], T.pU[:, 128:256], T.rr[:, hs], AL.subtract, ["rr" + H], ["pU"], 128)
+            tt(T.pr[:, hs], T.pU[:, 256:384], Fi, AL.mult, ["pU", fk], ["pr" + H], 128)
+            ts(T.qi[:, hs], T.pr[:, hs], c(C32 + t), None, AL.add, None, ["pr" + H, "c32%d" % t], ["qi" + H], 128)
+            s1 = RING + 256 * ((t + 1) % 3) + 128 * h
+            if h == 0:
+                tt(tl(SNN), tl(SPTR), tl(NH), AL.min, ["sptr", "nh0", "nh1"], ["snn"], 32)
+                tt(tl(SP2), tl(NP0 + (t + 1) % 3), tl(NH), AL.subtract, ["np%d" % ((t + 1) % 3), "nh0", "nh1"], ["sp2"], 32)
+                tt(tl(SPTR), tl(SNN), tl(SP2), AL.max, ["snn", "sp2"], ["sptr"], 32)
+                if not last:
+                    next_lists()
+                    ts(tl(LIM), T.pN[:, 0:16], 0.0, 8192.0, AL.is_equal, AL.mult, ["pN"], ["lim"], 16)
+                    pA = T.pN[:, 16:32]
+                    mm([(pA, T.o4[:], T.bo[:], True, True)], ["o4", "bo0", "bo1"], ["pN"], 64)
+                    op("s", lambda pA=pA: [S.activation(tl(13), pA, AF.Copy, accum_out=c(A4))], ["pN"], ["a4"], 250)
+                    ts(T.ti[:, 2:3], c(A4), 2.0 ** -17, -0.484375, AL.mult, AL.add, ["a4"], ["aq"], 1)
+                    act(c(C32 + t + 1), c(A4), AF.Identity, ["a4", "b37"], ["c32%d" % (t + 1)], 1, bias=c(B37), scale=2.0 ** -7)
+                    ts(c(AQ), T.ti[:, 2:3], -131072.0, c(A4), AL.mult, AL.add, ["aq", "a4"], ["am"], 1)
+                    act(T.thT[:], T.th0[:], AF.Identity, ["th0", "am"], ["thT"], 128, bias=c(AQ))
+            ts(T.VT[:, s1:s1 + 128], T.qi[:, hs], 5, 2047, AL.arith_shift_right, AL.bitwise_and, ["qi" + H], ["S%d%d" % ((t + 1) % 3, h)], 128)
+        tt(tl(OFF, 1), T.W[:, 264 * t + 256:264 * t + 264], tl(BASE, 1), AL.add, ["lY%d" % t, "base"], ["off1"], 16)
+        for hh in ([(0, 1)] if JOINT[0 if hop is None else 1] else [(0,), (1,)]):
+            a0, n, H = 128 * hh[0], 128 * len(hh), str(hh[0])
+            cs = slice(a0, a0 + n)
+            Y = T.W[:, 264 * t + a0:264 * t + a0 + n]
+            yk = [("W%d" % t, "lY%d" % t)[h] for h in hh]
+            wo = T.lst[:, 16 + a0 // 16:16 + (a0 + n) // 16]
+            wk = ["wo%d" % h for h in hh]
+            cp(wo, T.tf[:, 16 * OFF + a0 // 16:16 * OFF + (a0 + n) // 16], ["off%d" % h for h in hh], wk, 16)
+            if not last:
+                pa, pb, ka, kb = T["pK" + H][:, 0:n], T["pD" + H][:, 0:n], "pK" + H, "pD" + H
+                tt(T.dd[:, cs], T.X[:].indirect(wo), Y, AL.max, ["X", "Xs", "Xt"] + wk + yk, ["dd" + H], 50 + n * GATH)
+                act(T.ad[:, cs], T.P[:].indirect(wo), AF.Copy, Pk + ["Pt"] + wk, ["ad" + H], 65 + n * GATH)
+            cp(T.X[:].indirect(wo), Y, wk + yk, ["X", "Xs", "Xt"], 50 + n * SCAT)
+            if not last:
+                mm([(pb, T.Bc[:], T.CI[:, cs], True, False), (pb, T.WB[:, 0:128], Y, False, False)], ["Bc", "CI", "WB"] + yk, [kb], 2 * n)
+                mm([(pa, T.WA[:, 0:128], Y, True, False)], ["WA"] + yk, [ka], n)
+                mm([(pa, T.WA[:, 128:256], T.dd[:, cs], False, False), (pa, T.WA[:, 256:384], T.ad[:, cs], False, True)], ["dd" + H, "ad" + H], [ka], 2 * n)
+                mm([(pb, T.WB[:, 128:256], T.dd[:, cs], False, False), (pb, T.WB[:, 256:384], T.ad[:, cs], False, True)], ["dd" + H, "ad" + H], [kb], 2 * n)
+                ts(T.ra[:, cs], pa, 16 * M1, 16 * M1, AL.add, AL.subtract, [ka], ["ra" + H], n)
+                act(T.rb[:, cs], pb, AF.Identity, [kb, "BJ"], ["rb" + H], n, bias=T.col[:, 48 + t:49 + t])
+                tt(T.P[:].indirect(wo), T.rb[:, cs], T.ra[:, cs], AL.subtract, wk + ["ra" + H, "rb" + H], Pk + ["Pt"], 50 + n * SCAT)
+        if t == 4:
+            cp(T.VT[:, V0 + 128:V0 + 256], T.fl4[:], ["lF4"], ["V0a"], 128)
+    cp(T.lst[:, 32:48], tl(SPTR), ["sptr"], ["sl"], 16)
+    cp(T.pr[:], T.VT[:, 0:V0].indirect(T.lst[:, 32:48]), ring + ["sl"], ["pr0", "pr1"], 50 + 256 * GATH)
+    for h in (0, 1):
+        act(T.yso[:, h::2], T.pr[:, 128 * h:128 * h + 128], AF.Copy, ["pr0", "pr1"], ["yso%d" % h], 128)
+        act(T.yzo[:, h::2], T.zs[:, 256 * TS + 128 * h:256 * TS + 128 * h + 128], AF.Copy, ["z%d%d" % (TS, h)], ["yzo%d" % h], 128)
+    dma("y", "ox", T.yx[:], T.X[:, 0:2048], ["X"], [], 4500)
+    dma("s", "oz", T.yz[:], T.yzo[:], ["yzo0", "yzo1"], [], 2200)
+    dma("s", "os_", T.ys[:], T.yso[:], ["yso0", "yso1"], [], 2400)
+    return ops, sent
+
+
+def depend(ops):
+    lw, rd, deps = {}, {}, []
+    for i, o in enumerate(ops):
+        r = [k for k in o[2] if k[:2] not in ("pK", "pD", "pN", "pY", "pU", "pV") or len(k) > 3]
+        w = o[3] + [k for k in o[2] if k not in r]
+        d = set()
+        for k in r:
+            if k in lw:
+                d.add(lw[k])
+        for k in w:
+            if k in lw:
+                d.add(lw[k])
+            d.update(rd.get(k, ()))
+        for k in r:
+            rd.setdefault(k, []).append(i)
+        for k in w:
+            lw[k] = i
+            rd[k] = []
+        d.discard(i)
+        deps.append(sorted(d))
+    return deps
+
+
+def order(ops, deps):
+    n = len(ops)
+    succ = [[] for _ in range(n)]
+    for i in range(n):
+        for d in deps[i]:
+            succ[d].append(i)
+    prio = [0.0] * n
+    for i in range(n - 1, -1, -1):
+        prio[i] = ops[i][4] + max([LAT + prio[s] for s in succ[i]] + [0.0])
+    x = SEED[0]
+    for i in range(n):
+        x = (x * 1103515245 + 12345) % 2147483648
+        prio[i] += SEED[1] * (x / 2147483648.0 - 0.5)
+    left = [len(d) for d in deps]
+    ready_at = [0.0] * n
+    ready = [i for i in range(n) if not left[i]]
+    free = {}
+    out, end, starts = [], 0.0, []
+    while ready:
+        t0, e = min((max(ready_at[i], free.get(ops[i][0], 0.0)), ops[i][0]) for i in ready)
+        mine = sorted((i for i in ready if ops[i][0] == e), key=lambda i: -prio[i])
+        limit = 1e30
+        for i in mine:
+            st = max(ready_at[i], t0)
+            if st <= t0 + ALPHA[1] and st + ops[i][7] <= limit + ALPHA[0] * prio[i]:
+                break
+            limit = min(limit, st + ALPHA[2] - ALPHA[0] * prio[i])
+        else:
+            i = mine[0]
+            st = max(ready_at[i], t0)
+        ready.remove(i)
+        out.append(i)
+        starts.append(st)
+        free[ops[i][0]] = st + ops[i][7]
+        end = max(end, st + ops[i][4])
+        for s in succ[i]:
+            lat = 0.0 if ops[i][0] == "p" and ops[s][0] == "p" else LAT
+            ready_at[s] = max(ready_at[s], st + ops[i][4] + lat)
+            left[s] -= 1
+            if not left[s]:
+                ready.append(s)
+    return out, end, starts
+
+
+CACHE = {}
+
+
+def rank_program(g, core, T, topo):
+    rank = T.rank_of(core)
+    if rank is None:
+        helper_program(g, core, T, topo)
+        return
+    ops, sent = plan(g, core, T, topo, rank)
+    if "o" not in CACHE:
+        d = depend(ops)
+        CACHE["o"] = (d,) + order(ops, d)
+        CACHE["ops"] = ops
+    deps, seq = CACHE["o"][0], CACHE["o"][1]
+    Q = {"v": g.vector, "s": g.scalar, "p": g.tensor, "g": g, "y": g.sync}
+    count, mark, seen = {}, {}, {}
+    for i in seq:
+        e, fn, sem, n = ops[i][0], ops[i][1], ops[i][5], ops[i][6]
+        if e == "x":
+            mark[i] = (sem, n)
+            count[sem] = n
+            continue
+        need = {}
+        for d in deps[i]:
+            if d in mark and not (e == "p" and ops[d][0] == "p"):
+                s, v = mark[d]
+                need[s] = max(need.get(s, 0), v)
+        for s in sorted(need):
+            if seen.get((e, s), 0) < need[s]:
+                Q[e].wait_ge(T.sem[s], need[s])
+                seen[(e, s)] = need[s]
+        ins = fn()
+        if n:
+            s = sem or "c" + e
+            for x in ins:
+                x.then_inc(T.sem[s], n if sem else 1)
+            count[s] = count.get(s, 0) + n
+            mark[i] = (s, count[s])
+    count["sent"] = sent[0]
+    for s in sorted(count):
+        g.wait_ge(T.sem[s], count[s])

@@ -9,10 +9,14 @@ VW = VLOG + 4 * 256
 SPARE = 2304.0
 M1 = 12582912.0
 M2 = M1 * 2048.0
-DCH = {0: [(256, "s"), (256, "v"), (512, "s"), (512, "s"), (256, "s"), (256, "v")], 1: [(512, "s"), (512, "s"), (512, "s"), (256, "s"), (256, "s")]}
-ALPHA = [-0.05, 30, 150]
-FAR = [4000, 6500]
+DCH = {0: [(256, "s"), (256, "v"), (512, "s"), (512, "s"), (256, "s"), (256, "v")], 1: [(256, "s")] * 8}
+ALPHA = [-0.05, 30, 200]
+FAR = [4500, 8000]
 SEED = [3097, 1500]
+NFS = [True, True]
+PS = [2, 5]
+PASSES = [1]
+UNITS = [(1, (0,), 1), (1, (1,), 0), (0, (0,), 1), (0, (1,), 0)]
 JOINT = [True, False]
 
 bf, f32, i32, u16 = "bfloat16", "float32", "int32", "uint16"
@@ -25,7 +29,7 @@ SCRATCH = {
     "M0": ("sbuf", [128, 8, 256], bf), "M1": ("sbuf", [128, 8, 256], bf), "G0": ("sbuf", [128, 8, 256], bf), "G1": ("sbuf", [128, 8, 256], bf),
     "D0": ("sbuf", [128, 2048], bf), "D1": ("sbuf", [128, 2048], bf),
     "MX": ("sbuf", [128, 4096], bf), "MN": ("sbuf", [128, 4096], bf),
-    "mk0": ("sbuf", [128, 1024], bf), "mkB": ("sbuf", [128, 1024], bf),
+    "mk0": ("sbuf", [128, 512], bf), "mkB": ("sbuf", [128, 512], bf), "If": ("sbuf", [128, 128], f32),
     "soff": ("sbuf", [128, 256], u16), "fu": ("sbuf", [128, 256], u16), "lst": ("sbuf", [128, 64], u16),
     "fs": ("sbuf", [128, 6 * 128], i32), "fe": ("sbuf", [128, 128], i32), "fl4": ("sbuf", [128, 128], i32),
     "ysn": ("sbuf", [128, 6 * 136], bf), "W": ("sbuf", [128, 6 * 264], bf),
@@ -33,23 +37,23 @@ SCRATCH = {
     "fd": ("sbuf", [128, 256], f32), "s2": ("sbuf", [128, 256], f32),
     "dz": ("sbuf", [128, 512], f32), "r0": ("sbuf", [128, 256], f32), "rr": ("sbuf", [128, 256], f32), "pr": ("sbuf", [128, 256], f32), "qi": ("sbuf", [128, 256], i32),
     "dd": ("sbuf", [128, 256], bf), "ad": ("sbuf", [128, 256], bf), "t1": ("sbuf", [128, 512], bf),
-    "tf": ("sbuf", [128, 256], f32), "ti": ("sbuf", [128, 64], i32), "bo": ("sbuf", [128, 16], bf),
+    "tf": ("sbuf", [128, 256], f32), "ti": ("sbuf", [128, 96], i32), "bo": ("sbuf", [128, 16], bf),
     "col": ("sbuf", [128, 64], f32), "BI": ("sbuf", [128, 16], f32), "BS": ("sbuf", [128, 16], f32),
     "th0": ("sbuf", [128, 128], f32), "thT": ("sbuf", [128, 128], f32), "dkf": ("sbuf", [128, 128], f32), "Bf": ("sbuf", [128, 128], f32),
     "CI": ("sbuf", [128, 256], bf), "KI": ("sbuf", [128, 128], bf), "GI": ("sbuf", [128, 128], bf), "HI": ("sbuf", [128, 128], bf),
     "ZM": ("sbuf", [128, 144], bf), "ZR": ("sbuf", [128, 144], bf), "ZD": ("sbuf", [128, 144], bf), "ZW": ("sbuf", [128, 144], bf), "Z8": ("sbuf", [128, 144], bf),
-    "I1": ("sbuf", [128, 128], bf), "Ih": ("sbuf", [128, 128], bf), "In": ("sbuf", [128, 128], bf), "I8": ("sbuf", [128, 128], bf),
+    "I1": ("sbuf", [128, 128], bf), "Ih": ("sbuf", [128, 128], bf), "In": ("sbuf", [128, 128], bf),
     "BW": ("sbuf", [128, 128], bf), "BX": ("sbuf", [128, 128], bf), "Bc": ("sbuf", [128, 128], bf),
     "one": ("sbuf", [128, 128], bf), "o4": ("sbuf", [128, 128], bf), "TB": ("sbuf", [128, 128], bf),
-    "cY": ("sbuf", [128, 256], bf), "cU": ("sbuf", [128, 256], bf), "zer": ("sbuf", [128, 128], bf),
+    "cY": ("sbuf", [128, 256], bf), "cU": ("sbuf", [128, 256], bf), "nn": ("sbuf", [128, 256], bf),
     "yso": ("sbuf", [128, 256], f32), "yzo": ("sbuf", [128, 256], bf),
     "pK0": ("psum", [128, 512], f32), "pK1": ("psum", [128, 512], f32), "pD0": ("psum", [128, 512], f32), "pD1": ("psum", [128, 512], f32),
     "pN": ("psum", [128, 512], f32), "pY": ("psum", [128, 512], f32), "pU": ("psum", [128, 512], f32), "pV": ("psum", [128, 512], f32),
 }
-DMAS = ["reg", "vw", "scan", "z0", "wt", "th", "warm", "oz", "os_", "ox"]
+DMAS = ["reg", "rega", "vw", "scan", "z0", "wt", "th", "warm", "oz", "os_", "ox"]
 SEMAPHORES = (["cv", "cs", "cp", "cg", "sent"] + ["d" + n for n in DMAS]
               + ["aF%d" % t for t in range(TS)] + ["aY%d" % t for t in range(TS)])
-CYC, PCYC, GATH, SCAT, LAT = 1.04, 0.52, 1.56, 3.8, 110.0
+CYC, PCYC, GATH, SCAT, LAT = 0.95, 0.48, 1.56, 3.8, 160
 
 
 def route(T, topo, r, t):
@@ -140,13 +144,14 @@ def plan(g, core, T, topo, rank):
         return T.tf[:, 16 * j:16 * j + 16] if h is None else T.tf[:, 16 * j + 8 * h:16 * j + 8 * h + 8]
     NP0, BASE, SNN, SPTR, LIM, T3, NH, EE, SP2, OFF, CE = 0, 3, 4, 5, 6, 7, 8, 9, 10, 11, 12
 
-    dma("y", "reg", T.X[:, 0:2048], T.reg[:], [], ["X"], 4500)
+    dma("y", "rega", T.X[:, 0:1024], T.reg[:, 0:1024], [], ["Xa"], 3300)
+    dma("y", "reg", T.X[:, 1024:2048], T.reg[:, 1024:2048], [], ["X"], 4300)
     dma("s", "z0", T.zin[:], T.z0[:], [], ["zin"], 2200)
     dma("s", "scan", T.sci[:], T.scan[:], [], ["sci"], 2400)
     dma("s", "warm", T.wai[0:8, :], T.warm[:], [], ["wai"], 2400)
     dma("s", "wt", T.wti[:, 0:1], T.wt[:], [], ["wti"], 2500)
     dma("s", "th", T.thi[:, 0:1], T.th[:], [], ["thi"], 2600)
-    dma("y", "vw", T.vwi[:], T.vw[:], [], ["vwi"], 7000)
+    dma("y", "vw", T.vwi[:], T.vw[:], ["Xa"], ["vwi"], 4300)
     iota(T.ti[:, 0:1], [[0, 1]], 0, 1, ["ti0"], 1, small=False)
     iota(T.CI[:], [[1, 256]], 0, 0, ["CI"], 256)
     iota(T.KI[:], [[0, 8], [1, 16]], 0, 0, ["KI"], 128)
@@ -159,15 +164,16 @@ def plan(g, core, T, topo, rank):
     iota(T.X[:, 2064:XW], [[0, XW - 2064]], 0, 0, ["Xt"], XW - 2064)
     iota(T.P[:, 2064:XW], [[0, XW - 2064]], 0, 0, ["Pt"], XW - 2064)
     ms(T.VT[:, 0:RING], 2048, ["VTd"], 16)
-    ms(T.VT[:, RING + 256:V0], 0, ["S10", "S11", "S20", "S21"], 512)
-    ms(T.mk0[:], 1.0, ["mk0"], 512); ms(T.mk0[:, ::16], 0.0, ["mk0"], 32)
-    ms(T.mkB[:], 0.0, ["mkB"], 512); ms(T.mkB[:, ::16], 256.0, ["mkB"], 32)
-    ms(T.one[:], 1.0, ["one"], 64); ms(T.o4[:], 4096.0, ["o4"], 64); ms(T.zer[:], 0.0, ["zer"], 64)
+    iota(T.VT[:, RING + 256:V0], [[0, 512]], 0, 0, ["S10", "S11", "S20", "S21"], 512, small=False)
+    ms(T.mk0[:], 1.0, ["mk0"], 256); ms(T.mk0[:, ::16], 0.0, ["mk0"], 32)
+    ms(T.mkB[:], 0.0, ["mkB"], 256); ms(T.mkB[:, ::16], 256.0, ["mkB"], 32)
+    ms(T.one[:], 1.0, ["one"], 64); ms(T.o4[:], 4096.0, ["o4"], 64)
     ms(T.cY[0:1, :], -0.25, ["cY"], 128)
     ms(T.cU[0:2, 0:128], 0.5, ["cU"], 64); ms(T.cU[0:1, 0:128], -1024.0, ["cU"], 64); ms(T.cU[0:2, 128:256], 16.0, ["cU"], 64)
-    ms(tl(LIM), 8192.0, ["lim"], 16)
-    for j, v in enumerate((M1, -M1, M2, -M2)):
+    ms(tl(LIM), 1.0, ["mv200", "mv201", "mv210", "mv211"], 16)
+    for j, v in enumerate((M1, -M1, M2, SPARE)):
         ms(c(40 + j), v, ["m1"], 1)
+    ms(c(47), -0.484375, ["m1"], 1)
     cp(c(PF), T.ti[:, 0:1], ["ti0"], ["pf"], 1)
     ts(T.ti[:, 1:2], T.ti[:, 0:1], 15, None, AL.bitwise_and, None, ["ti0"], ["ti1"], 1)
     cp(c(LF), T.ti[:, 1:2], ["ti1"], ["lf"], 1)
@@ -200,7 +206,7 @@ def plan(g, core, T, topo, rank):
     for nm, s2, r in (("ZM", 2.0 ** -11, []), ("ZR", c(WR), ["wr"]), ("ZD", c(WD), ["wd"]), ("ZW", c(WF), ["wf"])):
         ts(T[nm][:], T.CI[:, 0:144], c(C15), s2, AL.is_equal, AL.mult, ["CI", "c15"] + r, [nm], 72)
     ts(T.Z8[0:8, :], T.CI[0:8, 0:144], T.col[0:8, P15:P15 + 1], None, AL.is_equal, None, ["CI", "p15"], ["Z8"], 72)
-    for nm, s2 in (("I1", 1.0), ("Ih", 0.5), ("In", -1.0), ("I8", 8192.0)):
+    for nm, s2 in (("I1", 1.0), ("Ih", 0.5), ("In", -1.0), ("If", 1.0)):
         ts(T[nm][:], T.CI[:, 0:128], c(PF), s2, AL.is_equal, AL.mult, ["CI", "pf"], [nm], 64)
     ts(T.BW[:], T.GI[:], c(GF), c(WF), AL.is_equal, AL.mult, ["GI", "gf", "wf"], ["BW"], 64)
     ts(T.Bf[:], T.GI[:], c(GF), None, AL.is_equal, None, ["GI", "gf"], ["Bf"], 128)
@@ -241,7 +247,7 @@ def plan(g, core, T, topo, rank):
         if k % 4 == 0:
             op("g", lambda k=k: [g.affine_select(T.zr0[:, k::16], T.zs[:, 0:256], [[0, 256]], AL.is_ge, 0.0, 0, 0)],
                ["z00", "z01"], ["zr0%d" % k], 210 + 512 * CYC)
-        elif k % 4 != 2 or k > 10:
+        elif k % 4 == 1 or k > 12:
             cp(T.zr0[:, k::16], T.zs[:, 0:256], ["z00", "z01"], ["zr0%d" % k], 128)
         else:
             act(T.zr0[:, k::16], T.zs[:, 0:256], AF.Copy, ["z00", "z01"], ["zr0%d" % k], 256)
@@ -250,9 +256,15 @@ def plan(g, core, T, topo, rank):
         sl = slice(256 * j, 256 * j + 256)
         tv = T.t1[:, 256 * (j % 2):256 * (j % 2) + 256]
         mm([(T[pb][:, 0:256], T.BX[:], T.X[:, sl], True, False), (T[pb][:, 0:256], T.Bc[:], T.CI[:], False, True)],
-           ["BX", "Bc", "CI", "X"], [pb], 512)
+           ["BX", "Bc", "CI", "X" if j > 3 else "Xa"], [pb], 512)
         act(tv, T[pb][:, 0:256], AF.Identity, [pb, "mlo", "BI"], ["t1%d" % (j % 2)], 256, bias=T.BI[:, j:j + 1], scale=c(MLO))
-        tt(T.P[:, sl], T[pb][:, 0:256], tv, AL.subtract, [pb, "t1%d" % (j % 2)], ["P%d" % j], 256)
+        if j in PS:
+            pc = ("pU", "pD1")[j % 2]
+            mm([(T[pc][:, 256:512], T.BX[:], T.X[:, sl], True, False), (T[pc][:, 256:512], T.Bc[:], T.CI[:], False, False),
+                (T[pc][:, 256:512], T.In[:], tv, False, True)], ["BX", "Bc", "CI", "In", "X" if j > 3 else "Xa", "t1%d" % (j % 2)], [pc], 768)
+            act(T.P[:, sl], T[pc][:, 256:512], AF.Copy, [pc], ["P%d" % j], 256)
+        else:
+            tt(T.P[:, sl], T[pb][:, 0:256], tv, AL.subtract, [pb, "t1%d" % (j % 2)], ["P%d" % j], 256)
     Pk = ["Ps"] + ["P%d" % j for j in range(8)]
     ts(T.VT[:, V0:V0 + 1024], T.vwi[:], 2047, None, AL.bitwise_and, None, ["vwi"], ["V0a"], 1024)
     ts(T.VT[:, V0 + 1024:V0 + 2048], T.vwi[:], 11, None, AL.logical_shift_right, None, ["vwi"], ["V0b"], 1024)
@@ -281,71 +293,83 @@ def plan(g, core, T, topo, rank):
                 op("g", lambda k=k, zn=zn, t=t: [g.affine_select(zn[0][:, k::16], T.zs[:, 256 * t:256 * t + 256], [[0, 256]], AL.is_ge, 0.0, 0, 0)],
                    ["z%d0" % t, "z%d1" % t], ["zr%d%d" % (zn[1], k)], 210 + 512 * CYC)
         vkeys = ring + ["V0a", "V0b"] + ["VL%d" % s for s in range(min(t, 4))] + ["lF%d" % s for s in range(min(t, 4))]
-        for h in (1, 0):
-            M, G, D = T["M%d" % h], T["G%d" % h], T["D%d" % h]
-            pK, pD, kK, kD = T["pK%d" % h], T["pD%d" % h], "pK%d" % h, "pD%d" % h
-            hs = slice(128 * h, 128 * h + 128)
-            mvn, mvo = 256 * (t % 2) + 128 * h, 256 * (1 - t % 2) + 128 * h
-            first = [(pK[:, 0:128], T.I1[:], T.TB[:], True, False)]
+        for h, qq, bank in UNITS:
+            M, G = T["M%d" % h], T["G%d" % h]
+            pK, pD, kK, kD = T["pK%d" % bank], T["pD%d" % bank], "pK%d" % bank, "pD%d" % bank
+            n, c0 = 64 * len(qq), 128 * h + 64 * qq[0]
+            hs = slice(c0, c0 + n)
+            mvn, mvo = 256 * (t % 2) + c0, 256 * (1 - t % 2) + c0
+
+            def kk(name, h=h, qq=qq):
+                return ["%s%d%d" % (name, h, q) for q in qq]
+            first = [(pK[:, 0:n], T.I1[:], T.TB[:, 0:n], True, False)]
             if t:
-                first.append((pK[:, 0:128], T.I1[:], T.mv[:, mvo:mvo + 128], False, False))
-            mm(first, ["I1", "TB", "mv%d%d" % (1 - t % 2, h)], [kK], 256)
-            mm([(pD[:, 0:128], T.I1[:], T.zer[:], True, False)], ["I1", "zer"], [kD], 128)
-            for q in range(8):
+                first.append((pK[:, 0:n], T.I1[:], T.mv[:, mvo:mvo + n], False, False))
+            mm(first, ["I1", "TB"] + kk("mv%d" % (1 - t % 2)), [kK], 2 * n)
+            for q in range(4 * qq[0], 4 * qq[-1] + 4):
                 off = T.soff[:, 128 * h + 16 * q:128 * h + 16 * q + 16]
                 e0 = 2048 * h + 256 * q
                 act(G[:, q, :], T.P[:, 0:2064].indirect(off), AF.Identity, Pk + ["soff%d" % h, "BS"], ["G%d%d" % (h, q)],
                     65 + 256 * GATH, bias=T.BS[:, t:t + 1])
                 tt(M[:, q, :], T.X[:, 0:2064].indirect(off), zr[:, e0:e0 + 256], AL.max,
-                   ["X", "Xs", "soff%d" % h] + zrk, ["M%d%d" % (h, q)], 50 + 256 * GATH)
-            for q in (0, 1):
+                   ["X", "Xa", "Xs", "soff%d" % h] + zrk, ["M%d%d" % (h, q)], 50 + 256 * GATH)
+            for q in qq:
                 qs = range(4 * q, 4 * q + 4)
-                o = slice(64 * q, 64 * q + 64)
-                mm([(pD[:, o], T.ZD[:, 15 - a:143 - a], G[:, 4 * q:4 * q + 4, 16 * a:16 * a + 16], False, q == 1 and a == 15) for a in range(16)],
+                o = slice(64 * (q - qq[0]), 64 * (q - qq[0]) + 64)
+                mm([(pD[:, o], T.ZD[:, 15 - a:143 - a], G[:, 4 * q:4 * q + 4, 16 * a:16 * a + 16], a == 0, a == 15) for a in range(16)],
                    ["ZD"] + ["G%d%d" % (h, x) for x in qs], [kD], 1024)
                 mm([(pK[:, o], T.ZM[:, 15 - a:143 - a], M[:, 4 * q:4 * q + 4, 16 * a:16 * a + 16], False, False) for a in range(16)],
                    ["ZM"] + ["M%d%d" % (h, x) for x in qs], [kK], 1024)
                 mm([(pK[:, o], T.ZR[:, 15 - a:143 - a], G[:, 4 * q:4 * q + 4, 16 * a:16 * a + 16], False, False) for a in range(16)],
                    ["ZR"] + ["G%d%d" % (h, x) for x in qs], [kK], 1024)
-            mvk = "mv%d%d" % (t % 2, h)
-            mv = T.mv[:, mvn:mvn + 128]
-            H = str(h)
-            tt(mv, pD[:, 0:128], thb[:], AL.is_gt, [kD, thk], [mvk], 128)
-            mm([(pK[:, 0:128], T.I1[:], mv, False, True)], ["I1", mvk], [kK], 128)
-            nB = T.pN[:, 8 * h:8 * h + 8]
-            mm([(nB, T.I8[:], T.mv[:, mvn + k:mvn + 128:16], k == 0, k == 15) for k in range(16)], ["I8", mvk], ["pN"], 1024)
-            scan(T.pm[:, hs], T.mk0[:, 0:128], pK[:, 0:128], AL.mult, AL.max, ["mk0", kK], ["pm" + H], 128)
-            tt(T.fg[:, hs], pK[:, 0:128], T.pm[:, hs], AL.is_equal, [kK, "pm" + H], ["fg" + H], 128)
-            tt(T.fd[:, hs], pD[:, 0:128], T.fg[:, hs], AL.mult, [kD, "fg" + H], ["fd" + H], 128)
-            ts(T.nf[:, hs], T.fg[:, hs], -1.0, 1.0, AL.mult, AL.add, ["fg" + H], ["nf" + H], 64)
-            tt(T.bo[:, 8 * h:8 * h + 8], nB, tl(LIM, h), AL.is_gt, ["pN", "lim"], ["bo" + H], 8)
-            tt(tl(EE, h), tl(SNN, h), nB, AL.subtract, ["pN", "snn"], ["ee" + H], 8)
-            scan(T.s2[:, hs], T.nf[:, hs], T.fd[:, hs], AL.mult, AL.add, ["nf" + H, "fd" + H], ["s2" + H], 128)
-            ia, ib = T.ti[:, 16 + 8 * h:24 + 8 * h], T.ti[:, 32 + 8 * h:40 + 8 * h]
-            tt(ia, T.s2[:, 128 * h + 15:128 * h + 128:16], T.bo[:, 8 * h:8 * h + 8], AL.mult, ["s2" + H, "bo" + H], ["ia" + H], 16)
-            ts(ib, ia, 4095, None, AL.bitwise_and, None, ["ia" + H], ["ib" + H], 8)
-            tt(tl(T3, h), ib, tl(EE, h), AL.max, ["ib" + H, "ee" + H], ["t3" + H], 16)
-            fo = T.lst[:, 8 * h:8 * h + 8]
-            cp(fo, tl(T3, h), ["t3" + H], ["fo" + H], 8)
-            cp(T.fu[:, hs], T.VT[:, 0:VLOG + 256 * min(t, 4)].indirect(fo), vkeys + ["fo" + H], ["fu" + H], 50 + 128 * GATH)
+            mvk = kk("mv%d" % (t % 2))
+            mv = T.mv[:, mvn:mvn + n]
+            b0, b1 = c0 // 16, (c0 + n) // 16
+
+            def tq(j, b0=b0, b1=b1):
+                return T.tf[:, 16 * j + b0:16 * j + b1]
+            tt(mv, pD[:, 0:n], thb[:, 0:n], AL.is_gt, [kD, thk], mvk, n)
+            mm([(pK[:, 0:n], T.I1[:], mv, False, True)], ["I1"] + mvk, [kK], n)
+            nB = T.nn[:, c0 + 15:c0 + n:16]
+            scan(T.nn[:, hs], T.mk0[:, 0:n], mv, AL.mult, AL.add, ["mk0"] + mvk, kk("nn"), n // 2)
+            lo, ln = (LIM, 14) if t % 2 == 0 else (14, LIM)
+            act(tq(ln), nB, AF.Relu, kk("nn"), kk("mv%d" % (3 - t % 2)), 8, bias=1.0, scale=-1.0)
+            scan(T.pm[:, hs], T.mk0[:, 0:n], pK[:, 0:n], AL.mult, AL.max, ["mk0", kK], kk("pm"), n)
+            tt(T.fg[:, hs], pK[:, 0:n], T.pm[:, hs], AL.is_equal, [kK] + kk("pm"), kk("fg"), n)
+            tt(T.fd[:, hs], pD[:, 0:n], T.fg[:, hs], AL.mult, [kD] + kk("fg"), kk("fd"), n)
+            if NFS[h]:
+                act(T.nf[:, hs], T.fg[:, hs], AF.Identity, kk("fg"), kk("nf"), n, bias=1.0, scale=-1.0)
+            else:
+                ts(T.nf[:, hs], T.fg[:, hs], -1.0, 1.0, AL.mult, AL.add, kk("fg"), kk("nf"), 64)
+            tt(T.bo[:, b0:b1], nB, tq(lo), AL.is_gt, kk("mv%d" % (2 + t % 2)) + kk("nn"), kk("bo"), 8)
+            tt(tq(EE), tq(SNN), tq(ln), AL.mult, kk("mv%d" % (3 - t % 2)) + ["snn"], kk("ee"), 8)
+            scan(T.s2[:, hs], T.nf[:, hs], T.fd[:, hs], AL.mult, AL.add, kk("nf") + kk("fd"), kk("s2"), n)
+            ia, ib = T.ti[:, 16 + b0:16 + b1], T.ti[:, 32 + b0:32 + b1]
+            tt(ia, T.s2[:, c0 + 15:c0 + n:16], T.bo[:, b0:b1], AL.mult, kk("s2") + kk("bo"), kk("ia"), 16)
+            ts(ib, ia, 4095, None, AL.bitwise_and, None, kk("ia"), kk("ib"), 8)
+            tt(tq(T3), ib, tq(EE), AL.max, kk("ib") + kk("ee"), kk("t3"), 16)
+            fo = T.lst[:, b0:b1]
+            cp(fo, tq(T3), kk("t3"), kk("fo"), 8)
+            cp(T.fu[:, hs], T.VT[:, 0:VLOG + 256 * min(t, 4)].indirect(fo), vkeys + kk("fo"), kk("fu"), 50 + n * GATH)
         for h in (1, 0):
             D, H = T["D%d" % h], str(h)
             hs = slice(128 * h, 128 * h + 128)
-            ia, ib = T.ti[:, 16 + 8 * h:24 + 8 * h], T.ti[:, 32 + 8 * h:40 + 8 * h]
+            ia, ib = T.ti[:, 48 + 8 * h:56 + 8 * h], T.ti[:, 64 + 8 * h:72 + 8 * h]
             p0 = 0
             ND = len(DCH[h])
             for q, (n, who) in enumerate(DCH[h]):
                 dq = D[:, p0:p0 + n]
                 src = T.X[:, 0:2064].indirect(T.fu[:, 128 * h + p0 // 16:128 * h + (p0 + n) // 16])
+                fuk = ["fu%d%d" % (h, x) for x in range(p0 // 1024, (p0 + n - 1) // 1024 + 1)]
                 if who == "s":
-                    act(dq, src, AF.Copy, ["X", "Xs", "fu" + H], ["D%d%d" % (h, q)], 65 + n * GATH)
+                    act(dq, src, AF.Copy, ["X", "Xs"] + fuk, ["D%d%d" % (h, q)], 65 + n * GATH)
                 else:
-                    cp(dq, src, ["X", "Xs", "fu" + H], ["D%d%d" % (h, q)], 50 + n * GATH)
+                    cp(dq, src, ["X", "Xs"] + fuk, ["D%d%d" % (h, q)], 50 + n * GATH)
                 e = slice(2048 * h + p0, 2048 * h + p0 + n)
                 scan(T.MX[:, e], T.mk0[:, 0:n], dq, AL.mult, AL.max, ["mk0", "D%d%d" % (h, q)], ["MX%d%d" % (h, q)], n // 2)
                 scan(T.MN[:, e], T.mkB[:, 0:n], dq, AL.add, AL.min, ["mkB", "D%d%d" % (h, q)], ["MN%d%d" % (h, q)], n // 2)
                 p0 += n
-            ts(tl(NH, h), tl(T3, h), 0.0, SPARE, AL.is_equal, AL.mult, ["t3" + H], ["nh" + H], 8)
+            act(tl(NH, h), tl(T3, h), AF.Relu, ["m1", "t3%d0" % h, "t3%d1" % h], ["nh" + H], 8, bias=c(43), scale=-SPARE)
             if h == 0:
                 tt(tl(CE, 0), tl(BASE, 0), tl(NH, 0), AL.add, ["base", "nh0"], ["ce"], 16)
             if h:
@@ -356,7 +380,7 @@ def plan(g, core, T, topo, rank):
                 Fi, fk = T.VT[:, V0:V0 + 128], "V0a"
             else:
                 Fi, fk = T.fe[:], "fe"
-            cp(Fi, T.fu[:, hs], ["fu" + H], [fk], 128)
+            cp(Fi, T.fu[:, hs], ["fu%d0" % h, "fu%d1" % h], [fk], 128)
             if h and not last:
                 send("F", Fi, [fk])
             ends = slice(2048 * h + 15, 2048 * h + 2048, 16)
@@ -368,25 +392,28 @@ def plan(g, core, T, topo, rank):
                 (T.pY[:, 0:128], T.Ih[:], T.MN[:, ends], False, False), (T.pY[:, 128:256], T.Ih[:], T.MN[:, ends], False, True)],
                ["Ih"] + ["M%s%d%d" % (x, h, q) for x in "XN" for q in range(ND)], ["pY"], 512)
             yo, yk = (T.ysn[:, 136 * t:136 * t + 128], "ya%d" % t) if h else (T.W[:, 264 * t:264 * t + 128], "W%d" % t)
-            act(T.dz[:, 256 * h:256 * h + 256], T.pY[:, 0:256], AF.Identity, ["pY", "m1"], ["dz" + H], 256, bias=c(40))
+            act(T.dz[:, 256 * h:256 * h + 128], T.pY[:, 0:128], AF.Identity, ["pY", "m1"], ["dz" + H], 128, bias=c(40))
+            act(T.dz[:, 256 * h + 128:256 * h + 256], T.pY[:, 128:256], AF.Identity, ["pY", "m1"], ["dy" + H], 128, bias=c(40))
             act(zn_, T.dz[:, 256 * h:256 * h + 128], AF.Abs, ["dz" + H, "m1"], [zk], 128, bias=c(41))
-            act(yo, T.dz[:, 256 * h + 128:256 * h + 256], AF.Identity, ["dz" + H, "m1"], [yk], 128, bias=c(41))
+            act(yo, T.dz[:, 256 * h + 128:256 * h + 256], AF.Identity, ["dy" + H, "m1"], [yk], 128, bias=c(41))
             z0c = 256 * (t + 1) + 128 * h
             mm([(T.pV[:, 256:264], T.ZW[:, 15 - a:143 - a], T.zs[:, z0c + a:z0c + 128:16], a == 0, a == 15) for a in range(16)],
                ["ZW", zk], ["pV"], 1024)
-            mm([(T.pU[:, 0:256], T.one[0:2, :], T.cU[0:2, :], True, False), (T.pU[:, 0:128], T.BW[:], zn_, False, False),
-                (T.pU[:, 128:256], T.BW[:], zn_, False, True)], ["one", "cU", "BW", zk], ["pU"], 512)
             cp(ia, T.pV[:, 256:264], ["pV"], ["ia" + H], 8)
+            mm([(T.pV[:, 0:128], T.one[0:2, :], T.cU[0:2, 0:128], True, False), (T.pV[:, 0:128], T.BW[:], zn_, False, True)],
+               ["one", "cU", "BW", zk], ["pV"], 256)
+            mm([(T.pU[:, 0:128], T.one[0:2, :], T.cU[0:2, 128:256], True, False), (T.pU[:, 0:128], T.BW[:], zn_, False, False)],
+               ["one", "cU", "BW", zk], ["pU"], 256)
             ts(ib, ia, 7, None, AL.bitwise_and, None, ["ia" + H], ["ib" + H], 8)
             if h:
                 tt(T.ysn[:, 136 * t + 128:136 * t + 136], ib, tl(NH, h), AL.add, ["ib" + H, "nh" + H], ["yb%d" % t], 16)
                 send("Y", T.ysn[:, 136 * t:136 * t + 136], ["ya%d" % t, "yb%d" % t])
             else:
                 tt(tl(OFF, 0), ib, tl(CE, 0), AL.add, ["ib0", "ce"], ["off0"], 16)
-            act(T.r0[:, hs], T.pU[:, 0:128], AF.Identity, ["pU", "m1"], ["r0" + H], 128, bias=c(42))
-            act(T.rr[:, hs], T.r0[:, hs], AF.Identity, ["r0" + H, "m1"], ["rr" + H], 128, bias=c(43))
-            tt(T.pU[:, 256:384], T.pU[:, 128:256], T.rr[:, hs], AL.subtract, ["rr" + H], ["pU"], 128)
-            tt(T.pr[:, hs], T.pU[:, 256:384], Fi, AL.mult, ["pU", fk], ["pr" + H], 128)
+            act(T.r0[:, hs], T.pV[:, 0:128], AF.Identity, ["pV", "m1"], ["r0" + H], 128, bias=c(42))
+            act(T.rr[:, hs], T.r0[:, hs], AF.Identity, ["r0" + H, "m1"], ["rr" + H], 128, bias=c(42), scale=-1.0)
+            mm([(T.pU[:, 0:128], T.If[:], T.rr[:, hs], False, True)], ["If", "rr" + H], ["pU"], 512)
+            tt(T.pr[:, hs], T.pU[:, 0:128], Fi, AL.mult, ["pU", fk], ["pr" + H], 128)
             ts(T.qi[:, hs], T.pr[:, hs], c(C32 + t), None, AL.add, None, ["pr" + H, "c32%d" % t], ["qi" + H], 128)
             s1 = RING + 256 * ((t + 1) % 3) + 128 * h
             if h == 0:
@@ -395,13 +422,14 @@ def plan(g, core, T, topo, rank):
                 tt(tl(SPTR), tl(SNN), tl(SP2), AL.max, ["snn", "sp2"], ["sptr"], 32)
                 if not last:
                     next_lists()
-                    ts(tl(LIM), T.pN[:, 0:16], 0.0, 8192.0, AL.is_equal, AL.mult, ["pN"], ["lim"], 16)
                     pA = T.pN[:, 16:32]
-                    mm([(pA, T.o4[:], T.bo[:], True, True)], ["o4", "bo0", "bo1"], ["pN"], 64)
+                    mm([(pA, T.o4[:], T.bo[:], True, True)], ["o4", "bo00", "bo01", "bo10", "bo11"], ["pN"], 64)
                     op("s", lambda pA=pA: [S.activation(tl(13), pA, AF.Copy, accum_out=c(A4))], ["pN"], ["a4"], 250)
-                    ts(T.ti[:, 2:3], c(A4), 2.0 ** -17, -0.484375, AL.mult, AL.add, ["a4"], ["aq"], 1)
+                    act(c(54), c(A4), AF.Identity, ["a4", "m1"], ["aq1"], 1, bias=c(47), scale=2.0 ** -17)
+                    act(c(55), c(54), AF.Identity, ["aq1", "m1"], ["aq2"], 1, bias=c(40))
+                    act(c(56), c(55), AF.Identity, ["aq2", "m1"], ["aq"], 1, bias=c(41))
                     act(c(C32 + t + 1), c(A4), AF.Identity, ["a4", "b37"], ["c32%d" % (t + 1)], 1, bias=c(B37), scale=2.0 ** -7)
-                    ts(c(AQ), T.ti[:, 2:3], -131072.0, c(A4), AL.mult, AL.add, ["aq", "a4"], ["am"], 1)
+                    act(c(AQ), c(56), AF.Identity, ["aq", "a4"], ["am"], 1, bias=c(A4), scale=-131072.0)
                     act(T.thT[:], T.th0[:], AF.Identity, ["th0", "am"], ["thT"], 128, bias=c(AQ))
             ts(T.VT[:, s1:s1 + 128], T.qi[:, hs], 5, 2047, AL.arith_shift_right, AL.bitwise_and, ["qi" + H], ["S%d%d" % ((t + 1) % 3, h)], 128)
         tt(tl(OFF, 1), T.W[:, 264 * t + 256:264 * t + 264], tl(BASE, 1), AL.add, ["lY%d" % t, "base"], ["off1"], 16)
@@ -462,6 +490,23 @@ def depend(ops):
     return deps
 
 
+def tag(o):
+    def bare(k):
+        if k[:2] == "zr":
+            return "zr"
+        if k[:2] == "mv":
+            return "mv" + k[3:]
+        if (len(k) == 3 and k[0] in "zS" and k[1].isdigit()):
+            return k[:-2] + k[-1]
+        if k[:-1] in ("W", "ya", "yb", "fs", "VL", "c32", "mF", "mY", "lF", "lY"):
+            return k[:-1]
+        return k
+    return o[0] + bare(o[3][0] if o[3] else "") + bare(o[2][-1] if o[2] else "")
+
+
+SHIFT = ["PKQPM=`mNFKIXQOF?TETR`]RU9>POHa]`>LEdODQSV=1iMYCABTeBKV]]YADXD;[AKGDLSQ``iTWRZRYPBPSVTPIINFWQ@Y`QNaT;HpHP0GMSWKSLLEYJ]]:PDPc]<UJRJKU[Dg8F[OUULUSAURGS`[ODWX]PVPPUMMMOPPOJJNKSBMCUK>hnUMIBb@FGL>PMXVBLSDT[AO`I]VRT]QSPJS7LOPEPTMQI@MXGR[^Zb?kURP@IQMU]VgOMB2OSQeWL[OBXPM]QQ8X[PDLABJ[M`YZSWM>0DVCO]Rgg`MSTTIhXUOPPPR=QJBhHdJTMO>k]DT`KDYNEVPQFCgSj]NC]NHOM?PE]Y`aZJ9MM6PMHY?9QWC"]
+
+
 def order(ops, deps):
     n = len(ops)
     succ = [[] for _ in range(n)]
@@ -471,10 +516,10 @@ def order(ops, deps):
     prio = [0.0] * n
     for i in range(n - 1, -1, -1):
         prio[i] = ops[i][4] + max([LAT + prio[s] for s in succ[i]] + [0.0])
-    x = SEED[0]
+    tags = [tag(o) for o in ops]
+    shift = dict(zip(sorted(set(tags)), SHIFT[0]))
     for i in range(n):
-        x = (x * 1103515245 + 12345) % 2147483648
-        prio[i] += SEED[1] * (x / 2147483648.0 - 0.5)
+        prio[i] += 300.0 * (ord(shift.get(tags[i], "P")) - 80)
     left = [len(d) for d in deps]
     ready_at = [0.0] * n
     ready = [i for i in range(n) if not left[i]]
@@ -503,7 +548,41 @@ def order(ops, deps):
             left[s] -= 1
             if not left[s]:
                 ready.append(s)
-    return out, end, starts
+    best = (end, out, starts)
+    fin = {i: s + ops[i][4] for i, s in zip(out, starts)}
+    for _ in range(PASSES[0]):
+        fin = pack(ops, sorted(fin, key=lambda i: (-fin[i], -i)), succ, True)[1]
+        st, fin = pack(ops, sorted(fin, key=lambda i: (-fin[i], i)), deps, False)
+        if max(fin.values()) < best[0]:
+            o = sorted(st, key=lambda i: (st[i], i))
+            best = (max(fin.values()), o, [st[i] for i in o])
+    return best[1], best[0], best[2]
+
+
+def pack(ops, seq, before, back):
+    busy, start, fin = {}, {}, {}
+    for i in seq:
+        e, cost, hold = ops[i][0], ops[i][4], ops[i][7]
+        r = 0.0
+        for d in before[i]:
+            r = max(r, fin[d] + (0.0 if e == "p" and ops[d][0] == "p" else LAT))
+        if back:
+            r += cost - hold
+        b = busy.setdefault(e, [])
+        lo, hi = 0, len(b)
+        while lo < hi:
+            mid = (lo + hi) // 2
+            if b[mid][1] <= r:
+                lo = mid + 1
+            else:
+                hi = mid
+        while lo < len(b) and b[lo][0] < r + hold:
+            r = max(r, b[lo][1])
+            lo += 1
+        b.insert(lo, (r, r + hold))
+        start[i] = r
+        fin[i] = r + (hold if back else cost)
+    return start, fin
 
 
 CACHE = {}
@@ -521,22 +600,25 @@ def rank_program(g, core, T, topo):
         CACHE["ops"] = ops
     deps, seq = CACHE["o"][0], CACHE["o"][1]
     Q = {"v": g.vector, "s": g.scalar, "p": g.tensor, "g": g, "y": g.sync}
-    count, mark, seen = {}, {}, {}
+    count, mark, seen, known = {}, {}, {}, {}
+    place = {i: p for p, i in enumerate(seq)}
     for i in seq:
         e, fn, sem, n = ops[i][0], ops[i][1], ops[i][5], ops[i][6]
         if e == "x":
             mark[i] = (sem, n)
             count[sem] = n
+            known[i] = {}
             continue
-        need = {}
-        for d in deps[i]:
+        mine = seen.setdefault(e, {})
+        for d in sorted(deps[i], key=lambda d: -place[d]):
             if d in mark and not (e == "p" and ops[d][0] == "p"):
                 s, v = mark[d]
-                need[s] = max(need.get(s, 0), v)
-        for s in sorted(need):
-            if seen.get((e, s), 0) < need[s]:
-                Q[e].wait_ge(T.sem[s], need[s])
-                seen[(e, s)] = need[s]
+                if mine.get(s, 0) < v:
+                    Q[e].wait_ge(T.sem[s], v)
+                    mine[s] = v
+                for s2, v2 in known[d].items():
+                    mine[s2] = max(mine.get(s2, 0), v2)
+        known[i] = dict(mine)
         ins = fn()
         if n:
             s = sem or "c" + e

@@ -4,56 +4,56 @@ AL = AluOpType
 AF = ActivationFunctionType
 TS = 6
 XW = 4352
-RING, V0, VLOG = 16, 784, 2832
-VW = VLOG + 4 * 256
+RING, V0, VL, VW = (16, 2320, 2848), 272, (2576, 3104, 3376, 3648, 3920), 4192
 SPARE = 2304.0
 M1 = 12582912.0
-M2 = M1 * 2048.0
-DCH = {0: [(256, "s"), (256, "v"), (512, "s"), (512, "s"), (256, "s"), (256, "v")], 1: [(256, "s")] * 8}
-ALPHA = [-0.05, 30, 200]
-FAR = [4500, 8000]
-SEED = [3097, 1500]
-NFS = [True, True]
-PS = [2, 5]
-PASSES = [1]
-UNITS = [(1, (0,), 1), (1, (1,), 0), (0, (0,), 1), (0, (1,), 0)]
-JOINT = [True, False]
+UNITS = [("a", 1, 0, 4, 1, 1), ("b", 1, 4, 4, 0, 1), ("c", 0, 0, 4, 1, 1), ("d", 0, 4, 4, 0, 1)]
+DCH = {0: [(512, "s"), (512, "s"), (512, "v"), (512, "s")], 1: [(512, "s")] * 4}
+PSCAT = ["s"]
+WORD = [(0, 1), (0, 1)]
+EARLY = [100, 30]
+FIRST = ("one",)
+ORDER = """
+Ma0 P1+ Ma1 Ga0 Ma2 Ga1 Ma3 zr1 Ga2 Mb0 ZMa Ga3 Mc0 K0b Gb0 Mb1 ZDa Gb1 qi0+ ZRa mva Mb2 Gb2 Kma ZVa nna pma Gb3 nfa Mb3 zr2 Vfa Gc0 ZDb sptr+ S0+ s2a Gc1 foa ZMb fua mvb Mc1 Gc2 ZRb Mc2 D11 Kmb ZVb nnb pmb nfb Mc3 D10 Vfb K0d K0c MN11 ZMc zr3 s2b fob MX11 Gc3 fub Md0 nh1 D12 ZDc yzo0+ Md1 ZRc MX10 D13 MN10 mvc MX12 Kmc ZVc MN12 Gd0 pmc MX13 W01 MN13 Gd1 YX1 nnc YN1 nfc fb F1 Gd2 Vfc Md2 K0a- sendF z1 s2c Gd3 W1 foc fuc y1 Md3 D00 ZDd r8 yb ZMd mvd sendY nnd MX00 cnt ZRd D01 MN00 W00 Kmd ZVd pmd nfd MX01 Vfd Y00 MN01 A s2d fod nh0 fud D03 D02 nb hf am MX02 c32 thT MN02 U1 MX03 MN03 YX0 snn YN0 lo sl dox+ sp2 soff0 z0 F0 W0 y0 soff1 pr1 yso1+ qi1 S1 yso0+ U0 wo0 ad0 dd0 Y01- doz yzo1 dos_ off1 Pa0 X0 Pb0 zr0- Pa1 wo1 rb0 dd1 ad1 pr0 P0 Pb1 X1 rb1
+""".split()
 
 bf, f32, i32, u16 = "bfloat16", "float32", "int32", "uint16"
 SCRATCH = {
     "X": ("sbuf", [128, XW], bf), "P": ("sbuf", [128, XW], f32), "WA": ("sbuf", [128, 384], bf), "WB": ("sbuf", [128, 384], bf),
-    "ra": ("sbuf", [128, 256], f32), "rb": ("sbuf", [128, 256], f32), "VT": ("sbuf", [128, VW], i32),
+    "rb": ("sbuf", [128, 256], f32), "VT": ("sbuf", [128, VW], i32),
     "vwi": ("sbuf", [128, 1024], i32), "sci": ("sbuf", [128, 256], i32), "zin": ("sbuf", [128, 256], bf),
     "wti": ("sbuf", [128, 4], i32), "thi": ("sbuf", [128, 4], i32), "wai": ("sbuf", [128, 256], i32), "wab": ("sbuf", [128, 256], bf),
     "zs": ("sbuf", [128, 7 * 256], bf), "zr0": ("sbuf", [128, 4096], bf), "zr1": ("sbuf", [128, 4096], bf),
     "M0": ("sbuf", [128, 8, 256], bf), "M1": ("sbuf", [128, 8, 256], bf), "G0": ("sbuf", [128, 8, 256], bf), "G1": ("sbuf", [128, 8, 256], bf),
     "D0": ("sbuf", [128, 2048], bf), "D1": ("sbuf", [128, 2048], bf),
     "MX": ("sbuf", [128, 4096], bf), "MN": ("sbuf", [128, 4096], bf),
-    "mk0": ("sbuf", [128, 512], bf), "mkB": ("sbuf", [128, 512], bf), "If": ("sbuf", [128, 128], f32),
+    "mk0": ("sbuf", [128, 1024], bf), "mkB": ("sbuf", [128, 1024], bf), "mkN": ("sbuf", [128, 128], bf),
+    "mkC": ("sbuf", [128, 256], bf), "CV": ("sbuf", [128, 256], bf),
+    "mvb": ("sbuf", [128, 1024], bf), "nn": ("sbuf", [128, 512], bf), "s2": ("sbuf", [128, 512], f32),
     "soff": ("sbuf", [128, 256], u16), "fu": ("sbuf", [128, 256], u16), "lst": ("sbuf", [128, 64], u16),
-    "fs": ("sbuf", [128, 6 * 128], i32), "fe": ("sbuf", [128, 128], i32), "fl4": ("sbuf", [128, 128], i32),
+    "fs": ("sbuf", [128, 6 * 136], i32), "fe": ("sbuf", [128, 128], i32), "fl5": ("sbuf", [128, 8], i32),
     "ysn": ("sbuf", [128, 6 * 136], bf), "W": ("sbuf", [128, 6 * 264], bf),
-    "mv": ("sbuf", [128, 512], bf), "pm": ("sbuf", [128, 256], f32), "fg": ("sbuf", [128, 256], bf), "nf": ("sbuf", [128, 256], bf),
-    "fd": ("sbuf", [128, 256], f32), "s2": ("sbuf", [128, 256], f32),
-    "dz": ("sbuf", [128, 512], f32), "r0": ("sbuf", [128, 256], f32), "rr": ("sbuf", [128, 256], f32), "pr": ("sbuf", [128, 256], f32), "qi": ("sbuf", [128, 256], i32),
-    "dd": ("sbuf", [128, 256], bf), "ad": ("sbuf", [128, 256], bf), "t1": ("sbuf", [128, 512], bf),
-    "tf": ("sbuf", [128, 256], f32), "ti": ("sbuf", [128, 96], i32), "bo": ("sbuf", [128, 16], bf),
-    "col": ("sbuf", [128, 64], f32), "BI": ("sbuf", [128, 16], f32), "BS": ("sbuf", [128, 16], f32),
+    "pm": ("sbuf", [128, 256], f32), "pr": ("sbuf", [128, 256], f32), "qi": ("sbuf", [128, 256], i32),
+    "dd": ("sbuf", [128, 256], bf), "ad": ("sbuf", [128, 256], bf),
+    "tf": ("sbuf", [128, 64], f32), "tb": ("sbuf", [128, 176], bf), "ti": ("sbuf", [128, 16], i32),
+    "col": ("sbuf", [128, 64], f32), "BI": ("sbuf", [128, 16], f32), "BJ": ("sbuf", [128, 16], f32),
     "th0": ("sbuf", [128, 128], f32), "thT": ("sbuf", [128, 128], f32), "dkf": ("sbuf", [128, 128], f32), "Bf": ("sbuf", [128, 128], f32),
+    "hf": ("sbuf", [128, 256], f32),
     "CI": ("sbuf", [128, 256], bf), "KI": ("sbuf", [128, 128], bf), "GI": ("sbuf", [128, 128], bf), "HI": ("sbuf", [128, 128], bf),
-    "ZM": ("sbuf", [128, 144], bf), "ZR": ("sbuf", [128, 144], bf), "ZD": ("sbuf", [128, 144], bf), "ZW": ("sbuf", [128, 144], bf), "Z8": ("sbuf", [128, 144], bf),
-    "I1": ("sbuf", [128, 128], bf), "Ih": ("sbuf", [128, 128], bf), "In": ("sbuf", [128, 128], bf),
-    "BW": ("sbuf", [128, 128], bf), "BX": ("sbuf", [128, 128], bf), "Bc": ("sbuf", [128, 128], bf),
-    "one": ("sbuf", [128, 128], bf), "o4": ("sbuf", [128, 128], bf), "TB": ("sbuf", [128, 128], bf),
-    "cY": ("sbuf", [128, 256], bf), "cU": ("sbuf", [128, 256], bf), "nn": ("sbuf", [128, 256], bf),
+    "ZM": ("sbuf", [128, 144], bf), "ZR": ("sbuf", [128, 144], bf), "ZD": ("sbuf", [128, 144], bf), "ZV": ("sbuf", [128, 144], bf),
+    "ZW": ("sbuf", [128, 144], bf), "ZN": ("sbuf", [128, 144], bf), "Z8": ("sbuf", [128, 144], bf),
+    "I1": ("sbuf", [128, 128], bf), "Ih": ("sbuf", [128, 128], bf), "In": ("sbuf", [128, 128], bf), "Is": ("sbuf", [128, 128], bf),
+    "BW": ("sbuf", [128, 128], bf), "BN": ("sbuf", [128, 128], bf), "BX": ("sbuf", [128, 128], bf), "Bc": ("sbuf", [128, 128], bf),
+    "one": ("sbuf", [128, 512], bf), "TB": ("sbuf", [128, 128], bf), "cl": ("sbuf", [128, 16 * 128], bf),
     "yso": ("sbuf", [128, 256], f32), "yzo": ("sbuf", [128, 256], bf),
     "pK0": ("psum", [128, 512], f32), "pK1": ("psum", [128, 512], f32), "pD0": ("psum", [128, 512], f32), "pD1": ("psum", [128, 512], f32),
-    "pN": ("psum", [128, 512], f32), "pY": ("psum", [128, 512], f32), "pU": ("psum", [128, 512], f32), "pV": ("psum", [128, 512], f32),
+    "pW": ("psum", [128, 512], f32), "pY": ("psum", [128, 512], f32), "pU": ("psum", [128, 512], f32), "pP": ("psum", [128, 512], f32),
 }
-DMAS = ["reg", "rega", "vw", "scan", "z0", "wt", "th", "warm", "oz", "os_", "ox"]
+BANKS = ("pK0", "pK1", "pD0", "pD1", "pW", "pY", "pU", "pP")
+DMAS = ["x0", "x1", "x2", "x3", "vw0", "vw1", "scan", "z0", "wt", "th", "warm", "oz", "os_", "ox"]
 SEMAPHORES = (["cv", "cs", "cp", "cg", "sent"] + ["d" + n for n in DMAS]
               + ["aF%d" % t for t in range(TS)] + ["aY%d" % t for t in range(TS)])
-CYC, PCYC, GATH, SCAT, LAT = 0.95, 0.48, 1.56, 3.8, 160
+CYC, PCYC, GATH, SCAT, LAT, HOLD, FAR = 0.95, 0.48, 1.56, 3.8, 130, 1200, [4500, 7000]
 
 
 def route(T, topo, r, t):
@@ -68,7 +68,7 @@ def route(T, topo, r, t):
 def landing(T, kind, t):
     if kind == "Y":
         return T.W[:, 264 * t + 128:264 * t + 264]
-    return T.VT[:, VLOG + 256 * t + 128:VLOG + 256 * t + 256] if t < 4 else T.fl4[:, :]
+    return T.VT[:, VL[t] + 128:VL[t] + 264] if t < TS - 1 else T.fl5[:, :]
 
 
 def write(g, T, topo, src, dst, in_ap, kind, t):
@@ -84,7 +84,7 @@ def helper_program(g, core, T, topo):
             dst, h = route(T, topo, r, t)
             if h != core:
                 continue
-            for kind in ("F", "Y") if t < TS - 1 else ("Y",):
+            for kind in ("F", "Y"):
                 g.wait_ge(T.sem["a%s%d" % (kind, t)], len(topo.engines(T.cores[r], core)))
                 n += write(g, T, topo, core, dst, landing(T, kind, t), kind, t)
     if n:
@@ -95,21 +95,22 @@ def plan(g, core, T, topo, rank):
     V, S, PE = g.vector, g.scalar, g.tensor
     ops = []
     sent = [0]
+    now = [-1]
 
-    def op(e, fn, r, w, cost, sem=None, n=1, hold=None):
-        ops.append((e, fn, list(r), list(w), float(cost), sem, n, float(cost if hold is None else hold)))
+    def op(e, fn, r, w, cost, sem=None, n=1, hold=None, nm=None):
+        ops.append((e, fn, list(r), list(w), float(cost), sem, n, float(cost if hold is None else hold), now[0], nm or (w[0] if w else sem)))
 
-    def ts(o, i, s1, s2, a, b, r, w, n):
+    def ts(o, i, s1, s2, a, b, r, w, n, nm=None):
         if b is None:
-            op("v", lambda: [V.tensor_scalar(o, i, s1, None, a)], r, w, max(64, n) * CYC)
+            op("v", lambda: [V.tensor_scalar(o, i, s1, None, a)], r, w, max(64, n) * CYC, nm=nm)
         else:
-            op("v", lambda: [V.tensor_scalar(o, i, s1, s2, a, b)], r, w, max(64, n) * CYC)
+            op("v", lambda: [V.tensor_scalar(o, i, s1, s2, a, b)], r, w, max(64, n) * CYC, nm=nm)
 
-    def tt(o, x, y, a, r, w, n):
-        op("v", lambda: [V.tensor_tensor(o, x, y, a)], r, w, max(64, n) * CYC)
+    def tt(o, x, y, a, r, w, n, nm=None):
+        op("v", lambda: [V.tensor_tensor(o, x, y, a)], r, w, max(64, n) * CYC, nm=nm)
 
-    def cp(o, i, r, w, n):
-        op("v", lambda: [V.tensor_copy(o, i)], r, w, max(64, n) * CYC)
+    def cp(o, i, r, w, n, nm=None):
+        op("v", lambda: [V.tensor_copy(o, i)], r, w, max(64, n) * CYC, nm=nm)
 
     def ms(o, c, w, n):
         op("v", lambda: [V.memset(o, c)], [], w, max(64, n) * CYC)
@@ -117,14 +118,11 @@ def plan(g, core, T, topo, rank):
     def scan(o, d0, d1, a, b, r, w, n):
         op("v", lambda: [V.tensor_tensor_scan(o, d0, d1, 0.0, a, b)], r, w, max(64, n) * CYC)
 
-    def act(o, i, f, r, w, n, bias=0.0, scale=1.0):
-        op("s", lambda: [S.activation(o, i, f, bias=bias, scale=scale)], r, w, max(64, n) * CYC)
+    def act(o, i, f, r, w, n, bias=0.0, scale=1.0, nm=None):
+        op("s", lambda: [S.activation(o, i, f, bias=bias, scale=scale)], r, w, max(64, n) * CYC, nm=nm)
 
-    def mm(lst, r, w, cols):
-        k = 2 if len(lst) == 16 else 1
-        for j in range(k):
-            part = lst[j * len(lst) // k:(j + 1) * len(lst) // k]
-            op("p", lambda part=part: [PE.matmul(*a) for a in part], r, w, cols * PCYC / k + 30, n=len(part))
+    def mm(lst, r, w, cols, nm=None):
+        op("p", lambda: [PE.matmul(*a) for a in lst], r, w, cols * PCYC, n=len(lst), nm=nm)
 
     def iota(o, pat, base, cm, w, n, small=True):
         if small:
@@ -132,147 +130,191 @@ def plan(g, core, T, topo, rank):
         else:
             op("g", lambda: [g.iota(o, pat, base, cm)], [], w, 160 + 2 * n * CYC)
 
+    def spread(o, i, n, r, w, nm=None):
+        op("g", lambda: [g.affine_select(o, i, [[0, n]], AL.is_ge, 0.0, 0, 0)], r, w, 200 + 2 * n * CYC, nm=nm)
+
     def dma(q, name, o, i, r, w, cost):
         e = g.sync if q == "y" else S
         op(q, lambda: [e.dma_start(o, i)], r, w, cost, sem="d" + name, n=16, hold=60)
 
     def c(j):
         return T.col[:, j:j + 1]
-    PF, LF, GF, C15, C16G, C8G, C8G1, C4, WF, THF, WR, MLO, WD, TA, TBc, TC, B37, L16, P15, A4, AQ = range(21)
-    C32 = 32
-    def tl(j, h=None):
-        return T.tf[:, 16 * j:16 * j + 16] if h is None else T.tf[:, 16 * j + 8 * h:16 * j + 8 * h + 8]
-    NP0, BASE, SNN, SPTR, LIM, T3, NH, EE, SP2, OFF, CE = 0, 3, 4, 5, 6, 7, 8, 9, 10, 11, 12
+    PF, LF, GF, C15, C16G, C4G, C4, WF, WN, THF, WR, MLO, WD, WV, TA, TBc, B37, L16, P15, CNT, AQ, NM1, SPC, NHF, LP, NA, L8 = range(27)
+    C32, AB = 32, 40
 
-    dma("y", "rega", T.X[:, 0:1024], T.reg[:, 0:1024], [], ["Xa"], 3300)
-    dma("y", "reg", T.X[:, 1024:2048], T.reg[:, 1024:2048], [], ["X"], 4300)
-    dma("s", "z0", T.zin[:], T.z0[:], [], ["zin"], 2200)
-    dma("s", "scan", T.sci[:], T.scan[:], [], ["sci"], 2400)
-    dma("s", "warm", T.wai[0:8, :], T.warm[:], [], ["wai"], 2400)
-    dma("s", "wt", T.wti[:, 0:1], T.wt[:], [], ["wti"], 2500)
+    def tl(j, h=None):
+        return T.tb[:, 16 * j:16 * j + 16] if h is None else T.tb[:, 16 * j + 8 * h:16 * j + 8 * h + 8]
+    NP0, BASE, SNN, SPTR, NH, SP2, SG, NB, HF = 0, 3, 4, 5, 6, 7, 8, 9, 10
+
+    consts = {"q": -0.25, "m": M1, "-3": -3.5, "3": 3.5, "8m": 8 * M1, "-8m": -8 * M1, "um": 2048 * M1, "-um": -2048 * M1,
+              "32": 32.0, "15": 15.5, "32m": 32 * M1, "-32m": -32 * M1, "u0": -0.5, "64m": None, "-64m": None}
+    names = sorted(consts)
+
+    def cm(o, name, n, start=False, stop=False):
+        j, k = names.index(name), 2 if name == "u0" else 1
+        return (o, T.cl[0:k, 128 * j:128 * j + 128], T.one[0:k, 0:n], start, stop)
+
+    dma("s", "warm", T.wai[0:8, :], T.warm[:], [], ["wai"], 2300)
+    dma("s", "scan", T.sci[:], T.scan[:], [], ["sci"], 2500)
+    dma("s", "z0", T.zin[:], T.z0[:], [], ["zin"], 2500)
     dma("s", "th", T.thi[:, 0:1], T.th[:], [], ["thi"], 2600)
-    dma("y", "vw", T.vwi[:], T.vw[:], ["Xa"], ["vwi"], 4300)
+    dma("s", "wt", T.wti[:, 0:1], T.wt[:], [], ["wti"], 2600)
+    for j in range(4):
+        dma("y", "x%d" % j, T.X[:, 512 * j:512 * j + 512], T.reg[:, 512 * j:512 * j + 512], [], ["X%d" % j], 3000 + 600 * j)
+    for j in range(2):
+        dma("y", "vw%d" % j, T.vwi[:, 512 * j:512 * j + 512], T.vw[:, 512 * j:512 * j + 512], ["X0"], ["vw%d" % j], 3200 + 1200 * j)
+    Xk = ["X0", "X1", "X2", "X3", "Xs"]
+    Xt = ["Xt%d" % j for j in range(5)]
     iota(T.ti[:, 0:1], [[0, 1]], 0, 1, ["ti0"], 1, small=False)
-    iota(T.CI[:], [[1, 256]], 0, 0, ["CI"], 256)
     iota(T.KI[:], [[0, 8], [1, 16]], 0, 0, ["KI"], 128)
+    iota(T.CI[:], [[1, 256]], 0, 0, ["CI"], 256)
     iota(T.HI[:], [[1, 32], [0, 4]], 0, 0, ["HI"], 128)
+    for s in range(3):
+        iota(tl(NP0 + s), [[16, 16]], RING[s], 0, ["np%d" % s], 16)
+    iota(T.BI[:, 0:8], [[256, 8]], V0, 0, ["BI"], 8)
     iota(T.GI[:], [[1, 8], [0, 16]], 0, 0, ["GI"], 128)
-    iota(tl(NP0), [[128, 2], [16, 8]], RING, 0, ["np0"], 16)
-    iota(tl(BASE), [[8, 2], [256, 8]], 0, 0, ["base"], 16)
-    ms(T.X[:, 2048:2064], 0.0, ["Xs"], 8)
-    ms(T.P[:, 2048:2064], 0.0, ["Ps"], 8)
-    iota(T.X[:, 2064:XW], [[0, XW - 2064]], 0, 0, ["Xt"], XW - 2064)
-    iota(T.P[:, 2064:XW], [[0, XW - 2064]], 0, 0, ["Pt"], XW - 2064)
-    ms(T.VT[:, 0:RING], 2048, ["VTd"], 16)
-    iota(T.VT[:, RING + 256:V0], [[0, 512]], 0, 0, ["S10", "S11", "S20", "S21"], 512, small=False)
-    ms(T.mk0[:], 1.0, ["mk0"], 256); ms(T.mk0[:, ::16], 0.0, ["mk0"], 32)
-    ms(T.mkB[:], 0.0, ["mkB"], 256); ms(T.mkB[:, ::16], 256.0, ["mkB"], 32)
-    ms(T.one[:], 1.0, ["one"], 64); ms(T.o4[:], 4096.0, ["o4"], 64)
-    ms(T.cY[0:1, :], -0.25, ["cY"], 128)
-    ms(T.cU[0:2, 0:128], 0.5, ["cU"], 64); ms(T.cU[0:1, 0:128], -1024.0, ["cU"], 64); ms(T.cU[0:2, 128:256], 16.0, ["cU"], 64)
-    ms(tl(LIM), 1.0, ["mv200", "mv201", "mv210", "mv211"], 16)
-    for j, v in enumerate((M1, -M1, M2, SPARE)):
-        ms(c(40 + j), v, ["m1"], 1)
-    ms(c(47), -0.484375, ["m1"], 1)
+    iota(tl(BASE, 0), [[256, 8]], 0, 0, ["base0"], 8)
+    iota(T.tf[:, 0:8], [[256, 8]], 8, 0, ["base1"], 8)
+    iota(T.col[:, AB:AB + 6], [[4096, 6]], 0, 0, ["ab"], 8)
+    iota(T.BJ[:, 0:2], [[128, 2]], VL[0] - 128, 0, ["BJ0"], 2)
+    iota(T.BJ[:, 2:10], [[VL[2] - VL[1], 4], [128, 2]], VL[1] - 128, 0, ["BJ"], 8)
+    iota(T.tf[:, 16:26], [[1, 5], [0, 2]], 1, 0, ["BS"], 10)
+    for s in range(4):
+        iota(T.VT[:, VL[s] + 264:VL[s] + 272], [[0, 8]], 0, 0, ["Vp%d" % s], 8, small=False)
+    iota(T.VT[:, 0:16], [[0, 16]], 2048, 0, ["VTd"], 16, small=False)
+    for j in range(5):
+        a, b = 2064 + 464 * j, min(XW, 2064 + 464 * j + 464)
+        iota(T.X[:, a:b], [[0, b - a]], 0, 0, [Xt[j]], b - a)
+    ms(T.one[:], 1.0, ["one"], 256)
+
+    def fill(o, v, w, n, p=128):
+        act(o, T.one[0:p, 0:n], AF.Copy, ["one"], w, n, scale=v)
+    fill(T.X[:, 2048:2064], 0.0, ["Xs"], 16)
+    fill(T.P[:, 2048:2064], 64.0, ["Ps"], 16)
+    nd = max(n for h in DCH for n, _ in DCH[h])
+    ms(T.mk0[:, 0:nd], 1.0, ["mk0"], nd // 2); fill(T.mk0[:, 0:nd:16], 0.0, ["mk0"], nd // 16)
+    ms(T.mkB[:, 0:nd], 0.0, ["mkB"], nd // 2); fill(T.mkB[:, 0:nd:16], 256.0, ["mkB"], nd // 16)
+    fill(T.mkN[:], 0.0, ["mkN"], 128); fill(T.mkN[:, ::16], -16.0, ["mkN"], 8)
+    ms(T.mvb[:, 1::2], 0.0, ["mvc"], 256)
+    for j, v in ((1, 2.0), (29, -1.0), (31, -2.0)):
+        fill(T.mvb[:, j::32], v, ["mvc", "lo0", "lo1"], 32)
+    for nm in names:
+        j = names.index(nm)
+        if nm == "u0":
+            fill(T.cl[0:2, 128 * j:128 * j + 128], -0.5, ["cl" + nm], 128, 2)
+            fill(T.cl[0:1, 128 * j:128 * j + 128], 1024.0, ["cl" + nm], 128, 1)
+        elif nm == "64m":
+            ts(T.cl[0:1, 128 * j:128 * j + 128], T.KI[0:1, :], 3.0, 64 * M1, AL.is_le, AL.mult, ["KI"], ["cl" + nm], 64)
+            k = names.index("-64m")
+            act(T.cl[0:1, 128 * k:128 * k + 128], T.cl[0:1, 128 * j:128 * j + 128], AF.Copy, ["cl64m"], ["cl-64m"], 128, scale=-1.0)
+        elif nm != "-64m":
+            fill(T.cl[0:1, 128 * j:128 * j + 128], consts[nm], ["cl" + nm], 128, 1)
+    act(T.hf[:, 0:128], T.one[:, 0:128], AF.Copy, ["one"], ["hf0"], 128, scale=-0.5)
+    act(T.hf[:, 128:256], T.one[:, 0:128], AF.Copy, ["one"], ["hf1"], 128, scale=0.5)
+    for j, v, k in ((NM1, -M1, "nm1"), (SPC, SPARE, "spc"), (NHF, -0.5, "nhf")):
+        act(c(j), T.one[:, 0:1], AF.Copy, ["one"], [k], 1, scale=v)
     cp(c(PF), T.ti[:, 0:1], ["ti0"], ["pf"], 1)
     ts(T.ti[:, 1:2], T.ti[:, 0:1], 15, None, AL.bitwise_and, None, ["ti0"], ["ti1"], 1)
     cp(c(LF), T.ti[:, 1:2], ["ti1"], ["lf"], 1)
     tt(c(C16G), c(PF), c(LF), AL.subtract, ["pf", "lf"], ["c16g"], 1)
     ts(c(C15), c(C16G), 15.0, None, AL.add, None, ["c16g"], ["c15"], 1)
     ts(c(C4), c(C16G), 4.0, None, AL.add, None, ["c16g"], ["c4"], 1)
-    ts(c(GF), c(C16G), 0.0625, None, AL.mult, None, ["c16g"], ["gf"], 1)
-    ts(c(C8G), c(C16G), 0.25, None, AL.mult, None, ["c16g"], ["c8g"], 1)
     ts(c(P15), c(PF), 16.0, 15.0, AL.mult, AL.add, ["pf"], ["p15"], 1)
-    ts(c(B37), c(LF), 1184.0, None, AL.mult, None, ["lf"], ["b37"], 1)
-    ts(c(L16), c(LF), 16.0, None, AL.mult, None, ["lf"], ["l16"], 1)
-    ts(c(WR), c(LF), 1.0, -2.0 ** -12, AL.is_le, AL.mult, ["lf"], ["wr"], 1)
-    cp(c(WF), T.wti[:, 0:1], ["wti"], ["wf"], 1)
-    cp(c(THF), T.thi[:, 0:1], ["thi"], ["thf"], 1)
+    ts(c(B37), c(LF), 1184.0, 32768.0, AL.mult, AL.add, ["lf"], ["b37"], 1)
+    for j, src, v, k in ((GF, C16G, 0.0625, "gf"), (C4G, C16G, 0.25, "c4g"), (C32, LF, 1184.0, "c320"), (L16, LF, 16.0, "l16"), (NA, LF, -2.0 ** -13, "na")):
+        act(c(j), c(src), AF.Copy, ["c16g", "lf"], [k], 1, scale=v)
+    ts(c(WF), T.wti[:, 0:1], 2048.0, None, AL.mult, None, ["wti"], ["wf"], 1)
+    act(c(WN), c(WF), AF.Copy, ["wf"], ["wn"], 1, scale=-1.0)
+    ts(c(THF), T.thi[:, 0:1], 2048.0, None, AL.mult, None, ["thi"], ["thf"], 1)
+    fill(c(AB + 6), 4096.0 * 64, ["ab6"], 1)
     ts(T.dkf[:], T.KI[:], c(LF), None, AL.is_equal, None, ["KI", "lf"], ["dkf"], 128)
+    ts(T.tf[:, 0:8], T.tf[:, 0:8], c(L16), None, AL.add, None, ["base1", "l16"], ["base1"], 8)
 
     def dk(k):
         return T.dkf[:, k:k + 1]
     tt(c(MLO), dk(1), dk(3), AL.add, ["dkf"], ["mlo"], 1)
-    tt(c(TA), dk(2), dk(3), AL.add, ["dkf"], ["ta"], 1)
-    tt(c(TBc), dk(4), dk(5), AL.add, ["dkf"], ["tb"], 1)
-    ts(c(TC), dk(6), 4080.0 * 4096.0, c(TBc), AL.mult, AL.add, ["dkf", "tb"], ["tc"], 1)
-    ts(c(WD), c(TA), 4096.0, c(TC), AL.mult, AL.add, ["ta", "tc"], ["wd"], 1)
-    ts(T.BI[:], T.CI[:, 0:16], -256.0, -float(V0), AL.mult, AL.add, ["CI"], ["BI"], 16)
-    ms(T.BI[:, 12:13], -float(V0), ["BI"], 1)
-    ts(T.BI[:], T.BI[:], dk(5), None, AL.mult, None, ["BI", "dkf"], ["BI"], 16)
-    ts(T.BS[:], T.CI[:, 0:16], -1.0, dk(6), AL.mult, AL.mult, ["CI", "dkf"], ["BS"], 16)
-    tt(T.BI[:, 8:13], T.BI[:, 8:13], T.BS[:, 1:6], AL.add, ["BI", "BS"], ["BI"], 16)
-    ts(T.col[:, 48:53], T.BI[:, 8:13], -1.0, None, AL.mult, None, ["BI"], ["BJ"], 16)
-    for nm, s2, r in (("ZM", 2.0 ** -11, []), ("ZR", c(WR), ["wr"]), ("ZD", c(WD), ["wd"]), ("ZW", c(WF), ["wf"])):
-        ts(T[nm][:], T.CI[:, 0:144], c(C15), s2, AL.is_equal, AL.mult, ["CI", "c15"] + r, [nm], 72)
+    tt(c(LP), dk(1), dk(0), AL.subtract, ["dkf"], ["lp"], 1)
+    act(c(WR), c(LP), AF.Copy, ["lp"], ["wr"], 1, scale=0.5)
+    ts(c(TA), dk(2), dk(3), 2048.0, AL.subtract, AL.mult, ["dkf"], ["ta"], 1)
+    act(c(WD), dk(6), AF.Identity, ["dkf", "ta"], ["wd"], 1, bias=c(TA), scale=2048.0 * 4096)
+    ts(c(WV), dk(4), dk(5), 0.25, AL.add, AL.mult, ["dkf"], ["wv"], 1)
+    ts(c(L8), c(LF), 3.0, 64.0, AL.is_le, AL.mult, ["lf"], ["l8"], 1)
+    ts(c(TBc), dk(6), 64.0, c(L8), AL.mult, AL.add, ["dkf", "l8"], ["tbc"], 1)
+    ts(T.BI[:, 0:8], T.BI[:, 0:8], dk(5), c(TBc), AL.mult, AL.add, ["BI", "dkf", "tbc"], ["BI"], 8)
+    act(T.BI[:, 8:16], T.BI[:, 0:8], AF.Copy, ["BI"], ["BIn"], 8, scale=-1.0)
+    act(T.BJ[:, 0:10], T.BJ[:, 0:10], AF.Identity, ["BJ", "BJ0", "dkf", "tbc"], ["BJ", "BJ0"], 10, bias=c(TBc), scale=dk(5))
+    act(T.tf[:, 16:26], T.tf[:, 16:26], AF.Identity, ["BS", "dkf"], ["BS"], 10, scale=dk(6))
+    tt(T.BJ[:, 0:10], T.BJ[:, 0:10], T.tf[:, 16:26], AL.add, ["BJ", "BS"], ["BJ"], 20)
+    ts(T.ZM[:], T.CI[:, 0:144], c(C15), 2.0 ** -11, AL.is_equal, AL.mult, ["CI", "c15"], ["ZM"], 72)
+    for nm, s2, r in (("ZR", WR, "wr"), ("ZD", WD, "wd"), ("ZV", WV, "wv"), ("ZW", WF, "wf"), ("ZN", WN, "wn")):
+        act(T[nm][:], T.ZM[:], AF.Identity, ["ZM", r], [nm], 144, scale=c(s2))
     ts(T.Z8[0:8, :], T.CI[0:8, 0:144], T.col[0:8, P15:P15 + 1], None, AL.is_equal, None, ["CI", "p15"], ["Z8"], 72)
-    for nm, s2 in (("I1", 1.0), ("Ih", 0.5), ("In", -1.0), ("If", 1.0)):
-        ts(T[nm][:], T.CI[:, 0:128], c(PF), s2, AL.is_equal, AL.mult, ["CI", "pf"], [nm], 64)
-    ts(T.BW[:], T.GI[:], c(GF), c(WF), AL.is_equal, AL.mult, ["GI", "gf", "wf"], ["BW"], 64)
-    ts(T.Bf[:], T.GI[:], c(GF), None, AL.is_equal, None, ["GI", "gf"], ["Bf"], 128)
-    ts(T.BX[:], T.HI[:], c(C8G), None, AL.is_equal, None, ["HI", "c8g"], ["BX"], 64)
-    ms(T.WA[:], 0.0, ["WA"], 192)
-    ts(c(TA + 32), c(LF), 1.0, None, AL.is_le, None, ["lf"], ["lp"], 1)
-    ts(c(TA + 33), c(LF), 1.0, -1.0, AL.is_le, AL.mult, ["lf"], ["ln"], 1)
-    for m0, j, s2 in ((0, 0, -1.0), (0, 1, 1.0), (0, 2, 1.0), (0, 3, -1.0), (128, 2, -2.0), (128, 3, 2.0), (256, 2, c(TA + 32)), (256, 3, c(TA + 33))):
-        ts(T.WA[:, m0 + j:m0 + 128:16], T.GI[:, 0::16], c(GF), s2, AL.is_equal, AL.mult, ["GI", "gf", "lp", "ln"], ["WA"], 8)
-    cp(T.WB[:], T.WA[:], ["WA"], ["WB"], 192)
-    ms(T.WB[:, 0::2], 0.0, ["WB"], 96)
+    ts(T.I1[:], T.CI[:, 0:128], c(PF), None, AL.is_equal, None, ["CI", "pf"], ["I1"], 64)
+    for nm, s2 in (("Ih", 0.5), ("In", -1.0), ("Is", 2.0 ** -13)):
+        act(T[nm][:], T.I1[:], AF.Copy, ["I1"], [nm], 128, scale=s2)
+    ts(T.Bf[:], T.GI[:], c(GF), 2.0 ** -11, AL.is_equal, AL.mult, ["GI", "gf"], ["Bf"], 128)
+    act(T.BW[:], T.Bf[:], AF.Identity, ["Bf", "wf"], ["BW"], 128, scale=c(WF))
+    act(T.BN[:], T.Bf[:], AF.Identity, ["Bf", "wn"], ["BN"], 128, scale=c(WN))
+    ts(T.BX[:, 0::2], T.HI[:, 0::2], c(C4G), None, AL.is_equal, None, ["HI", "c4g"], ["BX0"], 32)
+    ts(T.BX[:, 1::2], T.HI[:, 1::2], c(C4G), -1.0, AL.is_equal, AL.mult, ["HI", "c4g"], ["BX1"], 32)
     ts(T.Bc[:], T.CI[:, 0:128], c(C4), dk(0), AL.is_equal, AL.mult, ["CI", "c4", "dkf"], ["Bc"], 64)
-    ts(T.TB[:], T.KI[:], -2.0 ** -16, 15 * 2.0 ** -16, AL.mult, AL.add, ["KI"], ["TB"], 64)
-    ts(tl(NP0), tl(NP0), c(LF), None, AL.add, None, ["np0", "lf"], ["np0"], 16)
-    ts(tl(NP0 + 1), tl(NP0), 256.0, None, AL.add, None, ["np0"], ["np1"], 16)
-    ts(tl(NP0 + 2), tl(NP0), 512.0, None, AL.add, None, ["np0"], ["np2"], 16)
-    ts(tl(BASE), tl(BASE), c(L16), None, AL.add, None, ["base", "l16"], ["base"], 16)
-    cp(tl(SPTR), tl(NP0), ["np0"], ["sptr"], 16)
-    cp(c(C32), c(B37), ["b37"], ["c320"], 1)
-    ts(T.thT[:], T.dkf[:], c(THF), None, AL.mult, None, ["dkf", "thf"], ["thT"], 128)
+    fill(T.WA[:], 0.0, ["WA"], 384)
+    WAk = []
+    for m0, j, s2 in ((0, 0, 1.0), (0, 1, 1.0), (0, 2, -1.0), (0, 3, -1.0), (128, 2, 2.0), (128, 3, 2.0), (256, 2, -1.0), (256, 3, -1.0)):
+        WAk.append("WA%d" % len(WAk))
+        act(T.WA[:, m0 + j:m0 + 128:16], T.Bf[:, 0::16], AF.Copy, ["Bf", "WA"], WAk[-1:], 8, scale=2048 * s2)
+    fill(T.WB[:, 0::2], 0.0, ["WB0"], 192)
+    act(T.WB[:, 1::2], T.WA[:, 1::2], AF.Copy, WAk, ["WB1"], 192, scale=-1.0)
+    act(T.TB[:], T.KI[:], AF.Copy, ["KI"], ["TB"], 128, scale=-2.0 ** -16)
+    nv = 32 * max(u[3] for u in UNITS)
+    fill(T.CV[:, 1:nv:2], -1.0, ["CV"], nv // 2)
+    fill(T.CV[:, 31:nv:32], 0.0, ["CV"], nv // 32)
+    act(T.CV[:, 0:nv:2], T.one[:, 0:nv // 2], AF.Identity, ["one", "na"], ["CV"], nv // 2, scale=c(NA))
+    fill(T.mkC[:, 0:nv], 1.0, ["mkC"], nv); fill(T.mkC[:, 0:nv:32], 0.0, ["mkC"], nv // 32)
+    act(tl(SPTR), tl(NP0), AF.Copy, ["np0"], ["sptr"], 16)
+    act(T.thT[:], T.dkf[:], AF.Identity, ["dkf", "thf"], ["thT"], 128, scale=c(THF))
     mm([(T.pU[:, 0:128], T.Bf[:], T.thT[:], True, True)], ["Bf", "thT"], ["pU"], 512)
-    ts(T.th0[:], T.pU[:, 0:128], 4096.0, 4095.0, AL.mult, AL.add, ["pU"], ["th0"], 128)
+    act(T.th0[:], T.pU[:, 0:128], AF.Identity, ["pU", "ab6"], ["th0"], 128, bias=c(AB + 6))
     for h in (0, 1):
-        cp(T.VT[:, RING + 128 * h:RING + 128 * h + 128], T.sci[:, h::2], ["sci"], ["S0%d" % h], 128)
-        cp(T.zs[:, 128 * h:128 * h + 128], T.zin[:, h::2], ["zin"], ["z0%d" % h], 64)
+        cp(T.VT[:, RING[0] + 128 * h:RING[0] + 128 * h + 128], T.sci[:, h::2], ["sci"], ["S0%d" % h], 128)
+        act(T.zs[:, 128 * h:128 * h + 128], T.zin[:, h::2], AF.Copy, ["zin"], ["z0%d" % h], 128)
     cp(T.wab[0:8, :], T.wai[0:8, :], ["wai"], ["wab"], 256)
-    mm([(T.pN[:, 8 * h:8 * h + 8], T.Z8[0:8, 15 - a:143 - a], T.wab[0:8, 2 * a + h::32], a == 0, a == 15)
-        for h in (0, 1) for a in range(16)], ["Z8", "wab"], ["pN"], 32 * 64)
-    tt(tl(SNN), T.pN[:, 0:16], tl(NP0), AL.mult, ["pN", "np0"], ["snn"], 16)
-    ring = ["VTd"] + ["S%d%d" % (s, h) for s in range(3) for h in (0, 1)]
+    mm([(T.pW[:, 8 * h:8 * h + 8], T.Z8[0:8, 15 - a:143 - a], T.wab[0:8, 2 * a + h::32], a == 0, a == 15)
+        for h in (0, 1) for a in range(16)], ["Z8", "wab"], ["pW"], 32 * 64)
+    tt(tl(SNN), T.pW[:, 0:16], tl(NP0), AL.mult, ["pW", "np0"], ["snn"], 16)
+    parts = [(0, ["VTd"]), (V0, ["V0%d" % j for j in range(8)])] + [(RING[s], ["S%d0" % s, "S%d1" % s]) for s in range(3)]
+    parts += [(VL[s], ["VL%d" % s, "lF%d" % s]) for s in range(5)] + [(VL[s] + 264, ["Vp%d" % s]) for s in range(4)]
 
-    def next_lists():
-        cp(T.lst[:, 32:48], tl(SNN), ["snn"], ["sl"], 16)
+    def upto(end):
+        return T.VT[:, 0:end], [k for a, ks in parts if a < end for k in ks]
+
+    def next_lists(t):
+        win, keys = upto(RING[min(t, 2)] + 256)
+        ts(T.lst[:, 32:48], tl(SNN), c(LF), None, AL.add, None, ["snn", "lf"], ["sl"], 16)
         for h in (1, 0):
-            cp(T.soff[:, 128 * h:128 * h + 128], T.VT[:, 0:V0].indirect(T.lst[:, 32 + 8 * h:40 + 8 * h]), ring + ["sl"], ["soff%d" % h], 50 + 128 * GATH)
-    next_lists()
+            cp(T.soff[:, 128 * h:128 * h + 128], win.indirect(T.lst[:, 32 + 8 * h:40 + 8 * h]), keys + ["sl"], ["soff%d" % h], 50 + 128 * GATH)
+    next_lists(0)
     for k in range(16):
-        if k % 4 == 0:
-            op("g", lambda k=k: [g.affine_select(T.zr0[:, k::16], T.zs[:, 0:256], [[0, 256]], AL.is_ge, 0.0, 0, 0)],
-               ["z00", "z01"], ["zr0%d" % k], 210 + 512 * CYC)
-        elif k % 4 == 1 or k > 12:
-            cp(T.zr0[:, k::16], T.zs[:, 0:256], ["z00", "z01"], ["zr0%d" % k], 128)
-        else:
-            act(T.zr0[:, k::16], T.zs[:, 0:256], AF.Copy, ["z00", "z01"], ["zr0%d" % k], 256)
+        cp(T.zr0[:, 2048 + k::16], T.zin[:, 1::2], ["zin"], ["zr01%d" % k], 64)
+        spread(T.zr0[:, k:2048:16], T.zin[:, 0::2], 128, ["zin"], ["zr00%d" % k])
     for j in range(8):
-        pb = ("pK0", "pD0", "pV", "pY")[j % 4]
+        pb = ("pK1", "pK0", "pY", "pP")[j % 4]
         sl = slice(256 * j, 256 * j + 256)
-        tv = T.t1[:, 256 * (j % 2):256 * (j % 2) + 256]
-        mm([(T[pb][:, 0:256], T.BX[:], T.X[:, sl], True, False), (T[pb][:, 0:256], T.Bc[:], T.CI[:], False, True)],
-           ["BX", "Bc", "CI", "X" if j > 3 else "Xa"], [pb], 512)
-        act(tv, T[pb][:, 0:256], AF.Identity, [pb, "mlo", "BI"], ["t1%d" % (j % 2)], 256, bias=T.BI[:, j:j + 1], scale=c(MLO))
-        if j in PS:
-            pc = ("pU", "pD1")[j % 2]
-            mm([(T[pc][:, 256:512], T.BX[:], T.X[:, sl], True, False), (T[pc][:, 256:512], T.Bc[:], T.CI[:], False, False),
-                (T[pc][:, 256:512], T.In[:], tv, False, True)], ["BX", "Bc", "CI", "In", "X" if j > 3 else "Xa", "t1%d" % (j % 2)], [pc], 768)
-            act(T.P[:, sl], T[pc][:, 256:512], AF.Copy, [pc], ["P%d" % j], 256)
-        else:
-            tt(T.P[:, sl], T[pb][:, 0:256], tv, AL.subtract, [pb, "t1%d" % (j % 2)], ["P%d" % j], 256)
+        tv = T.MX[:, sl]
+        xk = ["BX0", "BX1", "Bc", "CI", "X%d" % (j // 2)]
+        mm([(T[pb][:, 0:256], T.Bc[:], T.CI[:], True, False), (T[pb][:, 0:256], T.BX[:], T.X[:, sl], False, True)], xk, [pb], 512)
+        act(tv, T[pb][:, 0:256], AF.Identity, [pb, "mlo", "BIn"], ["t1%d" % j], 256, bias=T.BI[:, 8 + j:9 + j], scale=c(MLO))
+        tt(T.P[:, sl], T[pb][:, 0:256], tv, AL.subtract, [pb, "t1%d" % j], ["P%d" % j], 256)
     Pk = ["Ps"] + ["P%d" % j for j in range(8)]
-    ts(T.VT[:, V0:V0 + 1024], T.vwi[:], 2047, None, AL.bitwise_and, None, ["vwi"], ["V0a"], 1024)
-    ts(T.VT[:, V0 + 1024:V0 + 2048], T.vwi[:], 11, None, AL.logical_shift_right, None, ["vwi"], ["V0b"], 1024)
+    for j in range(8):
+        o, i = T.VT[:, V0 + 256 * j:V0 + 256 * j + 256], T.vwi[:, 256 * (j % 4):256 * (j % 4) + 256]
+        ts(o, i, 11 if j > 3 else 2047, None, AL.logical_shift_right if j > 3 else AL.bitwise_and, None, ["vw%d" % (j // 2 % 2)], ["V0%d" % j], 256)
 
     for t in range(TS):
+        now[0] = t
         last = t == TS - 1
-        zr = T.zr0 if t < 2 or t % 2 else T.zr1
-        zrk = ["zr%d%d" % (0 if t < 2 or t % 2 else 1, k) for k in range(16)]
+        zb = 0 if t < 2 or t % 2 else 1
+        zr = T["zr%d" % zb]
         thk, thb = ("th0", T.th0) if t == 0 else ("thT", T.thT)
         dst, hop = route(T, topo, rank, t)
         srcrank = (rank - 1 - t % 3) % len(T.cores)
@@ -284,184 +326,181 @@ def plan(g, core, T, topo, rank):
             def fn():
                 sent[0] += write(g, T, topo, core, to, ap, kind, t)
                 return []
-            op("g", fn, r, ["m%s%d" % (kind, t)], far, n=0, hold=1500)
-            op("x", None, ["m%s%d" % (kind, t)], ["l%s%d" % (kind, t)], 0, sem="a%s%d" % (kind, t), n=narr)
+            op("g", fn, r, ["m%s%d" % (kind, t)], far, n=0, hold=HOLD, nm="send" + kind)
+            op("x", None, ["m%s%d" % (kind, t)], ["l%s%d" % (kind, t)], 0, sem="a%s%d" % (kind, t), n=narr, nm="send" + kind)
 
         if 1 <= t <= 4:
-            zn = (T.zr1, 1) if t % 2 else (T.zr0, 0)
             for k in range(16):
-                op("g", lambda k=k, zn=zn, t=t: [g.affine_select(zn[0][:, k::16], T.zs[:, 256 * t:256 * t + 256], [[0, 256]], AL.is_ge, 0.0, 0, 0)],
-                   ["z%d0" % t, "z%d1" % t], ["zr%d%d" % (zn[1], k)], 210 + 512 * CYC)
-        vkeys = ring + ["V0a", "V0b"] + ["VL%d" % s for s in range(min(t, 4))] + ["lF%d" % s for s in range(min(t, 4))]
-        for h, qq, bank in UNITS:
+                spread(T["zr%d" % (t % 2)][:, k::16], T.zs[:, 256 * t:256 * t + 256], 256,
+                       ["z%d0" % t, "z%d1" % t], ["zr%d%d%d" % (t % 2, h, k) for h in (0, 1)], nm="zr%d" % (k // 4))
+        vwin, vkeys = upto(VL[t - 1] + 264 if t else RING[1])
+        unit = {}
+        for U, h, b0, nb, bank, step in UNITS:
             M, G = T["M%d" % h], T["G%d" % h]
             pK, pD, kK, kD = T["pK%d" % bank], T["pD%d" % bank], "pK%d" % bank, "pD%d" % bank
-            n, c0 = 64 * len(qq), 128 * h + 64 * qq[0]
-            hs = slice(c0, c0 + n)
-            mvn, mvo = 256 * (t % 2) + c0, 256 * (1 - t % 2) + c0
-
-            def kk(name, h=h, qq=qq):
-                return ["%s%d%d" % (name, h, q) for q in qq]
+            n = 16 * nb
+            B0 = 8 * h + b0
+            bs = slice(B0, B0 + nb)
+            hs = slice(16 * B0, 16 * B0 + n)
+            mvn, mvo = 512 * (t % 2) + 32 * B0, 512 * (1 - t % 2) + 32 * B0
+            for b in range(b0, b0 + nb):
+                unit[(h, b)] = U
             first = [(pK[:, 0:n], T.I1[:], T.TB[:, 0:n], True, False)]
             if t:
-                first.append((pK[:, 0:n], T.I1[:], T.mv[:, mvo:mvo + n], False, False))
-            mm(first, ["I1", "TB"] + kk("mv%d" % (1 - t % 2)), [kK], 2 * n)
-            for q in range(4 * qq[0], 4 * qq[-1] + 4):
-                off = T.soff[:, 128 * h + 16 * q:128 * h + 16 * q + 16]
+                first.append((pK[:, 0:n], T.I1[:], T.mvb[:, mvo:mvo + 2 * n:2], False, False))
+            mm(first, ["I1", "TB", "mv%d%s" % (1 - t % 2, U)], [kK], 2 * max(64, n), "K0" + U)
+            Gk, Mk = [], []
+            for q in range(b0, b0 + nb, step):
+                off = T.soff[:, 128 * h + 16 * q:128 * h + 16 * (q + step)]
                 e0 = 2048 * h + 256 * q
-                act(G[:, q, :], T.P[:, 0:2064].indirect(off), AF.Identity, Pk + ["soff%d" % h, "BS"], ["G%d%d" % (h, q)],
-                    65 + 256 * GATH, bias=T.BS[:, t:t + 1])
-                tt(M[:, q, :], T.X[:, 0:2064].indirect(off), zr[:, e0:e0 + 256], AL.max,
-                   ["X", "Xa", "Xs", "soff%d" % h] + zrk, ["M%d%d" % (h, q)], 50 + 256 * GATH)
-            for q in qq:
-                qs = range(4 * q, 4 * q + 4)
-                o = slice(64 * (q - qq[0]), 64 * (q - qq[0]) + 64)
-                mm([(pD[:, o], T.ZD[:, 15 - a:143 - a], G[:, 4 * q:4 * q + 4, 16 * a:16 * a + 16], a == 0, a == 15) for a in range(16)],
-                   ["ZD"] + ["G%d%d" % (h, x) for x in qs], [kD], 1024)
-                mm([(pK[:, o], T.ZM[:, 15 - a:143 - a], M[:, 4 * q:4 * q + 4, 16 * a:16 * a + 16], False, False) for a in range(16)],
-                   ["ZM"] + ["M%d%d" % (h, x) for x in qs], [kK], 1024)
-                mm([(pK[:, o], T.ZR[:, 15 - a:143 - a], G[:, 4 * q:4 * q + 4, 16 * a:16 * a + 16], False, False) for a in range(16)],
-                   ["ZR"] + ["G%d%d" % (h, x) for x in qs], [kK], 1024)
-            mvk = kk("mv%d" % (t % 2))
-            mv = T.mv[:, mvn:mvn + n]
-            b0, b1 = c0 // 16, (c0 + n) // 16
+                Gk.append("G%s%d" % (U, len(Gk)))
+                Mk.append("M%s%d" % (U, len(Mk)))
+                act(G[:, q, :], T.P[:, 0:2064].indirect(off), AF.Copy, Pk + ["soff%d" % h], Gk[-1:], 65 + 256 * step * GATH)
+                tt(M[:, q, :], T.X[:, 0:2064].indirect(off), zr[:, e0:e0 + 256 * step], AL.max,
+                   Xk + (Pk if t == 0 else []) + ["soff%d" % h] + ["zr%d%d%d" % (zb, h, k) for k in range(16)], Mk[-1:], 50 + 256 * step * GATH)
 
-            def tq(j, b0=b0, b1=b1):
-                return T.tf[:, 16 * j + b0:16 * j + b1]
-            tt(mv, pD[:, 0:n], thb[:, 0:n], AL.is_gt, [kD, thk], mvk, n)
-            mm([(pK[:, 0:n], T.I1[:], mv, False, True)], ["I1"] + mvk, [kK], n)
-            nB = T.nn[:, c0 + 15:c0 + n:16]
-            scan(T.nn[:, hs], T.mk0[:, 0:n], mv, AL.mult, AL.add, ["mk0"] + mvk, kk("nn"), n // 2)
-            lo, ln = (LIM, 14) if t % 2 == 0 else (14, LIM)
-            act(tq(ln), nB, AF.Relu, kk("nn"), kk("mv%d" % (3 - t % 2)), 8, bias=1.0, scale=-1.0)
-            scan(T.pm[:, hs], T.mk0[:, 0:n], pK[:, 0:n], AL.mult, AL.max, ["mk0", kK], kk("pm"), n)
-            tt(T.fg[:, hs], pK[:, 0:n], T.pm[:, hs], AL.is_equal, [kK] + kk("pm"), kk("fg"), n)
-            tt(T.fd[:, hs], pD[:, 0:n], T.fg[:, hs], AL.mult, [kD] + kk("fg"), kk("fd"), n)
-            if NFS[h]:
-                act(T.nf[:, hs], T.fg[:, hs], AF.Identity, kk("fg"), kk("nf"), n, bias=1.0, scale=-1.0)
-            else:
-                ts(T.nf[:, hs], T.fg[:, hs], -1.0, 1.0, AL.mult, AL.add, kk("fg"), kk("nf"), 64)
-            tt(T.bo[:, b0:b1], nB, tq(lo), AL.is_gt, kk("mv%d" % (2 + t % 2)) + kk("nn"), kk("bo"), 8)
-            tt(tq(EE), tq(SNN), tq(ln), AL.mult, kk("mv%d" % (3 - t % 2)) + ["snn"], kk("ee"), 8)
-            scan(T.s2[:, hs], T.nf[:, hs], T.fd[:, hs], AL.mult, AL.add, kk("nf") + kk("fd"), kk("s2"), n)
-            ia, ib = T.ti[:, 16 + b0:16 + b1], T.ti[:, 32 + b0:32 + b1]
-            tt(ia, T.s2[:, c0 + 15:c0 + n:16], T.bo[:, b0:b1], AL.mult, kk("s2") + kk("bo"), kk("ia"), 16)
-            ts(ib, ia, 4095, None, AL.bitwise_and, None, kk("ia"), kk("ib"), 8)
-            tt(tq(T3), ib, tq(EE), AL.max, kk("ib") + kk("ee"), kk("t3"), 16)
-            fo = T.lst[:, b0:b1]
-            cp(fo, tq(T3), kk("t3"), kk("fo"), 8)
-            cp(T.fu[:, hs], T.VT[:, 0:VLOG + 256 * min(t, 4)].indirect(fo), vkeys + kk("fo"), kk("fu"), 50 + n * GATH)
+            def lanes(o, Z, src, first, h=h, b0=b0, nb=nb):
+                return [(o, Z[:, 15 - a:143 - a], src[:, b0:b0 + nb, 16 * a:16 * a + 16], first and a == 0, first and a == 15) for a in range(16)]
+            pc = 16 * max(64, n)
+            mm(lanes(pK[:, 0:n], T.ZM, M, False), ["ZM"] + Mk, [kK], pc, "ZM" + U)
+            mm(lanes(pD[:, 0:n], T.ZD, G, True), ["ZD"] + Gk, [kD], pc, "ZD" + U)
+            mm(lanes(pK[:, 0:n], T.ZR, G, False), ["ZR"] + Gk, [kK], pc, "ZR" + U)
+            n0, n1 = 32 * B0, 32 * B0 + 2 * n
+            mv, mvk = T.mvb[:, mvn:mvn + 2 * n:2], "mv%d%s" % (t % 2, U)
+            tt(mv, pD[:, 0:n], thb[:, 0:n], AL.is_gt, [kD, thk], [mvk], n, "mv" + U)
+            mm([(pK[:, 0:n], T.I1[:], mv, False, True)], ["I1", mvk], [kK], max(64, n), "Km" + U)
+            scan(T.nn[:, n0:n1], T.mkC[:, 0:2 * n], T.mvb[:, mvn:mvn + 2 * n], AL.mult, AL.add,
+                 ["mkC", "mvc", "lo%d" % (t % 2), mvk], ["nn" + U, "nf" + U], n)
+            pV, pR, pE = pD[:, 256:256 + 2 * n], pD[:, 256:256 + 2 * n:2], pD[:, 287:256 + 2 * n:32]
+            mm([(pV, T.I1[:], T.CV[:, 0:2 * n], True, False), (pE, T.Is[:], T.tb[:, 16 * SNN + B0:16 * SNN + B0 + nb], False, False),
+                (pE, T.I1[:], T.mvb[:, mvn + 29:mvn + 2 * n:32], False, False)] + lanes(pR, T.ZV, G, False),
+               ["I1", "Is", "CV", "ZV", "snn", "lo%d" % (t % 2)] + Gk, [kD], pc + 128 + 2 * n, "ZV" + U)
+            scan(T.pm[:, hs], T.mkN[:, 0:n], pK[:, 0:n], AL.add, AL.max, ["mkN", kK], ["pm" + U], n)
+            tt(T.nn[:, n0:n1:2], pK[:, 0:n], T.pm[:, hs], AL.not_equal, [kK, "pm" + U], ["nf" + U], n)
+            mm([(pE, T.In[:], T.nn[:, n0 + 31:n1:32], False, False), (pR, T.In[:], T.nn[:, n0:n1:2], False, True)],
+               ["In", "nn" + U, "nf" + U], [kD], 64 + max(64, n), "Vf" + U)
+            scan(T.s2[:, n0:n1], T.nn[:, n0:n1], pV, AL.min, AL.max, ["nn" + U, "nf" + U, kD], ["s2" + U], 2 * n)
+            fo = T.lst[:, bs]
+            ts(fo, T.s2[:, n0 + 31:n1:32], 8192.0, c(LF), AL.mult, AL.add, ["s2" + U, "lf"], ["fo" + U], 8)
+            cp(T.fu[:, hs], vwin.indirect(fo), vkeys + ["fo" + U], ["fu" + U], 50 + n * GATH)
+        allu = [u[0] for u in UNITS]
+        for h in (1, 0):
+            hu = sorted(set(unit[(h, b)] for b in range(8)))
+            act(tl(NH, h), T.s2[:, 256 * h + 31:256 * h + 256:32], AF.Relu, ["spc"] + ["s2" + u for u in hu], ["nh%d" % h], 8, bias=c(SPC), scale=-SPARE * 512)
+        act(tl(NB), T.s2[:, 31::32], AF.Relu, ["ab"] + ["s2" + u for u in allu], ["nb"], 16, bias=c(AB + 1), scale=-4096.0 * 512)
+        tt(tl(SNN), tl(SPTR), tl(NB), AL.min, ["sptr", "nb"], ["snn"], 32)
+        tt(tl(SP2), tl(NP0 + (t + 1) % 3), tl(NB), AL.subtract, ["np%d" % ((t + 1) % 3), "nb"], ["sp2"], 32)
+        tt(tl(SPTR), tl(SNN), tl(SP2), AL.max, ["snn", "sp2"], ["sptr"], 32)
+        if not last:
+            next_lists(t)
+            act(tl(HF), T.s2[:, 31::32], AF.Sign, ["s2" + u for u in allu], ["hf"], 16, scale=-1.0)
+            lo = 512 * (1 - t % 2)
+            tt(T.mvb[:, lo + 29:lo + 512:32], T.nn[:, 31::32], tl(HF), AL.min, ["hf"] + ["nn" + u for u in allu], ["lo%d" % (1 - t % 2)], 32, "lo")
+            op("s", lambda: [S.activation(tl(SG), T.nn[:, 31::32], AF.Sign, bias=c(NHF), accum_out=c(CNT))], ["nhf"] + ["nn" + u for u in allu], ["cnt"], 90)
+            pA = T.pU[:, 256:257]
+            mm([(T.pU[:, 260:261], T.hf[:, 128:256], c(CNT), True, True), (pA, T.hf[:, 0:128], c(CNT), True, False), cm(pA, "15", 1), cm(pA, "32m", 1),
+                cm(pA, "-32m", 1), (pA, T.hf[:, 128:256], c(CNT), False, True)], ["hf0", "hf1", "cnt", "one", "cl15", "cl32m", "cl-32m"], ["pU"], 960, "A")
+            act(c(AQ), pA, AF.Identity, ["pU", "ab"], ["am"], 1, bias=c(AB + t + 1))
+            act(c(C32 + t + 1), T.pU[:, 260:261], AF.Identity, ["pU", "b37"], ["c32%d" % (t + 1)], 1, bias=c(B37), scale=32.0, nm="c32")
+            act(T.thT[:], T.th0[:], AF.Identity, ["th0", "am"], ["thT"], 128, bias=c(AQ))
         for h in (1, 0):
             D, H = T["D%d" % h], str(h)
             hs = slice(128 * h, 128 * h + 128)
-            ia, ib = T.ti[:, 48 + 8 * h:56 + 8 * h], T.ti[:, 64 + 8 * h:72 + 8 * h]
+            hu = sorted(set(unit[(h, b)] for b in range(8)))
+            zo, zn_ = T.zs[:, 256 * t + 128 * h:256 * t + 128 * h + 128], T.zs[:, 256 * (t + 1) + 128 * h:256 * (t + 1) + 128 * h + 128]
+            zk = "z%d%d" % (t + 1, h)
+            mm([cm(T.pY[:, 0:256], "q", 256, True), (T.pY[:, 0:128], T.In[:], zo, False, False)], ["one", "clq", "In", "z%d%d" % (t, h)], ["pY"], 384, "Y0" + H)
             p0 = 0
             ND = len(DCH[h])
             for q, (n, who) in enumerate(DCH[h]):
                 dq = D[:, p0:p0 + n]
                 src = T.X[:, 0:2064].indirect(T.fu[:, 128 * h + p0 // 16:128 * h + (p0 + n) // 16])
-                fuk = ["fu%d%d" % (h, x) for x in range(p0 // 1024, (p0 + n - 1) // 1024 + 1)]
+                fuk = sorted(set("fu" + unit[(h, x)] for x in range(p0 // 256, (p0 + n - 1) // 256 + 1)))
                 if who == "s":
-                    act(dq, src, AF.Copy, ["X", "Xs"] + fuk, ["D%d%d" % (h, q)], 65 + n * GATH)
+                    act(dq, src, AF.Copy, Xk + fuk, ["D%d%d" % (h, q)], 65 + n * GATH)
                 else:
-                    cp(dq, src, ["X", "Xs"] + fuk, ["D%d%d" % (h, q)], 50 + n * GATH)
+                    cp(dq, src, Xk + fuk, ["D%d%d" % (h, q)], 50 + n * GATH)
                 e = slice(2048 * h + p0, 2048 * h + p0 + n)
                 scan(T.MX[:, e], T.mk0[:, 0:n], dq, AL.mult, AL.max, ["mk0", "D%d%d" % (h, q)], ["MX%d%d" % (h, q)], n // 2)
                 scan(T.MN[:, e], T.mkB[:, 0:n], dq, AL.add, AL.min, ["mkB", "D%d%d" % (h, q)], ["MN%d%d" % (h, q)], n // 2)
                 p0 += n
-            act(tl(NH, h), tl(T3, h), AF.Relu, ["m1", "t3%d0" % h, "t3%d1" % h], ["nh" + H], 8, bias=c(43), scale=-SPARE)
-            if h == 0:
-                tt(tl(CE, 0), tl(BASE, 0), tl(NH, 0), AL.add, ["base", "nh0"], ["ce"], 16)
             if h:
-                Fi, fk = T.fs[:, 128 * t:128 * t + 128], "fs%d" % t
-            elif t < 4:
-                Fi, fk = T.VT[:, VLOG + 256 * t:VLOG + 256 * t + 128], "VL%d" % t
-            elif t == 4:
-                Fi, fk = T.VT[:, V0:V0 + 128], "V0a"
+                Fi, fk = T.fs[:, 136 * t:136 * t + 128], "fs%d" % t
+            elif not last:
+                Fi, fk = T.VT[:, VL[t]:VL[t] + 128], "VL%d" % t
             else:
                 Fi, fk = T.fe[:], "fe"
-            cp(Fi, T.fu[:, hs], ["fu%d0" % h, "fu%d1" % h], [fk], 128)
-            if h and not last:
-                send("F", Fi, [fk])
-            ends = slice(2048 * h + 15, 2048 * h + 2048, 16)
-            zo, zn_ = T.zs[:, 256 * t + 128 * h:256 * t + 128 * h + 128], T.zs[:, 256 * (t + 1) + 128 * h:256 * (t + 1) + 128 * h + 128]
-            zk = "z%d%d" % (t + 1, h)
-            mm([(T.pY[:, 0:256], T.one[0:1, :], T.cY[0:1, :], True, False), (T.pY[:, 0:128], T.In[:], zo, False, False)],
-               ["one", "cY", "In", "z%d%d" % (t, h)], ["pY"], 384)
-            mm([(T.pY[:, 0:128], T.Ih[:], T.MX[:, ends], False, False), (T.pY[:, 128:256], T.Ih[:], T.MX[:, ends], False, False),
-                (T.pY[:, 0:128], T.Ih[:], T.MN[:, ends], False, False), (T.pY[:, 128:256], T.Ih[:], T.MN[:, ends], False, True)],
-               ["Ih"] + ["M%s%d%d" % (x, h, q) for x in "XN" for q in range(ND)], ["pY"], 512)
-            yo, yk = (T.ysn[:, 136 * t:136 * t + 128], "ya%d" % t) if h else (T.W[:, 264 * t:264 * t + 128], "W%d" % t)
-            act(T.dz[:, 256 * h:256 * h + 128], T.pY[:, 0:128], AF.Identity, ["pY", "m1"], ["dz" + H], 128, bias=c(40))
-            act(T.dz[:, 256 * h + 128:256 * h + 256], T.pY[:, 128:256], AF.Identity, ["pY", "m1"], ["dy" + H], 128, bias=c(40))
-            act(zn_, T.dz[:, 256 * h:256 * h + 128], AF.Abs, ["dz" + H, "m1"], [zk], 128, bias=c(41))
-            act(yo, T.dz[:, 256 * h + 128:256 * h + 256], AF.Identity, ["dy" + H, "m1"], [yk], 128, bias=c(41))
-            z0c = 256 * (t + 1) + 128 * h
-            mm([(T.pV[:, 256:264], T.ZW[:, 15 - a:143 - a], T.zs[:, z0c + a:z0c + 128:16], a == 0, a == 15) for a in range(16)],
-               ["ZW", zk], ["pV"], 1024)
-            cp(ia, T.pV[:, 256:264], ["pV"], ["ia" + H], 8)
-            mm([(T.pV[:, 0:128], T.one[0:2, :], T.cU[0:2, 0:128], True, False), (T.pV[:, 0:128], T.BW[:], zn_, False, True)],
-               ["one", "cU", "BW", zk], ["pV"], 256)
-            mm([(T.pU[:, 0:128], T.one[0:2, :], T.cU[0:2, 128:256], True, False), (T.pU[:, 0:128], T.BW[:], zn_, False, False)],
-               ["one", "cU", "BW", zk], ["pU"], 256)
-            ts(ib, ia, 7, None, AL.bitwise_and, None, ["ia" + H], ["ib" + H], 8)
+            cp(Fi, T.fu[:, hs], ["fu" + u for u in hu], [fk], 128, "F" + H)
             if h:
-                tt(T.ysn[:, 136 * t + 128:136 * t + 136], ib, tl(NH, h), AL.add, ["ib" + H, "nh" + H], ["yb%d" % t], 16)
+                tt(T.fs[:, 136 * t + 128:136 * t + 136], T.tf[:, 0:8], tl(NH, 1), AL.add, ["base1", "nh1"], ["fb%d" % t], 16, "fb")
+                if last:
+                    send("F", T.fs[:, 136 * t + 128:136 * t + 136], ["fb%d" % t])
+                else:
+                    send("F", T.fs[:, 136 * t:136 * t + 136], [fk, "fb%d" % t])
+            ends = slice(2048 * h + 15, 2048 * h + 2048, 16)
+            for x in ("MX", "MN"):
+                mm([(T.pY[:, 0:128], T.Ih[:], T[x][:, ends], False, False), (T.pY[:, 128:256], T.Ih[:], T[x][:, ends], False, False)]
+                   + ([cm(T.pY[:, 0:256], "m", 256, False, True)] if x == "MN" else []),
+                   ["Ih", "one", "clm"] + ["%s%d%d" % (x, h, q) for q in range(ND)], ["pY"], 512 if x == "MN" else 256, "Y" + x[1] + H)
+            yo, yk = (T.ysn[:, 136 * t:136 * t + 128], "ya%d" % t) if h else (T.W[:, 264 * t:264 * t + 128], "W%d" % t)
+            act(zn_, T.pY[:, 0:128], AF.Abs, ["pY", "nm1"], [zk], 128, bias=c(NM1), nm="z" + H)
+            act(yo, T.pY[:, 128:256], AF.Identity, ["pY", "nm1"], [yk], 128, bias=c(NM1), nm="y" + H)
+            z0c = 256 * (t + 1) + 128 * h
+            pw = T.pW[:, 0:8]
+
+            def wsum(Z, stop, z0c=z0c, pw=pw):
+                return [(pw, Z[:, 15 - a:143 - a], T.zs[:, z0c + a:z0c + 128:16], False, stop and a == 15) for a in range(16)]
+            if h:
+                mm([cm(pw, "-3", 8, True)], ["one", "cl-3"], ["pW"], 64, "W01")
+                mm(wsum(T.ZW, True), ["ZW", zk], ["pW"], 1024, "W1")
+                ts(T.tf[:, 32:40], pw, 8 * M1, 8 * M1, AL.add, AL.subtract, ["pW"], ["r8"], 8)
+                tt(T.ysn[:, 136 * t + 128:136 * t + 136], pw, T.tf[:, 32:40], AL.subtract, ["pW", "r8"], ["yb%d" % t], 8, "yb")
                 send("Y", T.ysn[:, 136 * t:136 * t + 136], ["ya%d" % t, "yb%d" % t])
             else:
-                tt(tl(OFF, 0), ib, tl(CE, 0), AL.add, ["ib0", "ce"], ["off0"], 16)
-            act(T.r0[:, hs], T.pV[:, 0:128], AF.Identity, ["pV", "m1"], ["r0" + H], 128, bias=c(42))
-            act(T.rr[:, hs], T.r0[:, hs], AF.Identity, ["r0" + H, "m1"], ["rr" + H], 128, bias=c(42), scale=-1.0)
-            mm([(T.pU[:, 0:128], T.If[:], T.rr[:, hs], False, True)], ["If", "rr" + H], ["pU"], 512)
-            tt(T.pr[:, hs], T.pU[:, 0:128], Fi, AL.mult, ["pU", fk], ["pr" + H], 128)
+                mm([cm(pw, "3", 8, True)], ["one", "cl3"], ["pW"], 64, "W00")
+                mm(wsum(T.ZN, False) + [cm(pw, "8m", 8), cm(pw, "-8m", 8), (pw, T.I1[:], tl(NH, 0), False, False), (pw, T.I1[:], tl(BASE, 0), False, False)]
+                   + wsum(T.ZW, True), ["ZW", "ZN", "I1", "one", "cl8m", "cl-8m", "nh0", "base0", zk], ["pW"], 2304, "W0")
+                ts(T.lst[:, 16:24], pw, c(L16), None, AL.add, None, ["pW", "l16"], ["wo0"], 8)
+            pu = T.pU[:, 0:128]
+            mm([cm(pu, "u0", 128, True), (pu, T.BN[:], zn_, False, False), cm(pu, "um", 128), cm(pu, "-um", 128), cm(pu, "32", 128),
+                (pu, T.BW[:], zn_, False, True)], ["one", "clu0", "clum", "cl-um", "cl32", "BW", "BN", zk], ["pU"], 768, "U" + H)
+            tt(T.pr[:, hs], pu, Fi, AL.mult, ["pU", fk], ["pr" + H], 128)
             ts(T.qi[:, hs], T.pr[:, hs], c(C32 + t), None, AL.add, None, ["pr" + H, "c32%d" % t], ["qi" + H], 128)
-            s1 = RING + 256 * ((t + 1) % 3) + 128 * h
-            if h == 0:
-                tt(tl(SNN), tl(SPTR), tl(NH), AL.min, ["sptr", "nh0", "nh1"], ["snn"], 32)
-                tt(tl(SP2), tl(NP0 + (t + 1) % 3), tl(NH), AL.subtract, ["np%d" % ((t + 1) % 3), "nh0", "nh1"], ["sp2"], 32)
-                tt(tl(SPTR), tl(SNN), tl(SP2), AL.max, ["snn", "sp2"], ["sptr"], 32)
-                if not last:
-                    next_lists()
-                    pA = T.pN[:, 16:32]
-                    mm([(pA, T.o4[:], T.bo[:], True, True)], ["o4", "bo00", "bo01", "bo10", "bo11"], ["pN"], 64)
-                    op("s", lambda pA=pA: [S.activation(tl(13), pA, AF.Copy, accum_out=c(A4))], ["pN"], ["a4"], 250)
-                    act(c(54), c(A4), AF.Identity, ["a4", "m1"], ["aq1"], 1, bias=c(47), scale=2.0 ** -17)
-                    act(c(55), c(54), AF.Identity, ["aq1", "m1"], ["aq2"], 1, bias=c(40))
-                    act(c(56), c(55), AF.Identity, ["aq2", "m1"], ["aq"], 1, bias=c(41))
-                    act(c(C32 + t + 1), c(A4), AF.Identity, ["a4", "b37"], ["c32%d" % (t + 1)], 1, bias=c(B37), scale=2.0 ** -7)
-                    act(c(AQ), c(56), AF.Identity, ["aq", "a4"], ["am"], 1, bias=c(A4), scale=-131072.0)
-                    act(T.thT[:], T.th0[:], AF.Identity, ["th0", "am"], ["thT"], 128, bias=c(AQ))
-            ts(T.VT[:, s1:s1 + 128], T.qi[:, hs], 5, 2047, AL.arith_shift_right, AL.bitwise_and, ["qi" + H], ["S%d%d" % ((t + 1) % 3, h)], 128)
-        tt(tl(OFF, 1), T.W[:, 264 * t + 256:264 * t + 264], tl(BASE, 1), AL.add, ["lY%d" % t, "base"], ["off1"], 16)
-        for hh in ([(0, 1)] if JOINT[0 if hop is None else 1] else [(0,), (1,)]):
-            a0, n, H = 128 * hh[0], 128 * len(hh), str(hh[0])
-            cs = slice(a0, a0 + n)
-            Y = T.W[:, 264 * t + a0:264 * t + a0 + n]
-            yk = [("W%d" % t, "lY%d" % t)[h] for h in hh]
-            wo = T.lst[:, 16 + a0 // 16:16 + (a0 + n) // 16]
-            wk = ["wo%d" % h for h in hh]
-            cp(wo, T.tf[:, 16 * OFF + a0 // 16:16 * OFF + (a0 + n) // 16], ["off%d" % h for h in hh], wk, 16)
+            s1 = RING[(t + 1) % 3] + 128 * h
+            ts(T.VT[:, s1:s1 + 128], T.qi[:, hs], 5, 2047, AL.arith_shift_right, AL.bitwise_and, ["qi" + H], ["S%d%d" % ((t + 1) % 3, h)], 128, "S" + H)
+        for h in WORD[0 if hop is None else 1]:
+            H = str(h)
+            cs = slice(128 * h, 128 * h + 128)
+            Y = T.W[:, 264 * t + 128 * h:264 * t + 128 * h + 128]
+            yk = ("W%d" % t, "lY%d" % t)[h]
+            wo, wk = T.lst[:, 16 + 8 * h:24 + 8 * h], "wo" + H
+            if h:
+                fb = T.fl5[:] if last else T.VT[:, VL[t] + 256:VL[t] + 264]
+                tt(T.tf[:, 48:56], T.W[:, 264 * t + 256:264 * t + 264], fb, AL.add, ["lY%d" % t, "lF%d" % t], ["off1"], 16)
+                ts(wo, T.tf[:, 48:56], 3.5, None, AL.add, None, ["off1"], [wk], 8)
+            pk = ("pP", "pK0")[h]
+            pp = T[pk][:, 0:128]
             if not last:
-                pa, pb, ka, kb = T["pK" + H][:, 0:n], T["pD" + H][:, 0:n], "pK" + H, "pD" + H
-                tt(T.dd[:, cs], T.X[:].indirect(wo), Y, AL.max, ["X", "Xs", "Xt"] + wk + yk, ["dd" + H], 50 + n * GATH)
-                act(T.ad[:, cs], T.P[:].indirect(wo), AF.Copy, Pk + ["Pt"] + wk, ["ad" + H], 65 + n * GATH)
-            cp(T.X[:].indirect(wo), Y, wk + yk, ["X", "Xs", "Xt"], 50 + n * SCAT)
+                tt(T.dd[:, cs], T.X[:].indirect(wo), Y, AL.max, Xk + Xt + [wk, yk], ["dd" + H], 50 + 128 * GATH)
+                act(T.ad[:, cs], T.X[:].indirect(wo), AF.Copy, Xk + Xt + [wk], ["ad" + H], 65 + 128 * GATH)
+            cp(T.X[:].indirect(wo), Y, [wk, yk], Xk + Xt, 50 + 128 * SCAT, "X" + H)
             if not last:
-                mm([(pb, T.Bc[:], T.CI[:, cs], True, False), (pb, T.WB[:, 0:128], Y, False, False)], ["Bc", "CI", "WB"] + yk, [kb], 2 * n)
-                mm([(pa, T.WA[:, 0:128], Y, True, False)], ["WA"] + yk, [ka], n)
-                mm([(pa, T.WA[:, 128:256], T.dd[:, cs], False, False), (pa, T.WA[:, 256:384], T.ad[:, cs], False, True)], ["dd" + H, "ad" + H], [ka], 2 * n)
-                mm([(pb, T.WB[:, 128:256], T.dd[:, cs], False, False), (pb, T.WB[:, 256:384], T.ad[:, cs], False, True)], ["dd" + H, "ad" + H], [kb], 2 * n)
-                ts(T.ra[:, cs], pa, 16 * M1, 16 * M1, AL.add, AL.subtract, [ka], ["ra" + H], n)
-                act(T.rb[:, cs], pb, AF.Identity, [kb, "BJ"], ["rb" + H], n, bias=T.col[:, 48 + t:49 + t])
-                tt(T.P[:].indirect(wo), T.rb[:, cs], T.ra[:, cs], AL.subtract, wk + ["ra" + H, "rb" + H], Pk + ["Pt"], 50 + n * SCAT)
-        if t == 4:
-            cp(T.VT[:, V0 + 128:V0 + 256], T.fl4[:], ["lF4"], ["V0a"], 128)
-    cp(T.lst[:, 32:48], tl(SPTR), ["sptr"], ["sl"], 16)
-    cp(T.pr[:], T.VT[:, 0:V0].indirect(T.lst[:, 32:48]), ring + ["sl"], ["pr0", "pr1"], 50 + 256 * GATH)
-    for h in (0, 1):
-        act(T.yso[:, h::2], T.pr[:, 128 * h:128 * h + 128], AF.Copy, ["pr0", "pr1"], ["yso%d" % h], 128)
+                mm([(pp, T.Bc[:], T.CI[:, 128:256], True, False), (pp, T.WA[:, 0:128], Y, False, False)], ["Bc", "CI", yk] + WAk, [pk], 256, "Pa" + H)
+                mm([(pp, T.WA[:, 128:256], T.dd[:, cs], False, False), (pp, T.WA[:, 256:384], T.ad[:, cs], False, False),
+                    cm(pp, "64m", 128), cm(pp, "-64m", 128), (pp, T.WB[:, 0:128], Y, False, False),
+                    (pp, T.WB[:, 128:256], T.dd[:, cs], False, False), (pp, T.WB[:, 256:384], T.ad[:, cs], False, True)],
+                   ["dd" + H, "ad" + H, "WB0", "WB1", "one", "cl64m", "cl-64m"], [pk], 896, "Pb" + H)
+                act(T.rb[:, cs], pp, AF.Identity, [pk, "BJ"], ["rb" + H], 128, bias=T.BJ[:, 2 * t + h:2 * t + h + 1])
+                if PSCAT[0] == "v":
+                    cp(T.P[:].indirect(wo), T.rb[:, cs], [wk, "rb" + H], Pk, 50 + 128 * SCAT, "P" + H)
+                else:
+                    op("s", lambda wo=wo, cs=cs: [S.activation(T.P[:].indirect(wo), T.rb[:, cs], AF.Silu)], [wk, "rb" + H], Pk, (65 + 128 * SCAT) * CYC, nm="P" + H)
+    ts(T.lst[:, 32:48], tl(SPTR), c(LF), None, AL.add, None, ["sptr", "lf"], ["sl"], 16)
+    for h in (1, 0):
+        win, keys = upto(RING[2] + 256)
+        cp(T.yso[:, h::2], win.indirect(T.lst[:, 32 + 8 * h:40 + 8 * h]), keys + ["sl"], ["yso%d" % h], 50 + 128 * GATH)
         act(T.yzo[:, h::2], T.zs[:, 256 * TS + 128 * h:256 * TS + 128 * h + 128], AF.Copy, ["z%d%d" % (TS, h)], ["yzo%d" % h], 128)
-    dma("y", "ox", T.yx[:], T.X[:, 0:2048], ["X"], [], 4500)
+    dma("y", "ox", T.yx[:], T.X[:, 0:2048], Xk, [], 4500)
     dma("s", "oz", T.yz[:], T.yzo[:], ["yzo0", "yzo1"], [], 2200)
     dma("s", "os_", T.ys[:], T.yso[:], ["yso0", "yso1"], [], 2400)
     return ops, sent
@@ -470,8 +509,8 @@ def plan(g, core, T, topo, rank):
 def depend(ops):
     lw, rd, deps = {}, {}, []
     for i, o in enumerate(ops):
-        r = [k for k in o[2] if k[:2] not in ("pK", "pD", "pN", "pY", "pU", "pV") or len(k) > 3]
-        w = o[3] + [k for k in o[2] if k not in r]
+        r = [k for k in o[2] if k not in BANKS]
+        w = o[3] + [k for k in o[2] if k in BANKS]
         d = set()
         for k in r:
             if k in lw:
@@ -490,99 +529,64 @@ def depend(ops):
     return deps
 
 
-def tag(o):
-    def bare(k):
-        if k[:2] == "zr":
-            return "zr"
-        if k[:2] == "mv":
-            return "mv" + k[3:]
-        if (len(k) == 3 and k[0] in "zS" and k[1].isdigit()):
-            return k[:-2] + k[-1]
-        if k[:-1] in ("W", "ya", "yb", "fs", "VL", "c32", "mF", "mY", "lF", "lY"):
-            return k[:-1]
-        return k
-    return o[0] + bare(o[3][0] if o[3] else "") + bare(o[2][-1] if o[2] else "")
-
-
-SHIFT = ["PKQPM=`mNFKIXQOF?TETR`]RU9>POHa]`>LEdODQSV=1iMYCABTeBKV]]YADXD;[AKGDLSQ``iTWRZRYPBPSVTPIINFWQ@Y`QNaT;HpHP0GMSWKSLLEYJ]]:PDPc]<UJRJKU[Dg8F[OUULUSAURGS`[ODWX]PVPPUMMMOPPOJJNKSBMCUK>hnUMIBb@FGL>PMXVBLSDT[AO`I]VRT]QSPJS7LOPEPTMQI@MXGR[^Zb?kURP@IQMU]VgOMB2OSQeWL[OBXPM]QQ8X[PDLABJ[M`YZSWM>0DVCO]Rgg`MSTTIhXUOPPPR=QJBhHdJTMO>k]DT`KDYNEVPQFCgSj]NC]NHOM?PE]Y`aZJ9MM6PMHY?9QWC"]
-
-
-def order(ops, deps):
+def order(ops, deps, place=None):
     n = len(ops)
+    if place is None:
+        place = {}
+        for p, name in enumerate(ORDER):
+            place[name.rstrip("+-")] = p / len(ORDER) + name.count("+") - name.count("-")
     succ = [[] for _ in range(n)]
     for i in range(n):
         for d in deps[i]:
             succ[d].append(i)
-    prio = [0.0] * n
+    key = [0.0] * n
     for i in range(n - 1, -1, -1):
-        prio[i] = ops[i][4] + max([LAT + prio[s] for s in succ[i]] + [0.0])
-    tags = [tag(o) for o in ops]
-    shift = dict(zip(sorted(set(tags)), SHIFT[0]))
-    for i in range(n):
-        prio[i] += 300.0 * (ord(shift.get(tags[i], "P")) - 80)
-    left = [len(d) for d in deps]
-    ready_at = [0.0] * n
-    ready = [i for i in range(n) if not left[i]]
-    free = {}
-    out, end, starts = [], 0.0, []
-    while ready:
-        t0, e = min((max(ready_at[i], free.get(ops[i][0], 0.0)), ops[i][0]) for i in ready)
-        mine = sorted((i for i in ready if ops[i][0] == e), key=lambda i: -prio[i])
-        limit = 1e30
-        for i in mine:
-            st = max(ready_at[i], t0)
-            if st <= t0 + ALPHA[1] and st + ops[i][7] <= limit + ALPHA[0] * prio[i]:
-                break
-            limit = min(limit, st + ALPHA[2] - ALPHA[0] * prio[i])
+        if ops[i][8] >= 0:
+            key[i] = ops[i][8] + place.get(ops[i][9], 1.9)
         else:
-            i = mine[0]
-            st = max(ready_at[i], t0)
+            key[i] = min([key[s] for s in succ[i]] + [9.0]) - (ops[i][4] + LAT) / 20000 - (ops[i][9] in FIRST)
+    left = [len(d) for d in deps]
+    ready = [i for i in range(n) if not left[i]]
+    line = []
+    while ready:
+        i = min(ready, key=lambda i: (key[i], i))
         ready.remove(i)
-        out.append(i)
-        starts.append(st)
-        free[ops[i][0]] = st + ops[i][7]
-        end = max(end, st + ops[i][4])
+        line.append(i)
         for s in succ[i]:
-            lat = 0.0 if ops[i][0] == "p" and ops[s][0] == "p" else LAT
-            ready_at[s] = max(ready_at[s], st + ops[i][4] + lat)
             left[s] -= 1
             if not left[s]:
                 ready.append(s)
-    best = (end, out, starts)
-    fin = {i: s + ops[i][4] for i, s in zip(out, starts)}
-    for _ in range(PASSES[0]):
-        fin = pack(ops, sorted(fin, key=lambda i: (-fin[i], -i)), succ, True)[1]
-        st, fin = pack(ops, sorted(fin, key=lambda i: (-fin[i], i)), deps, False)
-        if max(fin.values()) < best[0]:
-            o = sorted(st, key=lambda i: (st[i], i))
-            best = (max(fin.values()), o, [st[i] for i in o])
-    return best[1], best[0], best[2]
+    queue = {}
+    for i in line:
+        if ops[i][8] >= 0:
+            queue.setdefault(ops[i][0], []).append(i)
+    rest = [i for i in line if ops[i][8] < 0]
+    fin, free, out = {}, {}, []
 
-
-def pack(ops, seq, before, back):
-    busy, start, fin = {}, {}, {}
-    for i in seq:
-        e, cost, hold = ops[i][0], ops[i][4], ops[i][7]
-        r = 0.0
-        for d in before[i]:
-            r = max(r, fin[d] + (0.0 if e == "p" and ops[d][0] == "p" else LAT))
-        if back:
-            r += cost - hold
-        b = busy.setdefault(e, [])
-        lo, hi = 0, len(b)
-        while lo < hi:
-            mid = (lo + hi) // 2
-            if b[mid][1] <= r:
-                lo = mid + 1
-            else:
-                hi = mid
-        while lo < len(b) and b[lo][0] < r + hold:
-            r = max(r, b[lo][1])
-            lo += 1
-        b.insert(lo, (r, r + hold))
-        start[i] = r
-        fin[i] = r + (hold if back else cost)
-    return start, fin
+    def start(i):
+        if any(d not in fin for d in deps[i]):
+            return None
+        e = ops[i][0]
+        return max([free.get(e, 0.0)] + [fin[d] + (0.0 if e == "p" and ops[d][0] == "p" else LAT) for d in deps[i]])
+    while rest:
+        pick = []
+        for e in "vspgyx":
+            head = start(queue[e][0]) if queue.get(e) else None
+            mine = [(s, i) for s, i in ((start(i), i) for i in rest if ops[i][0] == e) if s is not None]
+            if mine:
+                t0 = min(mine)[0]
+                s, i = [x for x in mine if x[0] <= t0 + EARLY[0]][0]
+                if head is None or s + ops[i][7] <= head + EARLY[1] or key[i] < key[queue[e][0]] and s <= head:
+                    pick.append((s, i))
+                    continue
+            if head is not None:
+                pick.append((head, queue[e][0]))
+        s, i = min(pick)
+        (rest if ops[i][8] < 0 else queue[ops[i][0]]).remove(i)
+        out.append(i)
+        fin[i] = s + ops[i][4]
+        free[ops[i][0]] = s + ops[i][7] if ops[i][0] != "x" else 0.0
+    return out + [i for i in line if i not in fin]
 
 
 CACHE = {}
@@ -596,9 +600,8 @@ def rank_program(g, core, T, topo):
     ops, sent = plan(g, core, T, topo, rank)
     if "o" not in CACHE:
         d = depend(ops)
-        CACHE["o"] = (d,) + order(ops, d)
-        CACHE["ops"] = ops
-    deps, seq = CACHE["o"][0], CACHE["o"][1]
+        CACHE["o"] = (d, order(ops, d))
+    deps, seq = CACHE["o"]
     Q = {"v": g.vector, "s": g.scalar, "p": g.tensor, "g": g, "y": g.sync}
     count, mark, seen, known = {}, {}, {}, {}
     place = {i: p for p, i in enumerate(seq)}

@@ -7,14 +7,36 @@ XW = 4352
 RING, V0, VL, VW = (16, 2320, 2848), 272, (2576, 3104, 3376, 3648, 3920), 4192
 SPARE = 2304.0
 M1 = 12582912.0
-UNITS = [("a", 1, 0, 4, 1, 1), ("b", 1, 4, 4, 0, 1), ("c", 0, 0, 4, 1, 1), ("d", 0, 4, 4, 0, 1)]
-DCH = {0: [(512, "s"), (512, "s"), (512, "v"), (512, "s")], 1: [(512, "s")] * 4}
+UNITS = [("a", 1, 0, 4, 1, 2, 1), ("b", 1, 4, 4, 0, 2, 1), ("c", 0, 0, 4, 1, 2, 2), ("d", 0, 4, 4, 0, 2, 2)]
+DCH = {0: [(512, "s"), (512, "s"), (256, "v"), (256, "s"), (256, "s"), (256, "s")], 1: [(512, "s")] * 4}
 PSCAT = ["s"]
-WORD = [(0, 1), (0, 1)]
-EARLY = [100, 30]
-FIRST = ("one",)
+WORD = [(1, 0), (0, 1)]
+WV0 = [True]
+GV = []
+VCUT = 512
+PS = [6, 7]
+SETUP = """
+s.wai s.zin s.sci s.thi s.wti y.X0 y.X1 y.X2 y.X3 y.vw0 y.vw1
+v.one g.ti0 g.BI g.pmc g.CI v.ti1 v.ti3 v.pf v.ti2 v.lf g.KI g.np0 g.HI g.a4 g.VTd g.mvc g.GI v.q4 v.c16g v.c15 v.tn v.p15 v.dq v.Z8 v.turn
+v.l8 v.dkf v.lp v.c4 v.wab v.I1 v.ta v.c44 v.Bc v.tbc v.ZP v.BI v.mlo s.Xs s.cl-3 s.mkN s.Ps s.ab7 s.mkC s.gf s.na s.CV s.c4g v.BX1 s.hf1
+s.In s.wd s.wr s.z00 s.z01 s.spc s.TB s.zp g.ze s.cl-um v.ZM v.BX0 p.pW v.snn v.wtf v.zo1 v.zo3 v.zo2 v.zo0 v.S01 v.S00 s.BIn p.SL p.m0
+p.wt p.m1 p.m2 p.m3 s.ZR s.nhf s.mvc s.nm1 s.cl15 s.sptr s.cl32m s.t10 s.thf s.ZD s.thT s.t11 s.wf v.sl v.P0 v.Bf v.soff1 s.clm v.P1
+s.t12 s.t13 s.Ih s.l16 v.P2 v.soff0 v.P3 p.m4 s.t14 v.wv v.P4 p.m5 s.t15 v.P5 p.m6 p.m7 g.mk0 g.mkB p.pU s.ab6 s.ZV s.Is s.BW s.t16
+g.base1 s.t17 s.hf0 p.n6 s.clq s.WB0 s.c320 p.n7 @zr1 v.V04 v.V00 @Ga0 v.V05 s.P6 s.P7 s.th0 @Ga1 v.V07 @Gb0 s.ZW @zr2 s.wn
+@Gc1 s.BN s.mk0 @nna s.mkB v.V01 @nfa v.V06 @ZVa v.V03 @foa v.V02 @zr3 g.np1 g.BJ g.BJ0 g.BS g.ab g.base0 g.Xt0 @K0d v.base1
+@s2b s.BJ s.cl-32m @fuc v.b37 @yb v.cl64m @D00 s.cl32 @nnd g.Xt1 g.Xt2 g.Xt3 g.Xt4 g.np2 g.Vp0 g.Vp1 g.Vp2 g.Vp3 @cb s.clum @am s.clu0
+@c32 s.cl-8m @hf s.WA @U1 s.cl3 @y0 s.WAj s.BS @U0 s.cl-64m @Pb0 s.WB1 @pr0 s.ZN @X0 s.cl8m @wo1 v.BJ
+""".split()
+LAST = [("W0", "U0"), ("r80", "sptr pr0 sl qi0 S0"), ("off0", "yso1"), ("y0", "yso0"), ("thT", "yzo1 yzo0 doz"), ("off1", "dos_")]
+DIRECT = [("sptr", "off1"), ("W0", "wo1"), ("off0", "dd1"), ("y0", "Pa1"), ("U0", "ad1 X1"), ("thT", "Pb1"), ("Pb0", "rb1 P1")]
 ORDER = """
-Ma0 P1+ Ma1 Ga0 Ma2 Ga1 Ma3 zr1 Ga2 Mb0 ZMa Ga3 Mc0 K0b Gb0 Mb1 ZDa Gb1 qi0+ ZRa mva Mb2 Gb2 Kma ZVa nna pma Gb3 nfa Mb3 zr2 Vfa Gc0 ZDb sptr+ S0+ s2a Gc1 foa ZMb fua mvb Mc1 Gc2 ZRb Mc2 D11 Kmb ZVb nnb pmb nfb Mc3 D10 Vfb K0d K0c MN11 ZMc zr3 s2b fob MX11 Gc3 fub Md0 nh1 D12 ZDc yzo0+ Md1 ZRc MX10 D13 MN10 mvc MX12 Kmc ZVc MN12 Gd0 pmc MX13 W01 MN13 Gd1 YX1 nnc YN1 nfc fb F1 Gd2 Vfc Md2 K0a- sendF z1 s2c Gd3 W1 foc fuc y1 Md3 D00 ZDd r8 yb ZMd mvd sendY nnd MX00 cnt ZRd D01 MN00 W00 Kmd ZVd pmd nfd MX01 Vfd Y00 MN01 A s2d fod nh0 fud D03 D02 nb hf am MX02 c32 thT MN02 U1 MX03 MN03 YX0 snn YN0 lo sl dox+ sp2 soff0 z0 F0 W0 y0 soff1 pr1 yso1+ qi1 S1 yso0+ U0 wo0 ad0 dd0 Y01- doz yzo1 dos_ off1 Pa0 X0 Pb0 zr0- Pa1 wo1 rb0 dd1 ad1 pr0 P0 Pb1 X1 rb1
+Ma0 doz+ yso1++ yso0++ dos_++ dox++ Pa1+ Pb1+ P0+ Mb0 zr1 K0b rb1+ P1+ ZMa0 Ga0 ZRa0 ZMa1 ZDa0 Ga1 ZDa1 mva ZRa1 Kma
+Gb0 zr2 Gb1 Gc0 S0+ Gc1 nna pma nfa Mc0 ZVa Vfa s2a ZDb0 ZDb1 mvb ZMb0 ZRb0 ZMb1 ZRb1 Kmb ZVb foa nnb fua D10 zr3 Mc1 pmb D11 nfb Vfb
+K0d W01 s2b nh1 MN10 fob MX10 fub MN11 D12 D13 Gd0 ZDc0 fb F1 Md0 sendF ZDc1 mvc MX11 K0c ZMc0 ZRc0 ZMc1 MN12 nnc ZRc1 ZMd0 Kmc pmc
+YX1 ZVc MX13 nfc MN13 MX12 Vfc s2c foc fuc ZRd0 Gd1 YN1 ZDd0 ZDd1 Md1 z1 W1 r8 mvd yb ZMd1 ZRd1 Kmd D00 y1 D01 sendY
+nnd cnt MN00 pmd MX00 nfd ZVd Vfd MN01 s2d Y00 fod fud W00 MX01 cb A D02 am nb snn MN02 MX02 c32 D04 MX04 MN04 D05 MN05 MX05
+D03 MX03 MN03 nh0 hf U1 SL sl YX0 YN0 z0 lo soff1 sp2 ce F0 pr1 sptr W0 r80 off0 u30 zp- y0 U0 thT Pa0 wo0 ad0 dd0 Pb0 rb0 Y01-
+pr0 K0a- zr0- X0 off1 wo1 ad1 dd1 qi0 X1 yzo1 yzo0
 """.split()
 
 bf, f32, i32, u16 = "bfloat16", "float32", "int32", "uint16"
@@ -22,9 +44,10 @@ SCRATCH = {
     "X": ("sbuf", [128, XW], bf), "P": ("sbuf", [128, XW], f32), "WA": ("sbuf", [128, 384], bf), "WB": ("sbuf", [128, 384], bf),
     "rb": ("sbuf", [128, 256], f32), "VT": ("sbuf", [128, VW], i32),
     "vwi": ("sbuf", [128, 1024], i32), "sci": ("sbuf", [128, 256], i32), "zin": ("sbuf", [128, 256], bf),
-    "wti": ("sbuf", [128, 4], i32), "thi": ("sbuf", [128, 4], i32), "wai": ("sbuf", [128, 256], i32), "wab": ("sbuf", [128, 256], bf),
+    "wti": ("sbuf", [128, 256], i32), "wtf": ("sbuf", [128, 256], f32), "wai": ("sbuf", [128, 256], i32), "wab": ("sbuf", [128, 256], bf),
     "zs": ("sbuf", [128, 7 * 256], bf), "zr0": ("sbuf", [128, 4096], bf), "zr1": ("sbuf", [128, 4096], bf),
-    "M0": ("sbuf", [128, 8, 256], bf), "M1": ("sbuf", [128, 8, 256], bf), "G0": ("sbuf", [128, 8, 256], bf), "G1": ("sbuf", [128, 8, 256], bf),
+    "M0": ("sbuf", [128, 2048], bf), "M1": ("sbuf", [128, 2048], bf), "G0": ("sbuf", [128, 2048], bf), "G1": ("sbuf", [128, 2048], bf),
+    "zp": ("sbuf", [128, 256], bf), "ZP": ("sbuf", [128, 528], bf),
     "D0": ("sbuf", [128, 2048], bf), "D1": ("sbuf", [128, 2048], bf),
     "MX": ("sbuf", [128, 4096], bf), "MN": ("sbuf", [128, 4096], bf),
     "mk0": ("sbuf", [128, 1024], bf), "mkB": ("sbuf", [128, 1024], bf), "mkN": ("sbuf", [128, 128], bf),
@@ -35,10 +58,10 @@ SCRATCH = {
     "ysn": ("sbuf", [128, 6 * 136], bf), "W": ("sbuf", [128, 6 * 264], bf),
     "pm": ("sbuf", [128, 256], f32), "pr": ("sbuf", [128, 256], f32), "qi": ("sbuf", [128, 256], i32),
     "dd": ("sbuf", [128, 256], bf), "ad": ("sbuf", [128, 256], bf),
-    "tf": ("sbuf", [128, 64], f32), "tb": ("sbuf", [128, 176], bf), "ti": ("sbuf", [128, 16], i32),
+    "tf": ("sbuf", [128, 64], f32), "tb": ("sbuf", [128, 192], bf), "ti": ("sbuf", [128, 16], i32),
     "col": ("sbuf", [128, 64], f32), "BI": ("sbuf", [128, 16], f32), "BJ": ("sbuf", [128, 16], f32),
     "th0": ("sbuf", [128, 128], f32), "thT": ("sbuf", [128, 128], f32), "dkf": ("sbuf", [128, 128], f32), "Bf": ("sbuf", [128, 128], f32),
-    "hf": ("sbuf", [128, 256], f32),
+    "hf": ("sbuf", [128, 256], bf),
     "CI": ("sbuf", [128, 256], bf), "KI": ("sbuf", [128, 128], bf), "GI": ("sbuf", [128, 128], bf), "HI": ("sbuf", [128, 128], bf),
     "ZM": ("sbuf", [128, 144], bf), "ZR": ("sbuf", [128, 144], bf), "ZD": ("sbuf", [128, 144], bf), "ZV": ("sbuf", [128, 144], bf),
     "ZW": ("sbuf", [128, 144], bf), "ZN": ("sbuf", [128, 144], bf), "Z8": ("sbuf", [128, 144], bf),
@@ -53,7 +76,8 @@ BANKS = ("pK0", "pK1", "pD0", "pD1", "pW", "pY", "pU", "pP")
 DMAS = ["x0", "x1", "x2", "x3", "vw0", "vw1", "scan", "z0", "wt", "th", "warm", "oz", "os_", "ox"]
 SEMAPHORES = (["cv", "cs", "cp", "cg", "sent"] + ["d" + n for n in DMAS]
               + ["aF%d" % t for t in range(TS)] + ["aY%d" % t for t in range(TS)])
-CYC, PCYC, GATH, SCAT, LAT, HOLD, FAR = 0.95, 0.48, 1.56, 3.8, 130, 1200, [4500, 7000]
+FIX, ROW, RATE, OV = 1900, 30, 14.0, {"v": 20, "s": 30}
+CYC, PCYC, GATH, SCAT, LAT, HOLD, ONCE, FAR = 1.0, 0.52, 1.4, 3.5, 110, 1200, 2000, [4000, 6500]
 
 
 def route(T, topo, r, t):
@@ -95,10 +119,12 @@ def plan(g, core, T, topo, rank):
     V, S, PE = g.vector, g.scalar, g.tensor
     ops = []
     sent = [0]
-    now = [-1]
+    now = [-1, ""]
 
     def op(e, fn, r, w, cost, sem=None, n=1, hold=None, nm=None):
-        ops.append((e, fn, list(r), list(w), float(cost), sem, n, float(cost if hold is None else hold), now[0], nm or (w[0] if w else sem)))
+        nm = nm or (w[0] if w else sem)
+        cost += OV.get(e, 0) if sem is None else 0
+        ops.append((e, fn, list(r), list(w), float(cost), sem, n, float(cost if hold is None else hold), now[0], nm if now[0] >= 0 else e + "." + nm, now[1]))
 
     def ts(o, i, s1, s2, a, b, r, w, n, nm=None):
         if b is None:
@@ -139,12 +165,12 @@ def plan(g, core, T, topo, rank):
 
     def c(j):
         return T.col[:, j:j + 1]
-    PF, LF, GF, C15, C16G, C4G, C4, WF, WN, THF, WR, MLO, WD, WV, TA, TBc, B37, L16, P15, CNT, AQ, NM1, SPC, NHF, LP, NA, L8 = range(27)
+    PF, LF, GF, C15, C16G, C4G, C4, WF, WN, THF, WR, MLO, WD, WV, TA, TBc, B37, L16, P15, CNT, AQ, NM1, SPC, NHF, LP, NA, L8, Q4, C44, TURN = range(30)
     C32, AB = 32, 40
 
     def tl(j, h=None):
         return T.tb[:, 16 * j:16 * j + 16] if h is None else T.tb[:, 16 * j + 8 * h:16 * j + 8 * h + 8]
-    NP0, BASE, SNN, SPTR, NH, SP2, SG, NB, HF = 0, 3, 4, 5, 6, 7, 8, 9, 10
+    NP0, BASE, SNN, SPTR, NH, SP2, SG, NB, HF, A4 = 0, 3, 4, 5, 6, 7, 8, 9, 10, 11
 
     consts = {"q": -0.25, "m": M1, "-3": -3.5, "3": 3.5, "8m": 8 * M1, "-8m": -8 * M1, "um": 2048 * M1, "-um": -2048 * M1,
               "32": 32.0, "15": 15.5, "32m": 32 * M1, "-32m": -32 * M1, "u0": -0.5, "64m": None, "-64m": None}
@@ -154,15 +180,23 @@ def plan(g, core, T, topo, rank):
         j, k = names.index(name), 2 if name == "u0" else 1
         return (o, T.cl[0:k, 128 * j:128 * j + 128], T.one[0:k, 0:n], start, stop)
 
-    dma("s", "warm", T.wai[0:8, :], T.warm[:], [], ["wai"], 2300)
-    dma("s", "scan", T.sci[:], T.scan[:], [], ["sci"], 2500)
-    dma("s", "z0", T.zin[:], T.z0[:], [], ["zin"], 2500)
-    dma("s", "th", T.thi[:, 0:1], T.th[:], [], ["thi"], 2600)
-    dma("s", "wt", T.wti[:, 0:1], T.wt[:], [], ["wti"], 2600)
+    busy = [FIX]
+
+    landed = {None: 0.0}
+
+    def load(q, name, o, i, w, rows, size, after=None):
+        busy[0] = max(busy[0], landed[after] + FIX) + rows / 16 * (ROW + size / RATE)
+        landed[w] = busy[0]
+        dma(q, name, o, i, [after] if after else [], [w], busy[0] - landed[after])
+    load("s", "warm", T.wai[0:8, :], T.warm[:], "wai", 16, 512)
+    load("s", "z0", T.zin[:], T.z0[:], "zin", 128, 512)
+    load("s", "scan", T.sci[:], T.scan[:], "sci", 128, 1024)
+    load("s", "th", T.wti[0:1, 128:256], T.th[:], "thi", 4, 128)
+    load("s", "wt", T.wti[0:1, 0:128], T.wt[:], "wti", 4, 128)
     for j in range(4):
-        dma("y", "x%d" % j, T.X[:, 512 * j:512 * j + 512], T.reg[:, 512 * j:512 * j + 512], [], ["X%d" % j], 3000 + 600 * j)
-    for j in range(2):
-        dma("y", "vw%d" % j, T.vwi[:, 512 * j:512 * j + 512], T.vw[:, 512 * j:512 * j + 512], ["X0"], ["vw%d" % j], 3200 + 1200 * j)
+        load("y", "x%d" % j, T.X[:, 512 * j:512 * j + 512], T.reg[:, 512 * j:512 * j + 512], "X%d" % j, 128, 1024)
+    load("y", "vw0", T.vwi[:, 0:VCUT], T.vw[:, 0:VCUT], "vw0", 128, 4 * VCUT, "X0")
+    load("y", "vw1", T.vwi[:, VCUT:1024], T.vw[:, VCUT:1024], "vw1", 128, 4096 - 4 * VCUT, "X0")
     Xk = ["X0", "X1", "X2", "X3", "Xs"]
     Xt = ["Xt%d" % j for j in range(5)]
     iota(T.ti[:, 0:1], [[0, 1]], 0, 1, ["ti0"], 1, small=False)
@@ -192,10 +226,10 @@ def plan(g, core, T, topo, rank):
     fill(T.X[:, 2048:2064], 0.0, ["Xs"], 16)
     fill(T.P[:, 2048:2064], 64.0, ["Ps"], 16)
     nd = max(n for h in DCH for n, _ in DCH[h])
-    ms(T.mk0[:, 0:nd], 1.0, ["mk0"], nd // 2); fill(T.mk0[:, 0:nd:16], 0.0, ["mk0"], nd // 16)
-    ms(T.mkB[:, 0:nd], 0.0, ["mkB"], nd // 2); fill(T.mkB[:, 0:nd:16], 256.0, ["mkB"], nd // 16)
+    iota(T.mk0[:, 0:nd], [[0, nd]], 1, 0, ["mk0"], nd); fill(T.mk0[:, 0:nd:16], 0.0, ["mk0"], nd // 16)
+    iota(T.mkB[:, 0:nd], [[0, nd]], 0, 0, ["mkB"], nd); fill(T.mkB[:, 0:nd:16], 256.0, ["mkB"], nd // 16)
     fill(T.mkN[:], 0.0, ["mkN"], 128); fill(T.mkN[:, ::16], -16.0, ["mkN"], 8)
-    ms(T.mvb[:, 1::2], 0.0, ["mvc"], 256)
+    iota(T.mvb[:, 1::2], [[0, 512]], 0, 0, ["mvc"], 512)
     for j, v in ((1, 2.0), (29, -1.0), (31, -2.0)):
         fill(T.mvb[:, j::32], v, ["mvc", "lo0", "lo1"], 32)
     for nm in names:
@@ -223,9 +257,12 @@ def plan(g, core, T, topo, rank):
     ts(c(B37), c(LF), 1184.0, 32768.0, AL.mult, AL.add, ["lf"], ["b37"], 1)
     for j, src, v, k in ((GF, C16G, 0.0625, "gf"), (C4G, C16G, 0.25, "c4g"), (C32, LF, 1184.0, "c320"), (L16, LF, 16.0, "l16"), (NA, LF, -2.0 ** -13, "na")):
         act(c(j), c(src), AF.Copy, ["c16g", "lf"], [k], 1, scale=v)
-    ts(c(WF), T.wti[:, 0:1], 2048.0, None, AL.mult, None, ["wti"], ["wf"], 1)
+    cp(T.wtf[0:1, :], T.wti[0:1, :], ["wti", "thi"], ["wtf"], 256)
+    fill(c(AB + 7), 2048.0, ["ab7"], 1)
+    mm([(T.pU[:, 300 + j:301 + j], T.wtf[0:1, 128 * j:128 * j + 128], T.col[0:1, AB + 7:AB + 8], True, True) for j in (0, 1)], ["wtf", "ab7"], ["pU"], 512, "wt")
+    act(c(THF), T.pU[:, 301:302], AF.Copy, ["pU"], ["thf"], 1)
+    act(c(WF), T.pU[:, 300:301], AF.Copy, ["pU"], ["wf"], 1)
     act(c(WN), c(WF), AF.Copy, ["wf"], ["wn"], 1, scale=-1.0)
-    ts(c(THF), T.thi[:, 0:1], 2048.0, None, AL.mult, None, ["thi"], ["thf"], 1)
     fill(c(AB + 6), 4096.0 * 64, ["ab6"], 1)
     ts(T.dkf[:], T.KI[:], c(LF), None, AL.is_equal, None, ["KI", "lf"], ["dkf"], 128)
     ts(T.tf[:, 0:8], T.tf[:, 0:8], c(L16), None, AL.add, None, ["base1", "l16"], ["base1"], 8)
@@ -262,7 +299,7 @@ def plan(g, core, T, topo, rank):
     WAk = []
     for m0, j, s2 in ((0, 0, 1.0), (0, 1, 1.0), (0, 2, -1.0), (0, 3, -1.0), (128, 2, 2.0), (128, 3, 2.0), (256, 2, -1.0), (256, 3, -1.0)):
         WAk.append("WA%d" % len(WAk))
-        act(T.WA[:, m0 + j:m0 + 128:16], T.Bf[:, 0::16], AF.Copy, ["Bf", "WA"], WAk[-1:], 8, scale=2048 * s2)
+        act(T.WA[:, m0 + j:m0 + 128:16], T.Bf[:, 0::16], AF.Copy, ["Bf", "WA"], WAk[-1:], 8, scale=2048 * s2, nm="WAj")
     fill(T.WB[:, 0::2], 0.0, ["WB0"], 192)
     act(T.WB[:, 1::2], T.WA[:, 1::2], AF.Copy, WAk, ["WB1"], 192, scale=-1.0)
     act(T.TB[:], T.KI[:], AF.Copy, ["KI"], ["TB"], 128, scale=-2.0 ** -16)
@@ -290,25 +327,53 @@ def plan(g, core, T, topo, rank):
 
     def next_lists(t):
         win, keys = upto(RING[min(t, 2)] + 256)
-        ts(T.lst[:, 32:48], tl(SNN), c(LF), None, AL.add, None, ["snn", "lf"], ["sl"], 16)
+        pk = "pP" if now[0] >= 0 else "pD0"
+        ps = T[pk][:, 128:144]
+        mm([(ps, T.I1[:], tl(A4), True, False)]
+           + [(T[pk][:, 128 + j:144:4], T.ZP[:, 132 * j + 4 - b:132 * j + 132 - b], T.tb[:, 16 * SNN + b:16 * SNN + 16:4], False, j + b == 6)
+              for j in range(4) for b in range(4)], ["I1", "a4", "snn"] + ["ZP%d" % j for j in range(4)], [pk], 17 * 64, "SL")
+        ts(T.lst[:, 32:48], ps, c(Q4), None, AL.add, None, [pk, "q4"], ["sl"], 16)
+        if now[0] >= 0:
+            return cp(T.soff[:], win.indirect(T.lst[:, 32:48]), keys + ["sl"], ["soff1", "soff0"], 50 + 256 * GATH)
         for h in (1, 0):
             cp(T.soff[:, 128 * h:128 * h + 128], win.indirect(T.lst[:, 32 + 8 * h:40 + 8 * h]), keys + ["sl"], ["soff%d" % h], 50 + 128 * GATH)
+
+    def turn_z(t):
+        act(T.zp[:], T.zs[:, 256 * t:256 * t + 256].indirect(T.lst[:, 48:64]), AF.Copy, ["z%d0" % t, "z%d1" % t, "turn"], ["zp"], 65 + 256 * GATH)
+    ts(T.ti[:, 2:3], T.ti[:, 0:1], 3, None, AL.bitwise_and, None, ["ti0"], ["ti2"], 1)
+    ts(T.ti[:, 3:4], T.ti[:, 0:1], 2, 3, AL.arith_shift_right, AL.bitwise_and, ["ti0"], ["ti3"], 1)
+    cp(c(Q4), T.ti[:, 3:4], ["ti3"], ["q4"], 1)
+    ts(c(C44), T.ti[:, 2:3], 4.0, c(C4), AL.mult, AL.add, ["ti2", "c4"], ["c44"], 1)
+    ts(c(TURN), T.ti[:, 2:3], 16.0, c(Q4), AL.mult, AL.add, ["ti2", "q4"], ["tn"], 1)
+    ts(T.tf[:, 28:32], T.CI[:, 0:4], c(Q4), None, AL.is_equal, None, ["CI", "q4"], ["dq"], 4)
+    for j in range(4):
+        ts(T.ZP[:, 132 * j:132 * j + 132], T.CI[:, 0:132], c(C44), T.tf[:, 28 + j:29 + j], AL.is_equal, AL.mult, ["CI", "c44", "dq"], ["ZP%d" % j], 66, "ZP")
+    iota(tl(A4), [[0, 4], [4, 4]], 0, 0, ["a4"], 16)
+    iota(T.pm[:, 0:16], [[64, 4], [4, 4]], 0, 0, ["pmc", "pmd"], 16)
+    ts(T.lst[:, 48:64], T.pm[:, 0:16], c(TURN), None, AL.add, None, ["pmc", "tn"], ["turn"], 16)
     next_lists(0)
+    turn_z(0)
     for k in range(16):
-        cp(T.zr0[:, 2048 + k::16], T.zin[:, 1::2], ["zin"], ["zr01%d" % k], 64)
-        spread(T.zr0[:, k:2048:16], T.zin[:, 0::2], 128, ["zin"], ["zr00%d" % k])
+        cp(T.zr0[:, 2048 + k::16], T.zp[:, 128:256], ["zp"], ["zr01%d" % k], 64, "zo%d" % (k // 4))
+        spread(T.zr0[:, k:2048:16], T.zp[:, 0:128], 128, ["zp"], ["zr00%d" % k], "ze")
     for j in range(8):
         pb = ("pK1", "pK0", "pY", "pP")[j % 4]
         sl = slice(256 * j, 256 * j + 256)
         tv = T.MX[:, sl]
         xk = ["BX0", "BX1", "Bc", "CI", "X%d" % (j // 2)]
-        mm([(T[pb][:, 0:256], T.Bc[:], T.CI[:], True, False), (T[pb][:, 0:256], T.BX[:], T.X[:, sl], False, True)], xk, [pb], 512)
+        mm([(T[pb][:, 0:256], T.Bc[:], T.CI[:], True, False), (T[pb][:, 0:256], T.BX[:], T.X[:, sl], False, True)], xk, [pb], 512, "m%d" % j)
         act(tv, T[pb][:, 0:256], AF.Identity, [pb, "mlo", "BIn"], ["t1%d" % j], 256, bias=T.BI[:, 8 + j:9 + j], scale=c(MLO))
-        tt(T.P[:, sl], T[pb][:, 0:256], tv, AL.subtract, [pb, "t1%d" % j], ["P%d" % j], 256)
+        if j in PS:
+            pc = ("pD0", "pD1")[j % 2]
+            mm([(T[pc][:, 0:256], T.Bc[:], T.CI[:], True, False), (T[pc][:, 0:256], T.BX[:], T.X[:, sl], False, False),
+                (T[pc][:, 0:256], T.In[:], tv, False, True)], xk + ["In", "t1%d" % j], [pc], 768, "n%d" % j)
+            act(T.P[:, sl], T[pc][:, 0:256], AF.Copy, [pc], ["P%d" % j], 256)
+        else:
+            tt(T.P[:, sl], T[pb][:, 0:256], tv, AL.subtract, [pb, "t1%d" % j], ["P%d" % j], 256)
     Pk = ["Ps"] + ["P%d" % j for j in range(8)]
     for j in range(8):
         o, i = T.VT[:, V0 + 256 * j:V0 + 256 * j + 256], T.vwi[:, 256 * (j % 4):256 * (j % 4) + 256]
-        ts(o, i, 11 if j > 3 else 2047, None, AL.logical_shift_right if j > 3 else AL.bitwise_and, None, ["vw%d" % (j // 2 % 2)], ["V0%d" % j], 256)
+        ts(o, i, 11 if j > 3 else 2047, None, AL.logical_shift_right if j > 3 else AL.bitwise_and, None, ["vw%d" % (256 * (j % 4) >= VCUT)], ["V0%d" % j], 256)
 
     for t in range(TS):
         now[0] = t
@@ -321,21 +386,24 @@ def plan(g, core, T, topo, rank):
         shop = route(T, topo, srcrank, t)[1]
         narr = len(topo.engines(T.cores[srcrank] if shop is None else shop, core))
         far = FAR[0 if hop is None else 1]
+        now[1] = "@last" if last else "@direct" if hop is None else ""
 
         def send(kind, ap, r, t=t, to=dst if hop is None else hop, narr=narr, far=far):
             def fn():
                 sent[0] += write(g, T, topo, core, to, ap, kind, t)
                 return []
-            op("g", fn, r, ["m%s%d" % (kind, t)], far, n=0, hold=HOLD, nm="send" + kind)
+            once = ONCE if (kind, t) == ("F", 0) else 0
+            op("g", fn, r, ["m%s%d" % (kind, t)], far + 2 * once, n=0, hold=HOLD + once, nm="send" + kind)
             op("x", None, ["m%s%d" % (kind, t)], ["l%s%d" % (kind, t)], 0, sem="a%s%d" % (kind, t), n=narr, nm="send" + kind)
 
         if 1 <= t <= 4:
+            turn_z(t)
             for k in range(16):
-                spread(T["zr%d" % (t % 2)][:, k::16], T.zs[:, 256 * t:256 * t + 256], 256,
-                       ["z%d0" % t, "z%d1" % t], ["zr%d%d%d" % (t % 2, h, k) for h in (0, 1)], nm="zr%d" % (k // 4))
+                spread(T["zr%d" % (t % 2)][:, k::16], T.zp[:], 256,
+                       ["zp"], ["zr%d%d%d" % (t % 2, h, k) for h in (0, 1)], nm="zr%d" % (k // 4))
         vwin, vkeys = upto(VL[t - 1] + 264 if t else RING[1])
         unit = {}
-        for U, h, b0, nb, bank, step in UNITS:
+        for U, h, b0, nb, bank, gcalls, mcalls in UNITS:
             M, G = T["M%d" % h], T["G%d" % h]
             pK, pD, kK, kD = T["pK%d" % bank], T["pD%d" % bank], "pK%d" % bank, "pD%d" % bank
             n = 16 * nb
@@ -350,21 +418,27 @@ def plan(g, core, T, topo, rank):
                 first.append((pK[:, 0:n], T.I1[:], T.mvb[:, mvo:mvo + 2 * n:2], False, False))
             mm(first, ["I1", "TB", "mv%d%s" % (1 - t % 2, U)], [kK], 2 * max(64, n), "K0" + U)
             Gk, Mk = [], []
-            for q in range(b0, b0 + nb, step):
-                off = T.soff[:, 128 * h + 16 * q:128 * h + 16 * (q + step)]
-                e0 = 2048 * h + 256 * q
-                Gk.append("G%s%d" % (U, len(Gk)))
-                Mk.append("M%s%d" % (U, len(Mk)))
-                act(G[:, q, :], T.P[:, 0:2064].indirect(off), AF.Copy, Pk + ["soff%d" % h], Gk[-1:], 65 + 256 * step * GATH)
-                tt(M[:, q, :], T.X[:, 0:2064].indirect(off), zr[:, e0:e0 + 256 * step], AL.max,
-                   Xk + (Pk if t == 0 else []) + ["soff%d" % h] + ["zr%d%d%d" % (zb, h, k) for k in range(16)], Mk[-1:], 50 + 256 * step * GATH)
+            for kind, calls, keys in (("G", gcalls, Gk), ("M", mcalls, Mk)):
+                m = 1024 // calls
+                for q in range(calls):
+                    e = 256 * b0 + m * q
+                    off = T.soff[:, 128 * h + e // 16:128 * h + (e + m) // 16]
+                    keys.append("%s%s%d" % (kind, U, q))
+                    if kind == "G":
+                        act(G[:, e:e + m], T.P[:, 0:2064].indirect(off), AF.Copy, Pk + ["soff%d" % h], keys[-1:], 65 + m * GATH)
+                    else:
+                        tt(M[:, e:e + m], T.X[:, 0:2064].indirect(off), zr[:, 2048 * h + e:2048 * h + e + m], AL.max,
+                           Xk + ["soff%d" % h] + ["zr%d%d%d" % (zb, h, k) for k in range(16)], keys[-1:], 50 + m * GATH)
 
-            def lanes(o, Z, src, first, h=h, b0=b0, nb=nb):
-                return [(o, Z[:, 15 - a:143 - a], src[:, b0:b0 + nb, 16 * a:16 * a + 16], first and a == 0, first and a == 15) for a in range(16)]
+            def lanes(o, Z, src, first, some=range(16), b0=b0):
+                return [(o, Z[:, 15 - a:143 - a], src[:, 256 * b0 + 64 * a:256 * b0 + 64 * a + 64], first and a == 0, first and a == 15) for a in some]
             pc = 16 * max(64, n)
-            mm(lanes(pK[:, 0:n], T.ZM, M, False), ["ZM"] + Mk, [kK], pc, "ZM" + U)
-            mm(lanes(pD[:, 0:n], T.ZD, G, True), ["ZD"] + Gk, [kD], pc, "ZD" + U)
-            mm(lanes(pK[:, 0:n], T.ZR, G, False), ["ZR"] + Gk, [kK], pc, "ZR" + U)
+            for j in (0, 1):
+                some = range(8 * j, 8 * j + 8)
+                gk, mk = Gk[:(len(Gk) * (j + 1) + 1) // 2], Mk[:(len(Mk) * (j + 1) + 1) // 2]
+                mm(lanes(pK[:, 0:n], T.ZM, M, False, some), ["ZM"] + mk, [kK], pc // 2, "ZM%s%d" % (U, j))
+                mm(lanes(pD[:, 0:n], T.ZD, G, True, some), ["ZD"] + gk, [kD], pc // 2, "ZD%s%d" % (U, j))
+                mm(lanes(pK[:, 0:n], T.ZR, G, False, some), ["ZR"] + gk, [kK], pc // 2, "ZR%s%d" % (U, j))
             n0, n1 = 32 * B0, 32 * B0 + 2 * n
             mv, mvk = T.mvb[:, mvn:mvn + 2 * n:2], "mv%d%s" % (t % 2, U)
             tt(mv, pD[:, 0:n], thb[:, 0:n], AL.is_gt, [kD, thk], [mvk], n, "mv" + U)
@@ -398,8 +472,10 @@ def plan(g, core, T, topo, rank):
             tt(T.mvb[:, lo + 29:lo + 512:32], T.nn[:, 31::32], tl(HF), AL.min, ["hf"] + ["nn" + u for u in allu], ["lo%d" % (1 - t % 2)], 32, "lo")
             op("s", lambda: [S.activation(tl(SG), T.nn[:, 31::32], AF.Sign, bias=c(NHF), accum_out=c(CNT))], ["nhf"] + ["nn" + u for u in allu], ["cnt"], 90)
             pA = T.pU[:, 256:257]
-            mm([(T.pU[:, 260:261], T.hf[:, 128:256], c(CNT), True, True), (pA, T.hf[:, 0:128], c(CNT), True, False), cm(pA, "15", 1), cm(pA, "32m", 1),
-                cm(pA, "-32m", 1), (pA, T.hf[:, 128:256], c(CNT), False, True)], ["hf0", "hf1", "cnt", "one", "cl15", "cl32m", "cl-32m"], ["pU"], 960, "A")
+            cb = T.tb[:, 16 * BASE + 8:16 * BASE + 9]
+            act(cb, c(CNT), AF.Copy, ["cnt"], ["cb"], 1)
+            mm([(T.pU[:, 260:261], T.hf[:, 128:256], cb, True, True), (pA, T.hf[:, 0:128], cb, True, False), cm(pA, "15", 1), cm(pA, "32m", 1),
+                cm(pA, "-32m", 1), (pA, T.hf[:, 128:256], cb, False, True)], ["hf0", "hf1", "cb", "one", "cl15", "cl32m", "cl-32m"], ["pU"], 384, "A")
             act(c(AQ), pA, AF.Identity, ["pU", "ab"], ["am"], 1, bias=c(AB + t + 1))
             act(c(C32 + t + 1), T.pU[:, 260:261], AF.Identity, ["pU", "b37"], ["c32%d" % (t + 1)], 1, bias=c(B37), scale=32.0, nm="c32")
             act(T.thT[:], T.th0[:], AF.Identity, ["th0", "am"], ["thT"], 128, bias=c(AQ))
@@ -410,7 +486,7 @@ def plan(g, core, T, topo, rank):
             zo, zn_ = T.zs[:, 256 * t + 128 * h:256 * t + 128 * h + 128], T.zs[:, 256 * (t + 1) + 128 * h:256 * (t + 1) + 128 * h + 128]
             zk = "z%d%d" % (t + 1, h)
             mm([cm(T.pY[:, 0:256], "q", 256, True), (T.pY[:, 0:128], T.In[:], zo, False, False)], ["one", "clq", "In", "z%d%d" % (t, h)], ["pY"], 384, "Y0" + H)
-            p0 = 0
+            p0, cuts = 0, []
             ND = len(DCH[h])
             for q, (n, who) in enumerate(DCH[h]):
                 dq = D[:, p0:p0 + n]
@@ -424,6 +500,7 @@ def plan(g, core, T, topo, rank):
                 scan(T.MX[:, e], T.mk0[:, 0:n], dq, AL.mult, AL.max, ["mk0", "D%d%d" % (h, q)], ["MX%d%d" % (h, q)], n // 2)
                 scan(T.MN[:, e], T.mkB[:, 0:n], dq, AL.add, AL.min, ["mkB", "D%d%d" % (h, q)], ["MN%d%d" % (h, q)], n // 2)
                 p0 += n
+                cuts.append(p0)
             if h:
                 Fi, fk = T.fs[:, 136 * t:136 * t + 128], "fs%d" % t
             elif not last:
@@ -437,11 +514,12 @@ def plan(g, core, T, topo, rank):
                     send("F", T.fs[:, 136 * t + 128:136 * t + 136], ["fb%d" % t])
                 else:
                     send("F", T.fs[:, 136 * t:136 * t + 136], [fk, "fb%d" % t])
-            ends = slice(2048 * h + 15, 2048 * h + 2048, 16)
-            for x in ("MX", "MN"):
-                mm([(T.pY[:, 0:128], T.Ih[:], T[x][:, ends], False, False), (T.pY[:, 128:256], T.Ih[:], T[x][:, ends], False, False)]
-                   + ([cm(T.pY[:, 0:256], "m", 256, False, True)] if x == "MN" else []),
-                   ["Ih", "one", "clm"] + ["%s%d%d" % (x, h, q) for q in range(ND)], ["pY"], 512 if x == "MN" else 256, "Y" + x[1] + H)
+            for j in (0, 1):
+                ends = slice(2048 * h + 1024 * j + 15, 2048 * h + 1024 * j + 1024, 16)
+                outs = (T.pY[:, 64 * j:64 * j + 64], T.pY[:, 128 + 64 * j:192 + 64 * j])
+                qs = [q for q in range(ND) if (cuts[q] - 1) // 1024 == j]
+                mm([(o, T.Ih[:], T[x][:, ends], False, False) for x in ("MX", "MN") for o in outs] + [cm(outs[0], "m", 64), cm(outs[1], "m", 64, False, j == 1)],
+                   ["Ih", "one", "clm"] + ["%s%d%d" % (x, h, q) for x in ("MX", "MN") for q in qs], ["pY"], 384, "Y" + "XN"[j] + H)
             yo, yk = (T.ysn[:, 136 * t:136 * t + 128], "ya%d" % t) if h else (T.W[:, 264 * t:264 * t + 128], "W%d" % t)
             act(zn_, T.pY[:, 0:128], AF.Abs, ["pY", "nm1"], [zk], 128, bias=c(NM1), nm="z" + H)
             act(yo, T.pY[:, 128:256], AF.Identity, ["pY", "nm1"], [yk], 128, bias=c(NM1), nm="y" + H)
@@ -456,6 +534,16 @@ def plan(g, core, T, topo, rank):
                 ts(T.tf[:, 32:40], pw, 8 * M1, 8 * M1, AL.add, AL.subtract, ["pW"], ["r8"], 8)
                 tt(T.ysn[:, 136 * t + 128:136 * t + 136], pw, T.tf[:, 32:40], AL.subtract, ["pW", "r8"], ["yb%d" % t], 8, "yb")
                 send("Y", T.ysn[:, 136 * t:136 * t + 136], ["ya%d" % t, "yb%d" % t])
+            elif WV0[0]:
+                mm([cm(pw, "-3", 8, True)], ["one", "cl-3"], ["pW"], 64, "W00")
+                mm(wsum(T.ZW, True), ["ZW", zk], ["pW"], 1024, "W0")
+                pv = T.pK1[:, 0:8]
+                mm([cm(pv, "-3", 8, True), (pv, T.I1[:], tl(NH, 0), False, False), (pv, T.I1[:], tl(BASE, 0), False, False)],
+                   ["one", "cl-3", "I1", "nh0", "base0"], ["pK1"], 192, "ce")
+                mm([(pv,) + x[1:] for x in wsum(T.ZW, True)], ["ZW", zk], ["pK1"], 1024, "off0")
+                ts(T.tf[:, 32:40], pw, 8 * M1, 8 * M1, AL.add, AL.subtract, ["pW"], ["r8"], 8, "r80")
+                tt(T.tf[:, 40:48], pv, T.tf[:, 32:40], AL.subtract, ["pK1", "r8"], ["u30"], 8)
+                ts(T.lst[:, 16:24], T.tf[:, 40:48], c(L16), 3.5, AL.add, AL.add, ["u30", "l16"], ["wo0"], 8)
             else:
                 mm([cm(pw, "3", 8, True)], ["one", "cl3"], ["pW"], 64, "W00")
                 mm(wsum(T.ZN, False) + [cm(pw, "8m", 8), cm(pw, "-8m", 8), (pw, T.I1[:], tl(NH, 0), False, False), (pw, T.I1[:], tl(BASE, 0), False, False)]
@@ -465,9 +553,9 @@ def plan(g, core, T, topo, rank):
             mm([cm(pu, "u0", 128, True), (pu, T.BN[:], zn_, False, False), cm(pu, "um", 128), cm(pu, "-um", 128), cm(pu, "32", 128),
                 (pu, T.BW[:], zn_, False, True)], ["one", "clu0", "clum", "cl-um", "cl32", "BW", "BN", zk], ["pU"], 768, "U" + H)
             tt(T.pr[:, hs], pu, Fi, AL.mult, ["pU", fk], ["pr" + H], 128)
-            ts(T.qi[:, hs], T.pr[:, hs], c(C32 + t), None, AL.add, None, ["pr" + H, "c32%d" % t], ["qi" + H], 128)
-            s1 = RING[(t + 1) % 3] + 128 * h
-            ts(T.VT[:, s1:s1 + 128], T.qi[:, hs], 5, 2047, AL.arith_shift_right, AL.bitwise_and, ["qi" + H], ["S%d%d" % ((t + 1) % 3, h)], 128, "S" + H)
+        ts(T.qi[:], T.pr[:], c(C32 + t), None, AL.add, None, ["pr0", "pr1", "c32%d" % t], ["qi0"], 256)
+        s1 = RING[(t + 1) % 3]
+        ts(T.VT[:, s1:s1 + 256], T.qi[:], 5, 2047, AL.arith_shift_right, AL.bitwise_and, ["qi0"], ["S%d%d" % ((t + 1) % 3, h) for h in (0, 1)], 256, "S0")
         for h in WORD[0 if hop is None else 1]:
             H = str(h)
             cs = slice(128 * h, 128 * h + 128)
@@ -500,9 +588,9 @@ def plan(g, core, T, topo, rank):
         win, keys = upto(RING[2] + 256)
         cp(T.yso[:, h::2], win.indirect(T.lst[:, 32 + 8 * h:40 + 8 * h]), keys + ["sl"], ["yso%d" % h], 50 + 128 * GATH)
         act(T.yzo[:, h::2], T.zs[:, 256 * TS + 128 * h:256 * TS + 128 * h + 128], AF.Copy, ["z%d%d" % (TS, h)], ["yzo%d" % h], 128)
-    dma("y", "ox", T.yx[:], T.X[:, 0:2048], Xk, [], 4500)
-    dma("s", "oz", T.yz[:], T.yzo[:], ["yzo0", "yzo1"], [], 2200)
-    dma("s", "os_", T.ys[:], T.yso[:], ["yso0", "yso1"], [], 2400)
+    dma("y", "ox", T.yx[:], T.X[:, 0:2048], Xk, [], FIX + 8 * (ROW + 4096 / RATE))
+    dma("s", "oz", T.yz[:], T.yzo[:], ["yzo0", "yzo1"], [], FIX + 8 * (ROW + 512 / RATE))
+    dma("s", "os_", T.ys[:], T.yso[:], ["yso0", "yso1"], [], FIX + 8 * (2 * ROW + 5120 / RATE) - 600)
     return ops, sent
 
 
@@ -529,22 +617,32 @@ def depend(ops):
     return deps
 
 
+def places():
+    place = {}
+    for p, name in enumerate(ORDER):
+        place[name.rstrip("+-")] = p / len(ORDER) + name.count("+") - name.count("-")
+    at = -1.0
+    for name in SETUP:
+        if name[0] == "@":
+            at = place[name[1:]] - 0.5 / len(ORDER)
+        else:
+            at += 1e-5
+            place[name] = at
+    for kind, moves in (("@last", LAST), ("@direct", DIRECT)):
+        for before, names in moves:
+            for p, name in enumerate(names.split()):
+                place[name + kind] = place[before] - 0.4 / len(ORDER) + p * 1e-5
+    return place
+
+
 def order(ops, deps, place=None):
     n = len(ops)
-    if place is None:
-        place = {}
-        for p, name in enumerate(ORDER):
-            place[name.rstrip("+-")] = p / len(ORDER) + name.count("+") - name.count("-")
+    place = place or places()
     succ = [[] for _ in range(n)]
     for i in range(n):
         for d in deps[i]:
             succ[d].append(i)
-    key = [0.0] * n
-    for i in range(n - 1, -1, -1):
-        if ops[i][8] >= 0:
-            key[i] = ops[i][8] + place.get(ops[i][9], 1.9)
-        else:
-            key[i] = min([key[s] for s in succ[i]] + [9.0]) - (ops[i][4] + LAT) / 20000 - (ops[i][9] in FIRST)
+    key = [max(o[8], 0) + place.get(o[9] + o[10], place[o[9]]) for o in ops]
     left = [len(d) for d in deps]
     ready = [i for i in range(n) if not left[i]]
     line = []
@@ -556,37 +654,7 @@ def order(ops, deps, place=None):
             left[s] -= 1
             if not left[s]:
                 ready.append(s)
-    queue = {}
-    for i in line:
-        if ops[i][8] >= 0:
-            queue.setdefault(ops[i][0], []).append(i)
-    rest = [i for i in line if ops[i][8] < 0]
-    fin, free, out = {}, {}, []
-
-    def start(i):
-        if any(d not in fin for d in deps[i]):
-            return None
-        e = ops[i][0]
-        return max([free.get(e, 0.0)] + [fin[d] + (0.0 if e == "p" and ops[d][0] == "p" else LAT) for d in deps[i]])
-    while rest:
-        pick = []
-        for e in "vspgyx":
-            head = start(queue[e][0]) if queue.get(e) else None
-            mine = [(s, i) for s, i in ((start(i), i) for i in rest if ops[i][0] == e) if s is not None]
-            if mine:
-                t0 = min(mine)[0]
-                s, i = [x for x in mine if x[0] <= t0 + EARLY[0]][0]
-                if head is None or s + ops[i][7] <= head + EARLY[1] or key[i] < key[queue[e][0]] and s <= head:
-                    pick.append((s, i))
-                    continue
-            if head is not None:
-                pick.append((head, queue[e][0]))
-        s, i = min(pick)
-        (rest if ops[i][8] < 0 else queue[ops[i][0]]).remove(i)
-        out.append(i)
-        fin[i] = s + ops[i][4]
-        free[ops[i][0]] = s + ops[i][7] if ops[i][0] != "x" else 0.0
-    return out + [i for i in line if i not in fin]
+    return line
 
 
 CACHE = {}

from concourse.mybir import AluOpType, ActivationFunctionType

AL = AluOpType
AF = ActivationFunctionType
TS = 6
XW = 4352
RING, V0, VL, VW = (16, 2320, 2848), 272, (2576, 3104, 3376, 3648, 3920), 4192
SPARE = 2304.0
M1 = 12582912.0
UNITS = [("a", 1, 0, 4, 1, 2, 1), ("b", 1, 4, 4, 0, 2, 1), ("c", 0, 0, 4, 1, 2, 2), ("d", 0, 4, 4, 0, 2, 2)]
DCH = {0: [(512, "s"), (512, "s"), (256, "v"), (256, "s"), (256, "s"), (256, "s")], 1: [(512, "s")] * 4}
PSCAT = ["s"]
WORD = [(1, 0), (0, 1)]
WV0 = [True]
GV = []
VCUT = 512
PS = [6, 7]
SETUP = """
s.wai s.zin s.sci s.thi s.wti y.X0 y.X1 y.X2 y.X3 y.vw0 y.vw1
v.one g.ti0 g.BI g.pmc g.CI v.ti1 v.ti3 v.pf v.ti2 v.lf g.KI g.np0 g.HI g.a4 g.VTd g.mvc g.GI v.q4 v.c16g v.c15 v.tn v.p15 v.dq v.Z8 v.turn
v.l8 v.dkf v.lp v.c4 v.wab v.I1 v.ta v.c44 v.Bc v.tbc v.ZP v.BI v.mlo s.Xs s.cl-3 s.mkN s.Ps s.ab7 s.mkC s.gf s.na s.CV s.c4g v.BX1 s.hf1
s.In s.wd s.wr s.z00 s.z01 s.spc s.TB s.zp g.ze s.cl-um v.ZM v.BX0 p.pW v.snn v.wtf v.zo1 v.zo3 v.zo2 v.zo0 v.S01 v.S00 s.BIn p.SL p.m0
p.wt p.m1 p.m2 p.m3 s.ZR s.nhf s.mvc s.nm1 s.cl15 s.sptr s.cl32m s.t10 s.thf s.ZD s.thT s.t11 s.wf v.sl v.P0 v.Bf v.soff1 s.clm v.P1
s.t12 s.t13 s.Ih s.l16 v.P2 v.soff0 v.P3 p.m4 s.t14 v.wv v.P4 p.m5 s.t15 v.P5 p.m6 p.m7 g.mk0 g.mkB p.pU s.ab6 s.ZV s.Is s.BW s.t16
g.base1 s.t17 s.hf0 p.n6 s.clq s.WB0 s.c320 p.n7 @zr1 v.V04 v.V00 @Ga0 v.V05 s.P6 s.P7 s.th0 @Ga1 v.V07 @Gb0 s.ZW @zr2 s.wn
@Gc1 s.BN s.mk0 @nna s.mkB v.V01 @nfa v.V06 @ZVa v.V03 @foa v.V02 @zr3 g.np1 g.BJ g.BJ0 g.BS g.ab g.base0 g.Xt0 @K0d v.base1
@s2b s.BJ s.cl-32m @fuc v.b37 @yb v.cl64m @D00 s.cl32 @nnd g.Xt1 g.Xt2 g.Xt3 g.Xt4 g.np2 g.Vp0 g.Vp1 g.Vp2 g.Vp3 @cb s.clum @am s.clu0
@c32 s.cl-8m @hf s.WA @U1 s.cl3 @y0 s.WAj s.BS @U0 s.cl-64m @Pb0 s.WB1 @pr0 s.ZN @X0 s.cl8m @wo1 v.BJ
""".split()
LAST = [("W0", "U0"), ("r80", "sptr pr0 sl qi0 S0"), ("off0", "yso1"), ("y0", "yso0"), ("thT", "yzo1 yzo0 doz"), ("off1", "dos_")]
DIRECT = [("sptr", "off1"), ("W0", "wo1"), ("off0", "dd1"), ("y0", "Pa1"), ("U0", "ad1 X1"), ("thT", "Pb1"), ("Pb0", "rb1 P1")]
ORDER = """
Ma0 doz+ yso1++ yso0++ dos_++ dox++ Pa1+ Pb1+ P0+ Mb0 zr1 K0b rb1+ P1+ ZMa0 Ga0 ZRa0 ZMa1 ZDa0 Ga1 ZDa1 mva ZRa1 Kma
Gb0 zr2 Gb1 Gc0 S0+ Gc1 nna pma nfa Mc0 ZVa Vfa s2a ZDb0 ZDb1 mvb ZMb0 ZRb0 ZMb1 ZRb1 Kmb ZVb foa nnb fua D10 zr3 Mc1 pmb D11 nfb Vfb
K0d W01 s2b nh1 MN10 fob MX10 fub MN11 D12 D13 Gd0 ZDc0 fb F1 Md0 sendF ZDc1 mvc MX11 K0c ZMc0 ZRc0 ZMc1 MN12 nnc ZRc1 ZMd0 Kmc pmc
YX1 ZVc MX13 nfc MN13 MX12 Vfc s2c foc fuc ZRd0 Gd1 YN1 ZDd0 ZDd1 Md1 z1 W1 r8 mvd yb ZMd1 ZRd1 Kmd D00 y1 D01 sendY
nnd cnt MN00 pmd MX00 nfd ZVd Vfd MN01 s2d Y00 fod fud W00 MX01 cb A D02 am nb snn MN02 MX02 c32 D04 MX04 MN04 D05 MN05 MX05
D03 MX03 MN03 nh0 hf U1 SL sl YX0 YN0 z0 lo soff1 sp2 ce F0 pr1 sptr W0 r80 off0 u30 zp- y0 U0 thT Pa0 wo0 ad0 dd0 Pb0 rb0 Y01-
pr0 K0a- zr0- X0 off1 wo1 ad1 dd1 qi0 X1 yzo1 yzo0
""".split()

bf, f32, i32, u16 = "bfloat16", "float32", "int32", "uint16"
SCRATCH = {
    "X": ("sbuf", [128, XW], bf), "P": ("sbuf", [128, XW], f32), "WA": ("sbuf", [128, 384], bf), "WB": ("sbuf", [128, 384], bf),
    "rb": ("sbuf", [128, 256], f32), "VT": ("sbuf", [128, VW], i32),
    "vwi": ("sbuf", [128, 1024], i32), "sci": ("sbuf", [128, 256], i32), "zin": ("sbuf", [128, 256], bf),
    "wti": ("sbuf", [128, 256], i32), "wtf": ("sbuf", [128, 256], f32), "wai": ("sbuf", [128, 256], i32), "wab": ("sbuf", [128, 256], bf),
    "zs": ("sbuf", [128, 7 * 256], bf), "zr0": ("sbuf", [128, 4096], bf), "zr1": ("sbuf", [128, 4096], bf),
    "M0": ("sbuf", [128, 2048], bf), "M1": ("sbuf", [128, 2048], bf), "G0": ("sbuf", [128, 2048], bf), "G1": ("sbuf", [128, 2048], bf),
    "zp": ("sbuf", [128, 256], bf), "ZP": ("sbuf", [128, 528], bf),
    "D0": ("sbuf", [128, 2048], bf), "D1": ("sbuf", [128, 2048], bf),
    "MX": ("sbuf", [128, 4096], bf), "MN": ("sbuf", [128, 4096], bf),
    "mk0": ("sbuf", [128, 1024], bf), "mkB": ("sbuf", [128, 1024], bf), "mkN": ("sbuf", [128, 128], bf),
    "mkC": ("sbuf", [128, 256], bf), "CV": ("sbuf", [128, 256], bf),
    "mvb": ("sbuf", [128, 1024], bf), "nn": ("sbuf", [128, 512], bf), "s2": ("sbuf", [128, 512], f32),
    "soff": ("sbuf", [128, 256], u16), "fu": ("sbuf", [128, 256], u16), "lst": ("sbuf", [128, 64], u16),
    "fs": ("sbuf", [128, 6 * 136], i32), "fe": ("sbuf", [128, 128], i32), "fl5": ("sbuf", [128, 8], i32),
    "ysn": ("sbuf", [128, 6 * 136], bf), "W": ("sbuf", [128, 6 * 264], bf),
    "pm": ("sbuf", [128, 256], f32), "pr": ("sbuf", [128, 256], f32), "qi": ("sbuf", [128, 256], i32),
    "dd": ("sbuf", [128, 256], bf), "ad": ("sbuf", [128, 256], bf),
    "tf": ("sbuf", [128, 64], f32), "tb": ("sbuf", [128, 192], bf), "ti": ("sbuf", [128, 16], i32),
    "col": ("sbuf", [128, 64], f32), "BI": ("sbuf", [128, 16], f32), "BJ": ("sbuf", [128, 16], f32),
    "th0": ("sbuf", [128, 128], f32), "thT": ("sbuf", [128, 128], f32), "dkf": ("sbuf", [128, 128], f32), "Bf": ("sbuf", [128, 128], f32),
    "hf": ("sbuf", [128, 256], bf),
    "CI": ("sbuf", [128, 256], bf), "KI": ("sbuf", [128, 128], bf), "GI": ("sbuf", [128, 128], bf), "HI": ("sbuf", [128, 128], bf),
    "ZM": ("sbuf", [128, 144], bf), "ZR": ("sbuf", [128, 144], bf), "ZD": ("sbuf", [128, 144], bf), "ZV": ("sbuf", [128, 144], bf),
    "ZW": ("sbuf", [128, 144], bf), "ZN": ("sbuf", [128, 144], bf), "Z8": ("sbuf", [128, 144], bf),
    "I1": ("sbuf", [128, 128], bf), "Ih": ("sbuf", [128, 128], bf), "In": ("sbuf", [128, 128], bf), "Is": ("sbuf", [128, 128], bf),
    "BW": ("sbuf", [128, 128], bf), "BN": ("sbuf", [128, 128], bf), "BX": ("sbuf", [128, 128], bf), "Bc": ("sbuf", [128, 128], bf),
    "one": ("sbuf", [128, 512], bf), "TB": ("sbuf", [128, 128], bf), "cl": ("sbuf", [128, 16 * 128], bf),
    "yso": ("sbuf", [128, 256], f32), "yzo": ("sbuf", [128, 256], bf),
    "pK0": ("psum", [128, 512], f32), "pK1": ("psum", [128, 512], f32), "pD0": ("psum", [128, 512], f32), "pD1": ("psum", [128, 512], f32),
    "pW": ("psum", [128, 512], f32), "pY": ("psum", [128, 512], f32), "pU": ("psum", [128, 512], f32), "pP": ("psum", [128, 512], f32),
}
BANKS = ("pK0", "pK1", "pD0", "pD1", "pW", "pY", "pU", "pP")
DMAS = ["x0", "x1", "x2", "x3", "vw0", "vw1", "scan", "z0", "wt", "th", "warm", "oz", "os_", "ox"]
SEMAPHORES = (["cv", "cs", "cp", "cg", "sent"] + ["d" + n for n in DMAS]
              + ["aF%d" % t for t in range(TS)] + ["aY%d" % t for t in range(TS)])
FIX, ROW, RATE, OV = 1900, 30, 14.0, {"v": 20, "s": 30}
CYC, PCYC, GATH, SCAT, LAT, HOLD, ONCE, FAR = 1.0, 0.52, 1.4, 3.5, 110, 1200, 2000, [4000, 6500]


def route(T, topo, r, t):
    src, dst = T.cores[r], T.cores[(r + 1 + t % 3) % len(T.cores)]
    if topo.may_write(src, dst):
        return dst, None
    c = [h for h in topo.cores_of(src) if T.rank_of(h) is None and topo.may_write(h, dst)]
    c.sort(key=lambda h: (topo.die(h) != topo.die(src), h))
    return dst, c[0]


def landing(T, kind, t):
    if kind == "Y":
        return T.W[:, 264 * t + 128:264 * t + 264]
    return T.VT[:, VL[t] + 128:VL[t] + 264] if t < TS - 1 else T.fl5[:, :]


def write(g, T, topo, src, dst, in_ap, kind, t):
    rid, pid = topo.addr(dst, src)
    g.remote_dma(landing(T, kind, t), in_ap, T.sem["a%s%d" % (kind, t)], T.sem.sent, pid, rid, topo.mask(src, dst))
    return len(topo.engines(src, dst))


def helper_program(g, core, T, topo):
    n = 0
    for t in range(TS):
        for r in range(len(T.cores)):
            dst, h = route(T, topo, r, t)
            if h != core:
                continue
            for kind in ("F", "Y"):
                g.wait_ge(T.sem["a%s%d" % (kind, t)], len(topo.engines(T.cores[r], core)))
                n += write(g, T, topo, core, dst, landing(T, kind, t), kind, t)
    if n:
        g.wait_ge(T.sem.sent, n)


def plan(g, core, T, topo, rank):
    V, S, PE = g.vector, g.scalar, g.tensor
    ops = []
    sent = [0]
    now = [-1, ""]

    def op(e, fn, r, w, cost, sem=None, n=1, hold=None, nm=None):
        nm = nm or (w[0] if w else sem)
        cost += OV.get(e, 0) if sem is None else 0
        ops.append((e, fn, list(r), list(w), float(cost), sem, n, float(cost if hold is None else hold), now[0], nm if now[0] >= 0 else e + "." + nm, now[1]))

    def ts(o, i, s1, s2, a, b, r, w, n, nm=None):
        if b is None:
            op("v", lambda: [V.tensor_scalar(o, i, s1, None, a)], r, w, max(64, n) * CYC, nm=nm)
        else:
            op("v", lambda: [V.tensor_scalar(o, i, s1, s2, a, b)], r, w, max(64, n) * CYC, nm=nm)

    def tt(o, x, y, a, r, w, n, nm=None):
        op("v", lambda: [V.tensor_tensor(o, x, y, a)], r, w, max(64, n) * CYC, nm=nm)

    def cp(o, i, r, w, n, nm=None):
        op("v", lambda: [V.tensor_copy(o, i)], r, w, max(64, n) * CYC, nm=nm)

    def ms(o, c, w, n):
        op("v", lambda: [V.memset(o, c)], [], w, max(64, n) * CYC)

    def scan(o, d0, d1, a, b, r, w, n):
        op("v", lambda: [V.tensor_tensor_scan(o, d0, d1, 0.0, a, b)], r, w, max(64, n) * CYC)

    def act(o, i, f, r, w, n, bias=0.0, scale=1.0, nm=None):
        op("s", lambda: [S.activation(o, i, f, bias=bias, scale=scale)], r, w, max(64, n) * CYC, nm=nm)

    def mm(lst, r, w, cols, nm=None):
        op("p", lambda: [PE.matmul(*a) for a in lst], r, w, cols * PCYC, n=len(lst), nm=nm)

    def iota(o, pat, base, cm, w, n, small=True):
        if small:
            op("g", lambda: [g.iota(o, pat, base, cm, allow_small_or_imprecise_dtypes=True)], [], w, 160 + 2 * n * CYC)
        else:
            op("g", lambda: [g.iota(o, pat, base, cm)], [], w, 160 + 2 * n * CYC)

    def spread(o, i, n, r, w, nm=None):
        op("g", lambda: [g.affine_select(o, i, [[0, n]], AL.is_ge, 0.0, 0, 0)], r, w, 200 + 2 * n * CYC, nm=nm)

    def dma(q, name, o, i, r, w, cost):
        e = g.sync if q == "y" else S
        op(q, lambda: [e.dma_start(o, i)], r, w, cost, sem="d" + name, n=16, hold=60)

    def c(j):
        return T.col[:, j:j + 1]
    PF, LF, GF, C15, C16G, C4G, C4, WF, WN, THF, WR, MLO, WD, WV, TA, TBc, B37, L16, P15, CNT, AQ, NM1, SPC, NHF, LP, NA, L8, Q4, C44, TURN = range(30)
    C32, AB = 32, 40

    def tl(j, h=None):
        return T.tb[:, 16 * j:16 * j + 16] if h is None else T.tb[:, 16 * j + 8 * h:16 * j + 8 * h + 8]
    NP0, BASE, SNN, SPTR, NH, SP2, SG, NB, HF, A4 = 0, 3, 4, 5, 6, 7, 8, 9, 10, 11

    consts = {"q": -0.25, "m": M1, "-3": -3.5, "3": 3.5, "8m": 8 * M1, "-8m": -8 * M1, "um": 2048 * M1, "-um": -2048 * M1,
              "32": 32.0, "15": 15.5, "32m": 32 * M1, "-32m": -32 * M1, "u0": -0.5, "64m": None, "-64m": None}
    names = sorted(consts)

    def cm(o, name, n, start=False, stop=False):
        j, k = names.index(name), 2 if name == "u0" else 1
        return (o, T.cl[0:k, 128 * j:128 * j + 128], T.one[0:k, 0:n], start, stop)

    busy = [FIX]

    landed = {None: 0.0}

    def load(q, name, o, i, w, rows, size, after=None):
        busy[0] = max(busy[0], landed[after] + FIX) + rows / 16 * (ROW + size / RATE)
        landed[w] = busy[0]
        dma(q, name, o, i, [after] if after else [], [w], busy[0] - landed[after])
    load("s", "warm", T.wai[0:8, :], T.warm[:], "wai", 16, 512)
    load("s", "z0", T.zin[:], T.z0[:], "zin", 128, 512)
    load("s", "scan", T.sci[:], T.scan[:], "sci", 128, 1024)
    load("s", "th", T.wti[0:1, 128:256], T.th[:], "thi", 4, 128)
    load("s", "wt", T.wti[0:1, 0:128], T.wt[:], "wti", 4, 128)
    for j in range(4):
        load("y", "x%d" % j, T.X[:, 512 * j:512 * j + 512], T.reg[:, 512 * j:512 * j + 512], "X%d" % j, 128, 1024)
    load("y", "vw0", T.vwi[:, 0:VCUT], T.vw[:, 0:VCUT], "vw0", 128, 4 * VCUT, "X0")
    load("y", "vw1", T.vwi[:, VCUT:1024], T.vw[:, VCUT:1024], "vw1", 128, 4096 - 4 * VCUT, "X0")
    Xk = ["X0", "X1", "X2", "X3", "Xs"]
    Xt = ["Xt%d" % j for j in range(5)]
    iota(T.ti[:, 0:1], [[0, 1]], 0, 1, ["ti0"], 1, small=False)
    iota(T.KI[:], [[0, 8], [1, 16]], 0, 0, ["KI"], 128)
    iota(T.CI[:], [[1, 256]], 0, 0, ["CI"], 256)
    iota(T.HI[:], [[1, 32], [0, 4]], 0, 0, ["HI"], 128)
    for s in range(3):
        iota(tl(NP0 + s), [[16, 16]], RING[s], 0, ["np%d" % s], 16)
    iota(T.BI[:, 0:8], [[256, 8]], V0, 0, ["BI"], 8)
    iota(T.GI[:], [[1, 8], [0, 16]], 0, 0, ["GI"], 128)
    iota(tl(BASE, 0), [[256, 8]], 0, 0, ["base0"], 8)
    iota(T.tf[:, 0:8], [[256, 8]], 8, 0, ["base1"], 8)
    iota(T.col[:, AB:AB + 6], [[4096, 6]], 0, 0, ["ab"], 8)
    iota(T.BJ[:, 0:2], [[128, 2]], VL[0] - 128, 0, ["BJ0"], 2)
    iota(T.BJ[:, 2:10], [[VL[2] - VL[1], 4], [128, 2]], VL[1] - 128, 0, ["BJ"], 8)
    iota(T.tf[:, 16:26], [[1, 5], [0, 2]], 1, 0, ["BS"], 10)
    for s in range(4):
        iota(T.VT[:, VL[s] + 264:VL[s] + 272], [[0, 8]], 0, 0, ["Vp%d" % s], 8, small=False)
    iota(T.VT[:, 0:16], [[0, 16]], 2048, 0, ["VTd"], 16, small=False)
    for j in range(5):
        a, b = 2064 + 464 * j, min(XW, 2064 + 464 * j + 464)
        iota(T.X[:, a:b], [[0, b - a]], 0, 0, [Xt[j]], b - a)
    ms(T.one[:], 1.0, ["one"], 256)

    def fill(o, v, w, n, p=128):
        act(o, T.one[0:p, 0:n], AF.Copy, ["one"], w, n, scale=v)
    fill(T.X[:, 2048:2064], 0.0, ["Xs"], 16)
    fill(T.P[:, 2048:2064], 64.0, ["Ps"], 16)
    nd = max(n for h in DCH for n, _ in DCH[h])
    iota(T.mk0[:, 0:nd], [[0, nd]], 1, 0, ["mk0"], nd); fill(T.mk0[:, 0:nd:16], 0.0, ["mk0"], nd // 16)
    iota(T.mkB[:, 0:nd], [[0, nd]], 0, 0, ["mkB"], nd); fill(T.mkB[:, 0:nd:16], 256.0, ["mkB"], nd // 16)
    fill(T.mkN[:], 0.0, ["mkN"], 128); fill(T.mkN[:, ::16], -16.0, ["mkN"], 8)
    iota(T.mvb[:, 1::2], [[0, 512]], 0, 0, ["mvc"], 512)
    for j, v in ((1, 2.0), (29, -1.0), (31, -2.0)):
        fill(T.mvb[:, j::32], v, ["mvc", "lo0", "lo1"], 32)
    for nm in names:
        j = names.index(nm)
        if nm == "u0":
            fill(T.cl[0:2, 128 * j:128 * j + 128], -0.5, ["cl" + nm], 128, 2)
            fill(T.cl[0:1, 128 * j:128 * j + 128], 1024.0, ["cl" + nm], 128, 1)
        elif nm == "64m":
            ts(T.cl[0:1, 128 * j:128 * j + 128], T.KI[0:1, :], 3.0, 64 * M1, AL.is_le, AL.mult, ["KI"], ["cl" + nm], 64)
            k = names.index("-64m")
            act(T.cl[0:1, 128 * k:128 * k + 128], T.cl[0:1, 128 * j:128 * j + 128], AF.Copy, ["cl64m"], ["cl-64m"], 128, scale=-1.0)
        elif nm != "-64m":
            fill(T.cl[0:1, 128 * j:128 * j + 128], consts[nm], ["cl" + nm], 128, 1)
    act(T.hf[:, 0:128], T.one[:, 0:128], AF.Copy, ["one"], ["hf0"], 128, scale=-0.5)
    act(T.hf[:, 128:256], T.one[:, 0:128], AF.Copy, ["one"], ["hf1"], 128, scale=0.5)
    for j, v, k in ((NM1, -M1, "nm1"), (SPC, SPARE, "spc"), (NHF, -0.5, "nhf")):
        act(c(j), T.one[:, 0:1], AF.Copy, ["one"], [k], 1, scale=v)
    cp(c(PF), T.ti[:, 0:1], ["ti0"], ["pf"], 1)
    ts(T.ti[:, 1:2], T.ti[:, 0:1], 15, None, AL.bitwise_and, None, ["ti0"], ["ti1"], 1)
    cp(c(LF), T.ti[:, 1:2], ["ti1"], ["lf"], 1)
    tt(c(C16G), c(PF), c(LF), AL.subtract, ["pf", "lf"], ["c16g"], 1)
    ts(c(C15), c(C16G), 15.0, None, AL.add, None, ["c16g"], ["c15"], 1)
    ts(c(C4), c(C16G), 4.0, None, AL.add, None, ["c16g"], ["c4"], 1)
    ts(c(P15), c(PF), 16.0, 15.0, AL.mult, AL.add, ["pf"], ["p15"], 1)
    ts(c(B37), c(LF), 1184.0, 32768.0, AL.mult, AL.add, ["lf"], ["b37"], 1)
    for j, src, v, k in ((GF, C16G, 0.0625, "gf"), (C4G, C16G, 0.25, "c4g"), (C32, LF, 1184.0, "c320"), (L16, LF, 16.0, "l16"), (NA, LF, -2.0 ** -13, "na")):
        act(c(j), c(src), AF.Copy, ["c16g", "lf"], [k], 1, scale=v)
    cp(T.wtf[0:1, :], T.wti[0:1, :], ["wti", "thi"], ["wtf"], 256)
    fill(c(AB + 7), 2048.0, ["ab7"], 1)
    mm([(T.pU[:, 300 + j:301 + j], T.wtf[0:1, 128 * j:128 * j + 128], T.col[0:1, AB + 7:AB + 8], True, True) for j in (0, 1)], ["wtf", "ab7"], ["pU"], 512, "wt")
    act(c(THF), T.pU[:, 301:302], AF.Copy, ["pU"], ["thf"], 1)
    act(c(WF), T.pU[:, 300:301], AF.Copy, ["pU"], ["wf"], 1)
    act(c(WN), c(WF), AF.Copy, ["wf"], ["wn"], 1, scale=-1.0)
    fill(c(AB + 6), 4096.0 * 64, ["ab6"], 1)
    ts(T.dkf[:], T.KI[:], c(LF), None, AL.is_equal, None, ["KI", "lf"], ["dkf"], 128)
    ts(T.tf[:, 0:8], T.tf[:, 0:8], c(L16), None, AL.add, None, ["base1", "l16"], ["base1"], 8)

    def dk(k):
        return T.dkf[:, k:k + 1]
    tt(c(MLO), dk(1), dk(3), AL.add, ["dkf"], ["mlo"], 1)
    tt(c(LP), dk(1), dk(0), AL.subtract, ["dkf"], ["lp"], 1)
    act(c(WR), c(LP), AF.Copy, ["lp"], ["wr"], 1, scale=0.5)
    ts(c(TA), dk(2), dk(3), 2048.0, AL.subtract, AL.mult, ["dkf"], ["ta"], 1)
    act(c(WD), dk(6), AF.Identity, ["dkf", "ta"], ["wd"], 1, bias=c(TA), scale=2048.0 * 4096)
    ts(c(WV), dk(4), dk(5), 0.25, AL.add, AL.mult, ["dkf"], ["wv"], 1)
    ts(c(L8), c(LF), 3.0, 64.0, AL.is_le, AL.mult, ["lf"], ["l8"], 1)
    ts(c(TBc), dk(6), 64.0, c(L8), AL.mult, AL.add, ["dkf", "l8"], ["tbc"], 1)
    ts(T.BI[:, 0:8], T.BI[:, 0:8], dk(5), c(TBc), AL.mult, AL.add, ["BI", "dkf", "tbc"], ["BI"], 8)
    act(T.BI[:, 8:16], T.BI[:, 0:8], AF.Copy, ["BI"], ["BIn"], 8, scale=-1.0)
    act(T.BJ[:, 0:10], T.BJ[:, 0:10], AF.Identity, ["BJ", "BJ0", "dkf", "tbc"], ["BJ", "BJ0"], 10, bias=c(TBc), scale=dk(5))
    act(T.tf[:, 16:26], T.tf[:, 16:26], AF.Identity, ["BS", "dkf"], ["BS"], 10, scale=dk(6))
    tt(T.BJ[:, 0:10], T.BJ[:, 0:10], T.tf[:, 16:26], AL.add, ["BJ", "BS"], ["BJ"], 20)
    ts(T.ZM[:], T.CI[:, 0:144], c(C15), 2.0 ** -11, AL.is_equal, AL.mult, ["CI", "c15"], ["ZM"], 72)
    for nm, s2, r in (("ZR", WR, "wr"), ("ZD", WD, "wd"), ("ZV", WV, "wv"), ("ZW", WF, "wf"), ("ZN", WN, "wn")):
        act(T[nm][:], T.ZM[:], AF.Identity, ["ZM", r], [nm], 144, scale=c(s2))
    ts(T.Z8[0:8, :], T.CI[0:8, 0:144], T.col[0:8, P15:P15 + 1], None, AL.is_equal, None, ["CI", "p15"], ["Z8"], 72)
    ts(T.I1[:], T.CI[:, 0:128], c(PF), None, AL.is_equal, None, ["CI", "pf"], ["I1"], 64)
    for nm, s2 in (("Ih", 0.5), ("In", -1.0), ("Is", 2.0 ** -13)):
        act(T[nm][:], T.I1[:], AF.Copy, ["I1"], [nm], 128, scale=s2)
    ts(T.Bf[:], T.GI[:], c(GF), 2.0 ** -11, AL.is_equal, AL.mult, ["GI", "gf"], ["Bf"], 128)
    act(T.BW[:], T.Bf[:], AF.Identity, ["Bf", "wf"], ["BW"], 128, scale=c(WF))
    act(T.BN[:], T.Bf[:], AF.Identity, ["Bf", "wn"], ["BN"], 128, scale=c(WN))
    ts(T.BX[:, 0::2], T.HI[:, 0::2], c(C4G), None, AL.is_equal, None, ["HI", "c4g"], ["BX0"], 32)
    ts(T.BX[:, 1::2], T.HI[:, 1::2], c(C4G), -1.0, AL.is_equal, AL.mult, ["HI", "c4g"], ["BX1"], 32)
    ts(T.Bc[:], T.CI[:, 0:128], c(C4), dk(0), AL.is_equal, AL.mult, ["CI", "c4", "dkf"], ["Bc"], 64)
    fill(T.WA[:], 0.0, ["WA"], 384)
    WAk = []
    for m0, j, s2 in ((0, 0, 1.0), (0, 1, 1.0), (0, 2, -1.0), (0, 3, -1.0), (128, 2, 2.0), (128, 3, 2.0), (256, 2, -1.0), (256, 3, -1.0)):
        WAk.append("WA%d" % len(WAk))
        act(T.WA[:, m0 + j:m0 + 128:16], T.Bf[:, 0::16], AF.Copy, ["Bf", "WA"], WAk[-1:], 8, scale=2048 * s2, nm="WAj")
    fill(T.WB[:, 0::2], 0.0, ["WB0"], 192)
    act(T.WB[:, 1::2], T.WA[:, 1::2], AF.Copy, WAk, ["WB1"], 192, scale=-1.0)
    act(T.TB[:], T.KI[:], AF.Copy, ["KI"], ["TB"], 128, scale=-2.0 ** -16)
    nv = 32 * max(u[3] for u in UNITS)
    fill(T.CV[:, 1:nv:2], -1.0, ["CV"], nv // 2)
    fill(T.CV[:, 31:nv:32], 0.0, ["CV"], nv // 32)
    act(T.CV[:, 0:nv:2], T.one[:, 0:nv // 2], AF.Identity, ["one", "na"], ["CV"], nv // 2, scale=c(NA))
    fill(T.mkC[:, 0:nv], 1.0, ["mkC"], nv); fill(T.mkC[:, 0:nv:32], 0.0, ["mkC"], nv // 32)
    act(tl(SPTR), tl(NP0), AF.Copy, ["np0"], ["sptr"], 16)
    act(T.thT[:], T.dkf[:], AF.Identity, ["dkf", "thf"], ["thT"], 128, scale=c(THF))
    mm([(T.pU[:, 0:128], T.Bf[:], T.thT[:], True, True)], ["Bf", "thT"], ["pU"], 512)
    act(T.th0[:], T.pU[:, 0:128], AF.Identity, ["pU", "ab6"], ["th0"], 128, bias=c(AB + 6))
    for h in (0, 1):
        cp(T.VT[:, RING[0] + 128 * h:RING[0] + 128 * h + 128], T.sci[:, h::2], ["sci"], ["S0%d" % h], 128)
        act(T.zs[:, 128 * h:128 * h + 128], T.zin[:, h::2], AF.Copy, ["zin"], ["z0%d" % h], 128)
    cp(T.wab[0:8, :], T.wai[0:8, :], ["wai"], ["wab"], 256)
    mm([(T.pW[:, 8 * h:8 * h + 8], T.Z8[0:8, 15 - a:143 - a], T.wab[0:8, 2 * a + h::32], a == 0, a == 15)
        for h in (0, 1) for a in range(16)], ["Z8", "wab"], ["pW"], 32 * 64)
    tt(tl(SNN), T.pW[:, 0:16], tl(NP0), AL.mult, ["pW", "np0"], ["snn"], 16)
    parts = [(0, ["VTd"]), (V0, ["V0%d" % j for j in range(8)])] + [(RING[s], ["S%d0" % s, "S%d1" % s]) for s in range(3)]
    parts += [(VL[s], ["VL%d" % s, "lF%d" % s]) for s in range(5)] + [(VL[s] + 264, ["Vp%d" % s]) for s in range(4)]

    def upto(end):
        return T.VT[:, 0:end], [k for a, ks in parts if a < end for k in ks]

    def next_lists(t):
        win, keys = upto(RING[min(t, 2)] + 256)
        pk = "pP" if now[0] >= 0 else "pD0"
        ps = T[pk][:, 128:144]
        mm([(ps, T.I1[:], tl(A4), True, False)]
           + [(T[pk][:, 128 + j:144:4], T.ZP[:, 132 * j + 4 - b:132 * j + 132 - b], T.tb[:, 16 * SNN + b:16 * SNN + 16:4], False, j + b == 6)
              for j in range(4) for b in range(4)], ["I1", "a4", "snn"] + ["ZP%d" % j for j in range(4)], [pk], 17 * 64, "SL")
        ts(T.lst[:, 32:48], ps, c(Q4), None, AL.add, None, [pk, "q4"], ["sl"], 16)
        if now[0] >= 0:
            return cp(T.soff[:], win.indirect(T.lst[:, 32:48]), keys + ["sl"], ["soff1", "soff0"], 50 + 256 * GATH)
        for h in (1, 0):
            cp(T.soff[:, 128 * h:128 * h + 128], win.indirect(T.lst[:, 32 + 8 * h:40 + 8 * h]), keys + ["sl"], ["soff%d" % h], 50 + 128 * GATH)

    def turn_z(t):
        act(T.zp[:], T.zs[:, 256 * t:256 * t + 256].indirect(T.lst[:, 48:64]), AF.Copy, ["z%d0" % t, "z%d1" % t, "turn"], ["zp"], 65 + 256 * GATH)
    ts(T.ti[:, 2:3], T.ti[:, 0:1], 3, None, AL.bitwise_and, None, ["ti0"], ["ti2"], 1)
    ts(T.ti[:, 3:4], T.ti[:, 0:1], 2, 3, AL.arith_shift_right, AL.bitwise_and, ["ti0"], ["ti3"], 1)
    cp(c(Q4), T.ti[:, 3:4], ["ti3"], ["q4"], 1)
    ts(c(C44), T.ti[:, 2:3], 4.0, c(C4), AL.mult, AL.add, ["ti2", "c4"], ["c44"], 1)
    ts(c(TURN), T.ti[:, 2:3], 16.0, c(Q4), AL.mult, AL.add, ["ti2", "q4"], ["tn"], 1)
    ts(T.tf[:, 28:32], T.CI[:, 0:4], c(Q4), None, AL.is_equal, None, ["CI", "q4"], ["dq"], 4)
    for j in range(4):
        ts(T.ZP[:, 132 * j:132 * j + 132], T.CI[:, 0:132], c(C44), T.tf[:, 28 + j:29 + j], AL.is_equal, AL.mult, ["CI", "c44", "dq"], ["ZP%d" % j], 66, "ZP")
    iota(tl(A4), [[0, 4], [4, 4]], 0, 0, ["a4"], 16)
    iota(T.pm[:, 0:16], [[64, 4], [4, 4]], 0, 0, ["pmc", "pmd"], 16)
    ts(T.lst[:, 48:64], T.pm[:, 0:16], c(TURN), None, AL.add, None, ["pmc", "tn"], ["turn"], 16)
    next_lists(0)
    turn_z(0)
    for k in range(16):
        cp(T.zr0[:, 2048 + k::16], T.zp[:, 128:256], ["zp"], ["zr01%d" % k], 64, "zo%d" % (k // 4))
        spread(T.zr0[:, k:2048:16], T.zp[:, 0:128], 128, ["zp"], ["zr00%d" % k], "ze")
    for j in range(8):
        pb = ("pK1", "pK0", "pY", "pP")[j % 4]
        sl = slice(256 * j, 256 * j + 256)
        tv = T.MX[:, sl]
        xk = ["BX0", "BX1", "Bc", "CI", "X%d" % (j // 2)]
        mm([(T[pb][:, 0:256], T.Bc[:], T.CI[:], True, False), (T[pb][:, 0:256], T.BX[:], T.X[:, sl], False, True)], xk, [pb], 512, "m%d" % j)
        act(tv, T[pb][:, 0:256], AF.Identity, [pb, "mlo", "BIn"], ["t1%d" % j], 256, bias=T.BI[:, 8 + j:9 + j], scale=c(MLO))
        if j in PS:
            pc = ("pD0", "pD1")[j % 2]
            mm([(T[pc][:, 0:256], T.Bc[:], T.CI[:], True, False), (T[pc][:, 0:256], T.BX[:], T.X[:, sl], False, False),
                (T[pc][:, 0:256], T.In[:], tv, False, True)], xk + ["In", "t1%d" % j], [pc], 768, "n%d" % j)
            act(T.P[:, sl], T[pc][:, 0:256], AF.Copy, [pc], ["P%d" % j], 256)
        else:
            tt(T.P[:, sl], T[pb][:, 0:256], tv, AL.subtract, [pb, "t1%d" % j], ["P%d" % j], 256)
    Pk = ["Ps"] + ["P%d" % j for j in range(8)]
    for j in range(8):
        o, i = T.VT[:, V0 + 256 * j:V0 + 256 * j + 256], T.vwi[:, 256 * (j % 4):256 * (j % 4) + 256]
        ts(o, i, 11 if j > 3 else 2047, None, AL.logical_shift_right if j > 3 else AL.bitwise_and, None, ["vw%d" % (256 * (j % 4) >= VCUT)], ["V0%d" % j], 256)

    for t in range(TS):
        now[0] = t
        last = t == TS - 1
        zb = 0 if t < 2 or t % 2 else 1
        zr = T["zr%d" % zb]
        thk, thb = ("th0", T.th0) if t == 0 else ("thT", T.thT)
        dst, hop = route(T, topo, rank, t)
        srcrank = (rank - 1 - t % 3) % len(T.cores)
        shop = route(T, topo, srcrank, t)[1]
        narr = len(topo.engines(T.cores[srcrank] if shop is None else shop, core))
        far = FAR[0 if hop is None else 1]
        now[1] = "@last" if last else "@direct" if hop is None else ""

        def send(kind, ap, r, t=t, to=dst if hop is None else hop, narr=narr, far=far):
            def fn():
                sent[0] += write(g, T, topo, core, to, ap, kind, t)
                return []
            once = ONCE if (kind, t) == ("F", 0) else 0
            op("g", fn, r, ["m%s%d" % (kind, t)], far + 2 * once, n=0, hold=HOLD + once, nm="send" + kind)
            op("x", None, ["m%s%d" % (kind, t)], ["l%s%d" % (kind, t)], 0, sem="a%s%d" % (kind, t), n=narr, nm="send" + kind)

        if 1 <= t <= 4:
            turn_z(t)
            for k in range(16):
                spread(T["zr%d" % (t % 2)][:, k::16], T.zp[:], 256,
                       ["zp"], ["zr%d%d%d" % (t % 2, h, k) for h in (0, 1)], nm="zr%d" % (k // 4))
        vwin, vkeys = upto(VL[t - 1] + 264 if t else RING[1])
        unit = {}
        for U, h, b0, nb, bank, gcalls, mcalls in UNITS:
            M, G = T["M%d" % h], T["G%d" % h]
            pK, pD, kK, kD = T["pK%d" % bank], T["pD%d" % bank], "pK%d" % bank, "pD%d" % bank
            n = 16 * nb
            B0 = 8 * h + b0
            bs = slice(B0, B0 + nb)
            hs = slice(16 * B0, 16 * B0 + n)
            mvn, mvo = 512 * (t % 2) + 32 * B0, 512 * (1 - t % 2) + 32 * B0
            for b in range(b0, b0 + nb):
                unit[(h, b)] = U
            first = [(pK[:, 0:n], T.I1[:], T.TB[:, 0:n], True, False)]
            if t:
                first.append((pK[:, 0:n], T.I1[:], T.mvb[:, mvo:mvo + 2 * n:2], False, False))
            mm(first, ["I1", "TB", "mv%d%s" % (1 - t % 2, U)], [kK], 2 * max(64, n), "K0" + U)
            Gk, Mk = [], []
            for kind, calls, keys in (("G", gcalls, Gk), ("M", mcalls, Mk)):
                m = 1024 // calls
                for q in range(calls):
                    e = 256 * b0 + m * q
                    off = T.soff[:, 128 * h + e // 16:128 * h + (e + m) // 16]
                    keys.append("%s%s%d" % (kind, U, q))
                    if kind == "G":
                        act(G[:, e:e + m], T.P[:, 0:2064].indirect(off), AF.Copy, Pk + ["soff%d" % h], keys[-1:], 65 + m * GATH)
                    else:
                        tt(M[:, e:e + m], T.X[:, 0:2064].indirect(off), zr[:, 2048 * h + e:2048 * h + e + m], AL.max,
                           Xk + ["soff%d" % h] + ["zr%d%d%d" % (zb, h, k) for k in range(16)], keys[-1:], 50 + m * GATH)

            def lanes(o, Z, src, first, some=range(16), b0=b0):
                return [(o, Z[:, 15 - a:143 - a], src[:, 256 * b0 + 64 * a:256 * b0 + 64 * a + 64], first and a == 0, first and a == 15) for a in some]
            pc = 16 * max(64, n)
            for j in (0, 1):
                some = range(8 * j, 8 * j + 8)
                gk, mk = Gk[:(len(Gk) * (j + 1) + 1) // 2], Mk[:(len(Mk) * (j + 1) + 1) // 2]
                mm(lanes(pK[:, 0:n], T.ZM, M, False, some), ["ZM"] + mk, [kK], pc // 2, "ZM%s%d" % (U, j))
                mm(lanes(pD[:, 0:n], T.ZD, G, True, some), ["ZD"] + gk, [kD], pc // 2, "ZD%s%d" % (U, j))
                mm(lanes(pK[:, 0:n], T.ZR, G, False, some), ["ZR"] + gk, [kK], pc // 2, "ZR%s%d" % (U, j))
            n0, n1 = 32 * B0, 32 * B0 + 2 * n
            mv, mvk = T.mvb[:, mvn:mvn + 2 * n:2], "mv%d%s" % (t % 2, U)
            tt(mv, pD[:, 0:n], thb[:, 0:n], AL.is_gt, [kD, thk], [mvk], n, "mv" + U)
            mm([(pK[:, 0:n], T.I1[:], mv, False, True)], ["I1", mvk], [kK], max(64, n), "Km" + U)
            scan(T.nn[:, n0:n1], T.mkC[:, 0:2 * n], T.mvb[:, mvn:mvn + 2 * n], AL.mult, AL.add,
                 ["mkC", "mvc", "lo%d" % (t % 2), mvk], ["nn" + U, "nf" + U], n)
            pV, pR, pE = pD[:, 256:256 + 2 * n], pD[:, 256:256 + 2 * n:2], pD[:, 287:256 + 2 * n:32]
            mm([(pV, T.I1[:], T.CV[:, 0:2 * n], True, False), (pE, T.Is[:], T.tb[:, 16 * SNN + B0:16 * SNN + B0 + nb], False, False),
                (pE, T.I1[:], T.mvb[:, mvn + 29:mvn + 2 * n:32], False, False)] + lanes(pR, T.ZV, G, False),
               ["I1", "Is", "CV", "ZV", "snn", "lo%d" % (t % 2)] + Gk, [kD], pc + 128 + 2 * n, "ZV" + U)
            scan(T.pm[:, hs], T.mkN[:, 0:n], pK[:, 0:n], AL.add, AL.max, ["mkN", kK], ["pm" + U], n)
            tt(T.nn[:, n0:n1:2], pK[:, 0:n], T.pm[:, hs], AL.not_equal, [kK, "pm" + U], ["nf" + U], n)
            mm([(pE, T.In[:], T.nn[:, n0 + 31:n1:32], False, False), (pR, T.In[:], T.nn[:, n0:n1:2], False, True)],
               ["In", "nn" + U, "nf" + U], [kD], 64 + max(64, n), "Vf" + U)
            scan(T.s2[:, n0:n1], T.nn[:, n0:n1], pV, AL.min, AL.max, ["nn" + U, "nf" + U, kD], ["s2" + U], 2 * n)
            fo = T.lst[:, bs]
            ts(fo, T.s2[:, n0 + 31:n1:32], 8192.0, c(LF), AL.mult, AL.add, ["s2" + U, "lf"], ["fo" + U], 8)
            cp(T.fu[:, hs], vwin.indirect(fo), vkeys + ["fo" + U], ["fu" + U], 50 + n * GATH)
        allu = [u[0] for u in UNITS]
        for h in (1, 0):
            hu = sorted(set(unit[(h, b)] for b in range(8)))
            act(tl(NH, h), T.s2[:, 256 * h + 31:256 * h + 256:32], AF.Relu, ["spc"] + ["s2" + u for u in hu], ["nh%d" % h], 8, bias=c(SPC), scale=-SPARE * 512)
        act(tl(NB), T.s2[:, 31::32], AF.Relu, ["ab"] + ["s2" + u for u in allu], ["nb"], 16, bias=c(AB + 1), scale=-4096.0 * 512)
        tt(tl(SNN), tl(SPTR), tl(NB), AL.min, ["sptr", "nb"], ["snn"], 32)
        tt(tl(SP2), tl(NP0 + (t + 1) % 3), tl(NB), AL.subtract, ["np%d" % ((t + 1) % 3), "nb"], ["sp2"], 32)
        tt(tl(SPTR), tl(SNN), tl(SP2), AL.max, ["snn", "sp2"], ["sptr"], 32)
        if not last:
            next_lists(t)
            act(tl(HF), T.s2[:, 31::32], AF.Sign, ["s2" + u for u in allu], ["hf"], 16, scale=-1.0)
            lo = 512 * (1 - t % 2)
            tt(T.mvb[:, lo + 29:lo + 512:32], T.nn[:, 31::32], tl(HF), AL.min, ["hf"] + ["nn" + u for u in allu], ["lo%d" % (1 - t % 2)], 32, "lo")
            op("s", lambda: [S.activation(tl(SG), T.nn[:, 31::32], AF.Sign, bias=c(NHF), accum_out=c(CNT))], ["nhf"] + ["nn" + u for u in allu], ["cnt"], 90)
            pA = T.pU[:, 256:257]
            cb = T.tb[:, 16 * BASE + 8:16 * BASE + 9]
            act(cb, c(CNT), AF.Copy, ["cnt"], ["cb"], 1)
            mm([(T.pU[:, 260:261], T.hf[:, 128:256], cb, True, True), (pA, T.hf[:, 0:128], cb, True, False), cm(pA, "15", 1), cm(pA, "32m", 1),
                cm(pA, "-32m", 1), (pA, T.hf[:, 128:256], cb, False, True)], ["hf0", "hf1", "cb", "one", "cl15", "cl32m", "cl-32m"], ["pU"], 384, "A")
            act(c(AQ), pA, AF.Identity, ["pU", "ab"], ["am"], 1, bias=c(AB + t + 1))
            act(c(C32 + t + 1), T.pU[:, 260:261], AF.Identity, ["pU", "b37"], ["c32%d" % (t + 1)], 1, bias=c(B37), scale=32.0, nm="c32")
            act(T.thT[:], T.th0[:], AF.Identity, ["th0", "am"], ["thT"], 128, bias=c(AQ))
        for h in (1, 0):
            D, H = T["D%d" % h], str(h)
            hs = slice(128 * h, 128 * h + 128)
            hu = sorted(set(unit[(h, b)] for b in range(8)))
            zo, zn_ = T.zs[:, 256 * t + 128 * h:256 * t + 128 * h + 128], T.zs[:, 256 * (t + 1) + 128 * h:256 * (t + 1) + 128 * h + 128]
            zk = "z%d%d" % (t + 1, h)
            mm([cm(T.pY[:, 0:256], "q", 256, True), (T.pY[:, 0:128], T.In[:], zo, False, False)], ["one", "clq", "In", "z%d%d" % (t, h)], ["pY"], 384, "Y0" + H)
            p0, cuts = 0, []
            ND = len(DCH[h])
            for q, (n, who) in enumerate(DCH[h]):
                dq = D[:, p0:p0 + n]
                src = T.X[:, 0:2064].indirect(T.fu[:, 128 * h + p0 // 16:128 * h + (p0 + n) // 16])
                fuk = sorted(set("fu" + unit[(h, x)] for x in range(p0 // 256, (p0 + n - 1) // 256 + 1)))
                if who == "s":
                    act(dq, src, AF.Copy, Xk + fuk, ["D%d%d" % (h, q)], 65 + n * GATH)
                else:
                    cp(dq, src, Xk + fuk, ["D%d%d" % (h, q)], 50 + n * GATH)
                e = slice(2048 * h + p0, 2048 * h + p0 + n)
                scan(T.MX[:, e], T.mk0[:, 0:n], dq, AL.mult, AL.max, ["mk0", "D%d%d" % (h, q)], ["MX%d%d" % (h, q)], n // 2)
                scan(T.MN[:, e], T.mkB[:, 0:n], dq, AL.add, AL.min, ["mkB", "D%d%d" % (h, q)], ["MN%d%d" % (h, q)], n // 2)
                p0 += n
                cuts.append(p0)
            if h:
                Fi, fk = T.fs[:, 136 * t:136 * t + 128], "fs%d" % t
            elif not last:
                Fi, fk = T.VT[:, VL[t]:VL[t] + 128], "VL%d" % t
            else:
                Fi, fk = T.fe[:], "fe"
            cp(Fi, T.fu[:, hs], ["fu" + u for u in hu], [fk], 128, "F" + H)
            if h:
                tt(T.fs[:, 136 * t + 128:136 * t + 136], T.tf[:, 0:8], tl(NH, 1), AL.add, ["base1", "nh1"], ["fb%d" % t], 16, "fb")
                if last:
                    send("F", T.fs[:, 136 * t + 128:136 * t + 136], ["fb%d" % t])
                else:
                    send("F", T.fs[:, 136 * t:136 * t + 136], [fk, "fb%d" % t])
            for j in (0, 1):
                ends = slice(2048 * h + 1024 * j + 15, 2048 * h + 1024 * j + 1024, 16)
                outs = (T.pY[:, 64 * j:64 * j + 64], T.pY[:, 128 + 64 * j:192 + 64 * j])
                qs = [q for q in range(ND) if (cuts[q] - 1) // 1024 == j]
                mm([(o, T.Ih[:], T[x][:, ends], False, False) for x in ("MX", "MN") for o in outs] + [cm(outs[0], "m", 64), cm(outs[1], "m", 64, False, j == 1)],
                   ["Ih", "one", "clm"] + ["%s%d%d" % (x, h, q) for x in ("MX", "MN") for q in qs], ["pY"], 384, "Y" + "XN"[j] + H)
            yo, yk = (T.ysn[:, 136 * t:136 * t + 128], "ya%d" % t) if h else (T.W[:, 264 * t:264 * t + 128], "W%d" % t)
            act(zn_, T.pY[:, 0:128], AF.Abs, ["pY", "nm1"], [zk], 128, bias=c(NM1), nm="z" + H)
            act(yo, T.pY[:, 128:256], AF.Identity, ["pY", "nm1"], [yk], 128, bias=c(NM1), nm="y" + H)
            z0c = 256 * (t + 1) + 128 * h
            pw = T.pW[:, 0:8]

            def wsum(Z, stop, z0c=z0c, pw=pw):
                return [(pw, Z[:, 15 - a:143 - a], T.zs[:, z0c + a:z0c + 128:16], False, stop and a == 15) for a in range(16)]
            if h:
                mm([cm(pw, "-3", 8, True)], ["one", "cl-3"], ["pW"], 64, "W01")
                mm(wsum(T.ZW, True), ["ZW", zk], ["pW"], 1024, "W1")
                ts(T.tf[:, 32:40], pw, 8 * M1, 8 * M1, AL.add, AL.subtract, ["pW"], ["r8"], 8)
                tt(T.ysn[:, 136 * t + 128:136 * t + 136], pw, T.tf[:, 32:40], AL.subtract, ["pW", "r8"], ["yb%d" % t], 8, "yb")
                send("Y", T.ysn[:, 136 * t:136 * t + 136], ["ya%d" % t, "yb%d" % t])
            elif WV0[0]:
                mm([cm(pw, "-3", 8, True)], ["one", "cl-3"], ["pW"], 64, "W00")
                mm(wsum(T.ZW, True), ["ZW", zk], ["pW"], 1024, "W0")
                pv = T.pK1[:, 0:8]
                mm([cm(pv, "-3", 8, True), (pv, T.I1[:], tl(NH, 0), False, False), (pv, T.I1[:], tl(BASE, 0), False, False)],
                   ["one", "cl-3", "I1", "nh0", "base0"], ["pK1"], 192, "ce")
                mm([(pv,) + x[1:] for x in wsum(T.ZW, True)], ["ZW", zk], ["pK1"], 1024, "off0")
                ts(T.tf[:, 32:40], pw, 8 * M1, 8 * M1, AL.add, AL.subtract, ["pW"], ["r8"], 8, "r80")
                tt(T.tf[:, 40:48], pv, T.tf[:, 32:40], AL.subtract, ["pK1", "r8"], ["u30"], 8)
                ts(T.lst[:, 16:24], T.tf[:, 40:48], c(L16), 3.5, AL.add, AL.add, ["u30", "l16"], ["wo0"], 8)
            else:
                mm([cm(pw, "3", 8, True)], ["one", "cl3"], ["pW"], 64, "W00")
                mm(wsum(T.ZN, False) + [cm(pw, "8m", 8), cm(pw, "-8m", 8), (pw, T.I1[:], tl(NH, 0), False, False), (pw, T.I1[:], tl(BASE, 0), False, False)]
                   + wsum(T.ZW, True), ["ZW", "ZN", "I1", "one", "cl8m", "cl-8m", "nh0", "base0", zk], ["pW"], 2304, "W0")
                ts(T.lst[:, 16:24], pw, c(L16), None, AL.add, None, ["pW", "l16"], ["wo0"], 8)
            pu = T.pU[:, 0:128]
            mm([cm(pu, "u0", 128, True), (pu, T.BN[:], zn_, False, False), cm(pu, "um", 128), cm(pu, "-um", 128), cm(pu, "32", 128),
                (pu, T.BW[:], zn_, False, True)], ["one", "clu0", "clum", "cl-um", "cl32", "BW", "BN", zk], ["pU"], 768, "U" + H)
            tt(T.pr[:, hs], pu, Fi, AL.mult, ["pU", fk], ["pr" + H], 128)
        ts(T.qi[:], T.pr[:], c(C32 + t), None, AL.add, None, ["pr0", "pr1", "c32%d" % t], ["qi0"], 256)
        s1 = RING[(t + 1) % 3]
        ts(T.VT[:, s1:s1 + 256], T.qi[:], 5, 2047, AL.arith_shift_right, AL.bitwise_and, ["qi0"], ["S%d%d" % ((t + 1) % 3, h) for h in (0, 1)], 256, "S0")
        for h in WORD[0 if hop is None else 1]:
            H = str(h)
            cs = slice(128 * h, 128 * h + 128)
            Y = T.W[:, 264 * t + 128 * h:264 * t + 128 * h + 128]
            yk = ("W%d" % t, "lY%d" % t)[h]
            wo, wk = T.lst[:, 16 + 8 * h:24 + 8 * h], "wo" + H
            if h:
                fb = T.fl5[:] if last else T.VT[:, VL[t] + 256:VL[t] + 264]
                tt(T.tf[:, 48:56], T.W[:, 264 * t + 256:264 * t + 264], fb, AL.add, ["lY%d" % t, "lF%d" % t], ["off1"], 16)
                ts(wo, T.tf[:, 48:56], 3.5, None, AL.add, None, ["off1"], [wk], 8)
            pk = ("pP", "pK0")[h]
            pp = T[pk][:, 0:128]
            if not last:
                tt(T.dd[:, cs], T.X[:].indirect(wo), Y, AL.max, Xk + Xt + [wk, yk], ["dd" + H], 50 + 128 * GATH)
                act(T.ad[:, cs], T.X[:].indirect(wo), AF.Copy, Xk + Xt + [wk], ["ad" + H], 65 + 128 * GATH)
            cp(T.X[:].indirect(wo), Y, [wk, yk], Xk + Xt, 50 + 128 * SCAT, "X" + H)
            if not last:
                mm([(pp, T.Bc[:], T.CI[:, 128:256], True, False), (pp, T.WA[:, 0:128], Y, False, False)], ["Bc", "CI", yk] + WAk, [pk], 256, "Pa" + H)
                mm([(pp, T.WA[:, 128:256], T.dd[:, cs], False, False), (pp, T.WA[:, 256:384], T.ad[:, cs], False, False),
                    cm(pp, "64m", 128), cm(pp, "-64m", 128), (pp, T.WB[:, 0:128], Y, False, False),
                    (pp, T.WB[:, 128:256], T.dd[:, cs], False, False), (pp, T.WB[:, 256:384], T.ad[:, cs], False, True)],
                   ["dd" + H, "ad" + H, "WB0", "WB1", "one", "cl64m", "cl-64m"], [pk], 896, "Pb" + H)
                act(T.rb[:, cs], pp, AF.Identity, [pk, "BJ"], ["rb" + H], 128, bias=T.BJ[:, 2 * t + h:2 * t + h + 1])
                if PSCAT[0] == "v":
                    cp(T.P[:].indirect(wo), T.rb[:, cs], [wk, "rb" + H], Pk, 50 + 128 * SCAT, "P" + H)
                else:
                    op("s", lambda wo=wo, cs=cs: [S.activation(T.P[:].indirect(wo), T.rb[:, cs], AF.Silu)], [wk, "rb" + H], Pk, (65 + 128 * SCAT) * CYC, nm="P" + H)
    ts(T.lst[:, 32:48], tl(SPTR), c(LF), None, AL.add, None, ["sptr", "lf"], ["sl"], 16)
    for h in (1, 0):
        win, keys = upto(RING[2] + 256)
        cp(T.yso[:, h::2], win.indirect(T.lst[:, 32 + 8 * h:40 + 8 * h]), keys + ["sl"], ["yso%d" % h], 50 + 128 * GATH)
        act(T.yzo[:, h::2], T.zs[:, 256 * TS + 128 * h:256 * TS + 128 * h + 128], AF.Copy, ["z%d%d" % (TS, h)], ["yzo%d" % h], 128)
    dma("y", "ox", T.yx[:], T.X[:, 0:2048], Xk, [], FIX + 8 * (ROW + 4096 / RATE))
    dma("s", "oz", T.yz[:], T.yzo[:], ["yzo0", "yzo1"], [], FIX + 8 * (ROW + 512 / RATE))
    dma("s", "os_", T.ys[:], T.yso[:], ["yso0", "yso1"], [], FIX + 8 * (2 * ROW + 5120 / RATE) - 600)
    return ops, sent


def depend(ops):
    lw, rd, deps = {}, {}, []
    for i, o in enumerate(ops):
        r = [k for k in o[2] if k not in BANKS]
        w = o[3] + [k for k in o[2] if k in BANKS]
        d = set()
        for k in r:
            if k in lw:
                d.add(lw[k])
        for k in w:
            if k in lw:
                d.add(lw[k])
            d.update(rd.get(k, ()))
        for k in r:
            rd.setdefault(k, []).append(i)
        for k in w:
            lw[k] = i
            rd[k] = []
        d.discard(i)
        deps.append(sorted(d))
    return deps


def places():
    place = {}
    for p, name in enumerate(ORDER):
        place[name.rstrip("+-")] = p / len(ORDER) + name.count("+") - name.count("-")
    at = -1.0
    for name in SETUP:
        if name[0] == "@":
            at = place[name[1:]] - 0.5 / len(ORDER)
        else:
            at += 1e-5
            place[name] = at
    for kind, moves in (("@last", LAST), ("@direct", DIRECT)):
        for before, names in moves:
            for p, name in enumerate(names.split()):
                place[name + kind] = place[before] - 0.4 / len(ORDER) + p * 1e-5
    return place


def order(ops, deps, place=None):
    n = len(ops)
    place = place or places()
    succ = [[] for _ in range(n)]
    for i in range(n):
        for d in deps[i]:
            succ[d].append(i)
    key = [max(o[8], 0) + place.get(o[9] + o[10], place[o[9]]) for o in ops]
    left = [len(d) for d in deps]
    ready = [i for i in range(n) if not left[i]]
    line = []
    while ready:
        i = min(ready, key=lambda i: (key[i], i))
        ready.remove(i)
        line.append(i)
        for s in succ[i]:
            left[s] -= 1
            if not left[s]:
                ready.append(s)
    return line


CACHE = {}


def rank_program(g, core, T, topo):
    rank = T.rank_of(core)
    if rank is None:
        helper_program(g, core, T, topo)
        return
    ops, sent = plan(g, core, T, topo, rank)
    if "o" not in CACHE:
        d = depend(ops)
        CACHE["o"] = (d, order(ops, d))
    deps, seq = CACHE["o"]
    Q = {"v": g.vector, "s": g.scalar, "p": g.tensor, "g": g, "y": g.sync}
    count, mark, seen, known = {}, {}, {}, {}
    place = {i: p for p, i in enumerate(seq)}
    for i in seq:
        e, fn, sem, n = ops[i][0], ops[i][1], ops[i][5], ops[i][6]
        if e == "x":
            mark[i] = (sem, n)
            count[sem] = n
            known[i] = {}
            continue
        mine = seen.setdefault(e, {})
        for d in sorted(deps[i], key=lambda d: -place[d]):
            if d in mark and not (e == "p" and ops[d][0] == "p"):
                s, v = mark[d]
                if mine.get(s, 0) < v:
                    Q[e].wait_ge(T.sem[s], v)
                    mine[s] = v
                for s2, v2 in known[d].items():
                    mine[s2] = max(mine.get(s2, 0), v2)
        known[i] = dict(mine)
        ins = fn()
        if n:
            s = sem or "c" + e
            for x in ins:
                x.then_inc(T.sem[s], n if sem else 1)
            count[s] = count.get(s, 0) + n
            mark[i] = (s, count[s])
    count["sent"] = sent[0]
    for s in sorted(count):
        g.wait_ge(T.sem[s], count[s])
